import numpy as np
import ml_dtypes


def mxq(x, axis, fmt="e4m3"):
    dtype, down = {"e4m3": (ml_dtypes.float8_e4m3fn, 7), "e5m2": (ml_dtypes.float8_e5m2, 14)}[fmt]
    v = np.moveaxis(np.asarray(x, np.float32).astype(ml_dtypes.bfloat16).astype(np.float64), axis, -1)
    blocks = v.reshape(v.shape[:-1] + (-1, 32))
    amax = np.abs(blocks).max(-1, keepdims=True)
    byte = np.maximum(np.where(amax > 0, np.frexp(amax)[1] - 1 + 127, 0) - down, 1)
    scale = np.exp2(byte - 127.0)
    codes = (blocks / scale).astype(np.float32).astype(dtype).astype(np.float64)
    return np.moveaxis((codes * scale).reshape(v.shape), -1, axis)


WIDE = False


def mx_kscale(k):
    if not WIDE:
        return np.ones(k)
    levels = np.array([10, -10, 5, -5, 0])
    if k % 512:
        return np.exp2(np.random.permutation(np.resize(levels, k // 32))).repeat(32)
    a = np.empty((k // 512, 16))
    for p in range(k // 512):
        a[p, :8] = np.random.permutation(np.resize(levels, 8))
        for g in range(8):
            far = levels[np.abs(levels - a[p, g]) >= 10]
            a[p, g + 8] = far[np.random.randint(len(far))]
    return np.exp2(a.ravel()).repeat(32)


def f64(x):
    return np.asarray(x).astype(np.float64)


def striped(idx):
    return np.tile(idx.reshape(-1, 16).T, (8, 1)).astype(np.uint16)


def unstriped(offs):
    return offs[:16].T.reshape(-1).astype(np.int64)


E2M1 = np.array([0.0, 0.5, 1.0, 1.5, 2.0, 3.0, 4.0, 6.0, -0.0, -0.5, -1.0, -1.5, -2.0, -3.0, -4.0, -6.0])


def pack_weight(w, fmt):
    k, n = w.shape
    w = f64(np.asarray(w, np.float32).astype(ml_dtypes.bfloat16)).reshape(k // 32, 32, n)
    amax = np.abs(w).max(1)
    if fmt == "e4m3":
        byte = np.frexp(amax)[1] - 1 + 127 - 7
    else:
        mant, ex = np.frexp(amax / 6.0)
        byte = np.where(mant > 0.5, ex, ex - 1) + 127
    byte = np.clip(np.where(amax > 0, byte, 1), 1, 254)
    scaled = (w * np.exp2(127.0 - byte)[:, None, :]).reshape(k, n).astype(np.float32)
    by_word = np.ascontiguousarray(scaled.reshape(k // 512, 128, 4, n).transpose(0, 1, 3, 2))
    if fmt == "e4m3":
        words = by_word.astype(ml_dtypes.float8_e4m3fn).view(np.uint8)
    else:
        c = by_word.astype(ml_dtypes.float4_e2m1fn).view(np.uint8) & 0xF
        words = (c[..., 0::2] | (c[..., 1::2] << 4)).reshape(k // 512, 128, 2 * n)
    return np.ascontiguousarray(words), np.ascontiguousarray(byte.astype(np.uint8).reshape(k // 512, 16, n))


def unpack_weight(words, scales, fmt):
    g, _, n = scales.shape
    words = np.ascontiguousarray(words).reshape(g, 128, n, -1)
    if fmt == "e4m3":
        vals = words.view(ml_dtypes.float8_e4m3fn).astype(np.float64)
    else:
        nib = np.empty((g, 128, n, 4), np.uint8)
        nib[..., 0::2] = words & 0xF
        nib[..., 1::2] = words >> 4
        vals = E2M1[nib]
    vals = vals * np.repeat(np.exp2(scales.astype(np.float64) - 127.0), 8, axis=1)[..., None]
    return vals.transpose(0, 1, 3, 2).reshape(g * 512, n)


def gelu(v):
    return 0.5 * v * (1.0 + np.tanh(np.sqrt(2.0 / np.pi) * (v + 0.044715 * v**3)))


def striped8(idx):
    return np.concatenate([v.reshape(-1, 16).T for v in idx]).astype(np.uint16)


def unstriped8(offs):
    return np.stack([offs[16 * g:16 * g + 16].T.reshape(-1) for g in range(8)]).astype(np.int64)


def runs(v, idx8):
    k = np.arange(v.shape[0])
    return v[k[:, None], idx8[k % 512 // 64]]


def often(T, S):
    return np.random.permutation(T)[(T * np.random.uniform(0, 1, S) ** 4).astype(np.int64)]


K, H, N, T, S = 1024, 1024, 512, 2048, 512

def setup_inputs():
    n = np.random.standard_normal
    s = mx_kscale(K)[:, None]
    u = mx_kscale(H)[:, None]
    tab_words, tab_scales = pack_weight(n((K, T)) * s, "e4m3")
    offs = striped8(np.stack([often(T, S) for _ in range(8)]))
    w1 = n((K, H)) / np.sqrt(K) / s * u.T
    w2_words, w2_scales = pack_weight(n((K, H)) / np.sqrt(K) / s, "e2m1")
    w3_words, w3_scales = pack_weight(n((K, H)) / np.sqrt(K) / s * u.T, "e4m3")
    b3 = 0.4 * n(H) * u[:, 0]
    w4 = n((H, N)) / np.sqrt(H) / u
    bq = 0.5 * n(N)
    return {"tab_words": tab_words, "tab_scales": tab_scales, "offs": offs,
            "w1": w1.astype(np.float32),
            "w2_words": w2_words, "w2_scales": w2_scales,
            "w3_words": w3_words, "w3_scales": w3_scales,
            "b3": b3.astype(np.float32),
            "w4": w4.astype(np.float32), "bq": bq.astype(np.float32)}

def reference(tab_words, tab_scales, offs, w1, w2_words, w2_scales, w3_words, w3_scales, b3, w4, bq):
    v = runs(unpack_weight(tab_words, tab_scales, "e4m3"), unstriped8(offs))
    a = mxq(f64(w1), 0, "e4m3").T @ v
    b = unpack_weight(w2_words, w2_scales, "e2m1").T @ v
    c = unpack_weight(w3_words, w3_scales, "e4m3").T @ v
    box = a * b
    bound = c + f64(b3)[:, None]
    h = np.maximum(box, bound)
    y = mxq(f64(w4), 0, "e4m3").T @ mxq(h, 0, "e4m3")
    return y + f64(bq)[:, None]

@@ -1,0 +1,253 @@
+from contextlib import ExitStack
+
+import concourse.mybir as mybir
+
+K, H, N, T, S = 1024, 1024, 512, 2048, 512
+FLOPS = 2 * S * (3 * K * H + H * N)
+
+F32 = mybir.dt.float32
+BF16 = mybir.dt.bfloat16
+I32 = mybir.dt.int32
+U32 = mybir.dt.uint32
+U16 = mybir.dt.uint16
+U8 = mybir.dt.uint8
+FP8X4 = mybir.dt.float8_e4m3fn_x4
+FP4X4 = mybir.dt.float4_e2m1fn_x4
+ALU = mybir.AluOpType
+ACT = mybir.ActivationFunctionType
+
+P = 128
+HALF = S // 2
+
+
+def tile_list_subsumption_box_features_kernel(
+    tc, tab_words, tab_scales, offs, w1, w2_words, w2_scales, w3_words, w3_scales, b3, w4, bq, out
+):
+    nc = tc.nc
+    with ExitStack() as ctx:
+        keep = ctx.enter_context(tc.tile_pool(name="keep", bufs=1))
+        psum = ctx.enter_context(tc.psum_pool(name="psum", bufs=8))
+
+        def tl(shape, dtype, name, tag=None):
+            return keep.tile(shape, dtype, name=name, tag=tag or name, align_bytes=64)
+
+        offsets = keep.tile([P, S // 16], U16, name="offsets")
+        nc.sync.dma_start(offsets[:], offs)
+
+        swin = [tl([P, T], U8, "swin0", "slotA"), tl([P, T], U8, "swin1")]
+        wsc_raw = tl([P, 4 * H], U8, "wsc_raw")
+        for a in range(2):
+            nc.vector.memset(swin[a][:].bitcast(I32), 0)
+            nc.scalar.dma_start(swin[a][:].bitcast(I32)[0:P:8, :], tab_scales[a].bitcast(I32))
+        nc.vector.memset(wsc_raw[:].bitcast(I32), 0)
+        for x, src in enumerate((w2_scales, w3_scales)):
+            dst = wsc_raw[:].bitcast(I32)[0:P:8, x * 512 : (x + 1) * 512]
+            nc.gpsimd.dma_start(dst.rearrange("q (a n) -> q a n", a=2), src.bitcast(I32).rearrange("a q n -> q a n"))
+        b3c = tl([P, 2, 16], F32, "b3c")
+        bqc = tl([P, 4], F32, "bqc")
+        with nc.allow_non_contiguous_dma(reason="small bias columns"):
+            b3v = b3.rearrange("(g q s) -> q g s", g=2, s=16)
+            for e in range(4):
+                nc.gpsimd.dma_start(b3c[e:P:4, :, 0:13], b3v[:, :, e : e + 13])
+            nc.gpsimd.dma_start(bqc[:], bq.rearrange("(u p) -> p u", p=P))
+
+        twin = [tl([P, T], I32, "twin0", "slotB"), tl([P, T], I32, "twin1", "slotC")]
+        for a in range(2):
+            nc.sync.dma_start(twin[a][:], tab_words[a].rearrange("p t i -> p (t i)").bitcast(I32))
+        w2raw = tl([P, 2, 512], I32, "w2raw", "slotD")
+        nc.sync.dma_start(w2raw[:], w2_words.bitcast(I32).rearrange("a p n -> p a n"))
+
+        sgath = tl([P, 2 * S], U8, "sgath")
+        for a in range(2):
+            nc.vector.tensor_copy(sgath[:, a * S : (a + 1) * S], swin[a][:].indirect(offsets[:]))
+        w3raw = tl([P, 2, H], I32, "w3raw", "slotA")
+        nc.sync.dma_start(w3raw[:], w3_words.rearrange("a p n i -> a p (n i)").bitcast(I32).rearrange("a p n -> p a n"))
+
+        planes = tl([P, 2 * S + 4 * H], U8, "planes")
+        planes_i = planes[:].bitcast(I32)
+        nc.vector.tensor_copy(planes_i[:, 0:256], sgath[:].bitcast(I32))
+        nc.vector.tensor_copy(
+            planes_i[:, 256:1280].rearrange("p (x t Q i) -> p x Q t i", x=8, t=4, i=4),
+            wsc_raw[:].bitcast(I32).rearrange("p (x Q i t) -> p x Q t i", x=8, t=4, i=4),
+        )
+        for r in range(1, 4):
+            nc.scalar.dma_start(planes_i[r:P:32, :], planes_i[8 * r : P : 32, :])
+
+        vw = []
+        for a in range(2):
+            g_words = tl([P, S], U32, "vw%d" % a)
+            nc.vector.tensor_copy(g_words[:], twin[a][:].bitcast(U32).indirect(offsets[:]))
+            vw.append(g_words)
+
+        w1raw = {}
+
+        def load_w1(g, a, tag):
+            raw = tl([P, 4, 512], F32, "w1raw%d%d" % (g, a), tag)
+            nc.sync.dma_start(raw[:], w1[512 * a : 512 * (a + 1), 512 * g : 512 * (g + 1)].rearrange("(p j) c -> p j c", j=4))
+            w1raw[g, a] = raw
+
+        load_w1(0, 0, "slotB")
+        load_w1(0, 1, "slotC")
+
+        w2p, w3p = [], []
+        for g in range(2):
+            perm = tl([P, 2, 256], I32, "w2p%d" % g)
+            nc.vector.tensor_copy(
+                perm[:].rearrange("p a (t q e) -> p a t q e", t=4, e=2),
+                w2raw[:, :, 256 * g : 256 * (g + 1)].rearrange("p a (q t e) -> p a t q e", t=4, e=2),
+            )
+            w2p.append(perm)
+        load_w1(1, 0, "slotD")
+        for g in range(2):
+            perm = tl([P, 2, 512], I32, "w3p%d" % g)
+            nc.vector.tensor_copy(
+                perm[:].rearrange("p a (t q e) -> p a t q e", t=4, e=4),
+                w3raw[:, :, 512 * g : 512 * (g + 1)].rearrange("p a (q t e) -> p a t q e", t=4, e=4),
+            )
+            w3p.append(perm)
+        load_w1(1, 1, "slotA")
+
+        def v_operand(a, j0, n):
+            return dict(rhs=vw[a][:, j0 : j0 + n].bitcast(FP8X4), rhs_scale=planes[:, a * S + j0 : a * S + j0 + n])
+
+        def w_scale(x, a, g, t):
+            c0 = 2 * S + 2 * H * x + H * a + 512 * g + P * t
+            return planes[:, c0 : c0 + P]
+
+        b_sb, c_sb = {}, {}
+
+        def product_b(g):
+            for tp in range(2):
+                b_sb[g, tp] = tl([P, 2, S], F32, "b%d%d" % (g, tp))
+                for t in (2 * tp, 2 * tp + 1):
+                    bank = psum.tile([P, S], F32, name="bank", tag="bank")
+                    for a in range(2):
+                        nc.tensor.matmul_mx(
+                            bank[:], lhsT=w2p[g][:, a, 64 * t : 64 * (t + 1)].bitcast(U8).bitcast(FP4X4),
+                            lhsT_scale=w_scale(0, a, g, t), start=(a == 0), stop=(a == 1), **v_operand(a, 0, S))
+                    nc.scalar.copy(b_sb[g, tp][:, t % 2, :], bank[:])
+
+        def product_c(g):
+            c_sb[g] = tl([P, 4, S], F32, "c%d" % g)
+            for t in range(4):
+                bank = psum.tile([P, S], F32, name="bank", tag="bank")
+                for a in range(2):
+                    nc.tensor.matmul_mx(
+                        bank[:], lhsT=w3p[g][:, a, P * t : P * (t + 1)].bitcast(FP8X4),
+                        lhsT_scale=w_scale(1, a, g, t), start=(a == 0), stop=(a == 1), **v_operand(a, 0, S))
+                nc.scalar.activation(c_sb[g][:, t, :], bank[:], ACT.Identity, bias=b3c[:, g, 4 * t : 4 * t + 1])
+
+        def cast(on_vector, dst, src):
+            if on_vector:
+                nc.vector.tensor_copy(dst, src)
+            else:
+                nc.scalar.copy(dst, src)
+
+        def quantize(name, rounded):
+            codes = tl([P, 256], U32, name + "_codes")
+            scales = tl([P, 256], U8, name + "_scales")
+            nc.vector.quantize_mx(codes[:].bitcast(FP8X4), scales[:], rounded[:])
+            return codes, scales
+
+        w1r, w1q = {}, {}
+
+        def round_w1(g, a, tp, on_vector):
+            rounded = tl([P, 1024], BF16, "w1r%d%d%d" % (g, a, tp))
+            src = w1raw[g, a][:].rearrange("p j (q t e) -> p t q j e", t=4, e=4)[:, 2 * tp : 2 * tp + 2]
+            cast(on_vector, rounded[:].rearrange("p (t q e j) -> p t q j e", t=2, e=4, j=4), src)
+            w1r[g, a, tp] = rounded
+
+        def quant_w1(g, a, tp):
+            w1q[g, a, tp] = quantize("w1q%d%d%d" % (g, a, tp), w1r[g, a, tp])
+
+        hq = {}
+
+        def product_a(g, jh):
+            js = slice(jh * HALF, (jh + 1) * HALF)
+            ab = tl([P, 4, HALF], F32, "ab%d%d" % (g, jh))
+            for tp in range(2):
+                bank = psum.tile([P, 2, HALF], F32, name="bank", tag="bank")
+                for t2 in range(2):
+                    for a in range(2):
+                        codes, scales = w1q[g, a, tp]
+                        nc.tensor.matmul_mx(
+                            bank[:, t2, :], lhsT=codes[:, P * t2 : P * (t2 + 1)].bitcast(FP8X4),
+                            lhsT_scale=scales[:, P * t2 : P * (t2 + 1)], start=(a == 0), stop=(a == 1),
+                            **v_operand(a, jh * HALF, HALF))
+                nc.vector.tensor_tensor(ab[:, 2 * tp : 2 * tp + 2, :], bank[:], b_sb[g, tp][:, :, js], ALU.mult)
+            return ab
+
+        def make_h(g, jh, ab):
+            js = slice(jh * HALF, (jh + 1) * HALF)
+            h = tl([P, 4 * HALF], BF16, "h%d%d" % (g, jh))
+            nc.vector.tensor_tensor(
+                h[:].rearrange("p (c i t) -> p c t i", i=4, t=4),
+                ab[:].rearrange("p t (c i) -> p c t i", i=4),
+                c_sb[g][:, :, js].rearrange("p t (c i) -> p c t i", i=4), ALU.max)
+            return h
+
+        w4raw, w4r, w4q = {}, {}, {}
+
+        def load_w4(g, tag):
+            raw = tl([P, 4, N], F32, "w4raw%d" % g, tag)
+            rows = w4[512 * g : 512 * (g + 1), :].rearrange("(q t e) n -> e q t n", t=4, e=4)
+            for e in range(4):
+                nc.sync.dma_start(raw[e:P:4, :, :], rows[e])
+            w4raw[g] = raw
+
+        def round_w4(g, nh, on_vector):
+            rounded = tl([P, 1024], BF16, "w4r%d%d" % (g, nh))
+            src = w4raw[g][:, :, 256 * nh : 256 * (nh + 1)].rearrange("p t (c i) -> p c t i", i=4)
+            cast(on_vector, rounded[:].rearrange("p (c i t) -> p c t i", i=4, t=4), src)
+            w4r[g, nh] = rounded
+
+        product_b(0)
+        product_c(0)
+        for a in range(2):
+            for tp in range(2):
+                round_w1(0, a, tp, True)
+            for tp in range(2):
+                quant_w1(0, a, tp)
+        load_w4(0, "slotB")
+        load_w4(1, "slotC")
+        product_b(1)
+        abs0 = [product_a(0, jh) for jh in range(2)]
+        for tp in range(2):
+            round_w1(1, 0, tp, False)
+        product_c(1)
+        hs0 = [make_h(0, jh, abs0[jh]) for jh in range(2)]
+        round_w1(1, 1, 0, True)
+        round_w1(1, 1, 1, False)
+        for a in range(2):
+            for tp in range(2):
+                quant_w1(1, a, tp)
+        for jh in range(2):
+            hq[0, jh] = quantize("hq0%d" % jh, hs0[jh])
+        for g in range(2):
+            for nh in range(2):
+                round_w4(g, nh, False)
+        ab10 = product_a(1, 0)
+        h10 = make_h(1, 0, ab10)
+        ab11 = product_a(1, 1)
+        hq[1, 0] = quantize("hq10", h10)
+        for g in range(2):
+            for nh in range(2):
+                w4q[g, nh] = quantize("w4q%d%d" % (g, nh), w4r[g, nh])
+        h11 = make_h(1, 1, ab11)
+        hq[1, 1] = quantize("hq11", h11)
+
+        for jh in range(2):
+            for u in range(4):
+                bank = psum.tile([P, HALF], F32, name="bank", tag="bank")
+                cols = slice(P * (u % 2), P * (u % 2 + 1))
+                for g in range(2):
+                    codes, scales = w4q[g, u // 2]
+                    nc.tensor.matmul_mx(
+                        bank[:], lhsT=codes[:, cols].bitcast(FP8X4), lhsT_scale=scales[:, cols],
+                        rhs=hq[g, jh][0][:].bitcast(FP8X4), rhs_scale=hq[g, jh][1][:], start=(g == 0), stop=(g == 1))
+                res = tl([P, HALF], F32, "res%d%d" % (jh, u))
+                if jh == 0 or u % 2 == 0:
+                    nc.scalar.activation(res[:], bank[:], ACT.Identity, bias=bqc[:, u : u + 1])
+                else:
+                    nc.vector.tensor_scalar(res[:], bank[:], bqc[:, u : u + 1], None, ALU.add)
+                nc.sync.dma_start(out[P * u : P * (u + 1), jh * HALF : (jh + 1) * HALF], res[:])

@@ -34,7 +34,7 @@ def tile_list_subsumption_box_features_kernel(
         offsets = keep.tile([P, S // 16], U16, name="offsets")
         nc.sync.dma_start(offsets[:], offs)
 
-        swin = [tl([P, T], U8, "swin0", "slotA"), tl([P, T], U8, "swin1")]
+        swin = [tl([P, T], U8, "swin0"), tl([P, T], U8, "swin1")]
         wsc_raw = tl([P, 4 * H], U8, "wsc_raw")
         for a in range(2):
             nc.vector.memset(swin[a][:].bitcast(I32), 0)
@@ -43,41 +43,52 @@ def tile_list_subsumption_box_features_kernel(
         for x, src in enumerate((w2_scales, w3_scales)):
             dst = wsc_raw[:].bitcast(I32)[0:P:8, x * 512 : (x + 1) * 512]
             nc.gpsimd.dma_start(dst.rearrange("q (a n) -> q a n", a=2), src.bitcast(I32).rearrange("a q n -> q a n"))
-        b3c = tl([P, 2, 16], F32, "b3c")
-        bqc = tl([P, 4], F32, "bqc")
+
+        w2raw = tl([P, 2, 512], I32, "w2raw", "slotD")
+        nc.sync.dma_start(w2raw[:], w2_words.bitcast(I32).rearrange("a p n -> p a n"))
+        twin = [tl([P, T], I32, "twin0", "slotB")]
+        nc.sync.dma_start(twin[0][:], tab_words[0].rearrange("p t i -> p (t i)").bitcast(I32))
+        twin.append(tl([P, T], I32, "twin1", "slotA"))
+        nc.sync.dma_start(twin[1][:], tab_words[1].rearrange("p t i -> p (t i)").bitcast(I32))
+
+        sgath = tl([P, 2 * S], U8, "sgath")
+        for a in range(2):
+            nc.vector.tensor_copy(sgath[:, a * S : (a + 1) * S], swin[a][:].indirect(offsets[:]))
+        b3c = tl([P, 2, 16], F32, "b3c", "swin0")
+        bqc = tl([P, 4], F32, "bqc", "swin1")
         with nc.allow_non_contiguous_dma(reason="small bias columns"):
             b3v = b3.rearrange("(g q s) -> q g s", g=2, s=16)
             for e in range(4):
                 nc.gpsimd.dma_start(b3c[e:P:4, :, 0:13], b3v[:, :, e : e + 13])
             nc.gpsimd.dma_start(bqc[:], bq.rearrange("(u p) -> p u", p=P))
 
-        twin = [tl([P, T], I32, "twin0", "slotB"), tl([P, T], I32, "twin1", "slotC")]
-        for a in range(2):
-            nc.sync.dma_start(twin[a][:], tab_words[a].rearrange("p t i -> p (t i)").bitcast(I32))
-        w2raw = tl([P, 2, 512], I32, "w2raw", "slotD")
-        nc.sync.dma_start(w2raw[:], w2_words.bitcast(I32).rearrange("a p n -> p a n"))
-
-        sgath = tl([P, 2 * S], U8, "sgath")
-        for a in range(2):
-            nc.vector.tensor_copy(sgath[:, a * S : (a + 1) * S], swin[a][:].indirect(offsets[:]))
-        w3raw = tl([P, 2, H], I32, "w3raw", "slotA")
-        nc.sync.dma_start(w3raw[:], w3_words.rearrange("a p n i -> a p (n i)").bitcast(I32).rearrange("a p n -> p a n"))
 
         planes = tl([P, 2 * S + 4 * H], U8, "planes")
         planes_i = planes[:].bitcast(I32)
-        nc.vector.tensor_copy(planes_i[:, 0:256], sgath[:].bitcast(I32))
         nc.vector.tensor_copy(
             planes_i[:, 256:1280].rearrange("p (x t Q i) -> p x Q t i", x=8, t=4, i=4),
             wsc_raw[:].bitcast(I32).rearrange("p (x Q i t) -> p x Q t i", x=8, t=4, i=4),
         )
+        nc.vector.tensor_copy(planes_i[:, 0:256], sgath[:].bitcast(I32))
         for r in range(1, 4):
             nc.scalar.dma_start(planes_i[r:P:32, :], planes_i[8 * r : P : 32, :])
 
-        vw = []
+        w2p, w3p = [], []
+        w2perm = tl([P, 2, 2, 256], I32, "w2p", "wsc_raw")
+        for g in range(2):
+            perm = w2perm[:, g, :, :]
+            nc.vector.tensor_copy(
+                perm.rearrange("p a (t q e) -> p a t q e", t=4, e=2),
+                w2raw[:, :, 256 * g : 256 * (g + 1)].rearrange("p a (q t e) -> p a t q e", t=4, e=2),
+            )
+            w2p.append(perm)
+        w3raw = tl([P, 2, H], I32, "w3raw", "slotD")
+        nc.sync.dma_start(w3raw[:], w3_words.rearrange("a p n i -> a p (n i)").bitcast(I32).rearrange("a p n -> p a n"))
+
+        v_words = tl([P, 2 * S], U32, "v_words", "sgath")
+        vw = [v_words[:, a * S : (a + 1) * S] for a in range(2)]
         for a in range(2):
-            g_words = tl([P, S], U32, "vw%d" % a)
-            nc.vector.tensor_copy(g_words[:], twin[a][:].bitcast(U32).indirect(offsets[:]))
-            vw.append(g_words)
+            nc.vector.tensor_copy(vw[a], twin[a][:].bitcast(U32).indirect(offsets[:]))
 
         w1raw = {}
 
@@ -87,17 +98,8 @@ def tile_list_subsumption_box_features_kernel(
             w1raw[g, a] = raw
 
         load_w1(0, 0, "slotB")
-        load_w1(0, 1, "slotC")
+        load_w1(0, 1, "slotA")
 
-        w2p, w3p = [], []
-        for g in range(2):
-            perm = tl([P, 2, 256], I32, "w2p%d" % g)
-            nc.vector.tensor_copy(
-                perm[:].rearrange("p a (t q e) -> p a t q e", t=4, e=2),
-                w2raw[:, :, 256 * g : 256 * (g + 1)].rearrange("p a (q t e) -> p a t q e", t=4, e=2),
-            )
-            w2p.append(perm)
-        load_w1(1, 0, "slotD")
         for g in range(2):
             perm = tl([P, 2, 512], I32, "w3p%d" % g)
             nc.vector.tensor_copy(
@@ -105,7 +107,7 @@ def tile_list_subsumption_box_features_kernel(
                 w3raw[:, :, 512 * g : 512 * (g + 1)].rearrange("p a (q t e) -> p a t q e", t=4, e=4),
             )
             w3p.append(perm)
-        load_w1(1, 1, "slotA")
+        load_w1(1, 0, "slotD")
 
         def v_operand(a, j0, n):
             return dict(rhs=vw[a][:, j0 : j0 + n].bitcast(FP8X4), rhs_scale=planes[:, a * S + j0 : a * S + j0 + n])
@@ -208,12 +210,13 @@ def tile_list_subsumption_box_features_kernel(
                 round_w1(0, a, tp, True)
             for tp in range(2):
                 quant_w1(0, a, tp)
-        load_w4(0, "slotB")
-        load_w4(1, "slotC")
+        load_w1(1, 1, "slotB")
+        load_w4(0, "slotA")
         product_b(1)
         abs0 = [product_a(0, jh) for jh in range(2)]
         for tp in range(2):
             round_w1(1, 0, tp, False)
+        load_w4(1, "slotD")
         product_c(1)
         hs0 = [make_h(0, jh, abs0[jh]) for jh in range(2)]
         round_w1(1, 1, 0, True)
@@ -230,11 +233,12 @@ def tile_list_subsumption_box_features_kernel(
         h10 = make_h(1, 0, ab10)
         ab11 = product_a(1, 1)
         hq[1, 0] = quantize("hq10", h10)
-        for g in range(2):
-            for nh in range(2):
-                w4q[g, nh] = quantize("w4q%d%d" % (g, nh), w4r[g, nh])
+        for nh in range(2):
+            w4q[0, nh] = quantize("w4q0%d" % nh, w4r[0, nh])
         h11 = make_h(1, 1, ab11)
+        w4q[1, 0] = quantize("w4q10", w4r[1, 0])
         hq[1, 1] = quantize("hq11", h11)
+        w4q[1, 1] = quantize("w4q11", w4r[1, 1])
 
         for jh in range(2):
             for u in range(4):

@@ -26,40 +26,68 @@ def tile_list_subsumption_box_features_kernel(
     nc = tc.nc
     with ExitStack() as ctx:
         keep = ctx.enter_context(tc.tile_pool(name="keep", bufs=1))
+        late = ctx.enter_context(tc.tile_pool(name="late", bufs=1))
+        early = ctx.enter_context(tc.tile_pool(name="early", bufs=1))
         psum = ctx.enter_context(tc.psum_pool(name="psum", bufs=8))
 
         def tl(shape, dtype, name, tag=None):
             return keep.tile(shape, dtype, name=name, tag=tag or name, align_bytes=64)
 
+        def late_tile(shape, dtype, name, slot):
+            return late.tile(shape, dtype, name=name, offset=slot * 8192, align_bytes=64)
+
+        def early_tile(shape, dtype, name, slot):
+            return early.tile(shape, dtype, name=name, offset=slot * 8192, align_bytes=64)
+
         offsets = keep.tile([P, S // 16], U16, name="offsets")
         nc.sync.dma_start(offsets[:], offs)
 
+        w2raw = tl([P, 2, 512], I32, "w2raw")
+        nc.sync.dma_start(w2raw[:], w2_words.bitcast(I32).rearrange("a p n -> p a n"))
         swin = [tl([P, T], U8, "swin0"), tl([P, T], U8, "swin1")]
         wsc_raw = tl([P, 4 * H], U8, "wsc_raw")
         for a in range(2):
             nc.vector.memset(swin[a][:].bitcast(I32), 0)
-            nc.scalar.dma_start(swin[a][:].bitcast(I32)[0:P:8, :], tab_scales[a].bitcast(I32))
-        nc.vector.memset(wsc_raw[:].bitcast(I32), 0)
+            nc.sync.dma_start(swin[a][:].bitcast(I32)[0:P:8, :], tab_scales[a].bitcast(I32))
+        zeros = early_tile([P, 3 * 2048], I32, "zeros", 0)
+        nc.gpsimd.memset(wsc_raw[:].bitcast(I32)[:, 512:1024], 0)
+        nc.vector.memset(zeros[:, 0:8], 0)
+        nc.vector.tensor_copy(wsc_raw[:].bitcast(I32)[:, 0:512], zeros[:, 0:1].to_broadcast([P, 512]))
         for x, src in enumerate((w2_scales, w3_scales)):
             dst = wsc_raw[:].bitcast(I32)[0:P:8, x * 512 : (x + 1) * 512]
-            nc.gpsimd.dma_start(dst.rearrange("q (a n) -> q a n", a=2), src.bitcast(I32).rearrange("a q n -> q a n"))
+            nc.sync.dma_start(dst.rearrange("q (a n) -> q a n", a=2), src.bitcast(I32).rearrange("a q n -> q a n"))
 
-        w2raw = tl([P, 2, 512], I32, "w2raw", "slotD")
-        nc.sync.dma_start(w2raw[:], w2_words.bitcast(I32).rearrange("a p n -> p a n"))
-        twin = [tl([P, T], I32, "twin0", "slotB")]
+        b3c = tl([P, 2, 16], F32, "b3c")
+        b3v = b3.rearrange("(g q s) -> q g s", g=2, s=16)
+        for e in range(4):
+            nc.gpsimd.dma_start(b3c[e:P:4, :, 0:13], b3v[:, :, e : e + 13])
+        twin = [early_tile([P, T], I32, "twin0", 1)]
         nc.sync.dma_start(twin[0][:], tab_words[0].rearrange("p t i -> p (t i)").bitcast(I32))
-        twin.append(tl([P, T], I32, "twin1", "slotA"))
+        twin.append(early_tile([P, T], I32, "twin1", 2))
         nc.sync.dma_start(twin[1][:], tab_words[1].rearrange("p t i -> p (t i)").bitcast(I32))
+        w1raw = {}
 
-        sgath = tl([P, 2 * S], U8, "sgath")
+        def load_w1(g, a, tag):
+            raw = late_tile([P, 4, 512], F32, "w1raw%d%d" % (g, a), tag)
+            nc.sync.dma_start(raw[:], w1[512 * a : 512 * (a + 1), 512 * g : 512 * (g + 1)].rearrange("(p j) c -> p j c", j=4))
+            w1raw[g, a] = raw
+
+
+        w3raw = {}
+
+        def load_w3(g, slot):
+            raw = (early_tile, late_tile)[g]([P, 2, 512], I32, "w3raw%d" % g, slot)
+            words = w3_words.rearrange("a p n i -> a p (n i)").bitcast(I32)
+            nc.sync.dma_start(raw[:], words[:, :, 512 * g : 512 * (g + 1)].rearrange("a p n -> p a n"))
+            w3raw[g] = raw
+
+        load_w3(0, 0)
+
+        sgath = late_tile([P, 9 * 8192], U8, "sgath", 0)
         for a in range(2):
             nc.vector.tensor_copy(sgath[:, a * S : (a + 1) * S], swin[a][:].indirect(offsets[:]))
-        b3c = tl([P, 2, 16], F32, "b3c", "swin0")
         bqc = tl([P, 4], F32, "bqc", "swin1")
         with nc.allow_non_contiguous_dma(reason="small bias columns"):
-            b3v = b3.rearrange("(g q s) -> q g s", g=2, s=16)
-            for e in range(4):
-                nc.gpsimd.dma_start(b3c[e:P:4, :, 0:13], b3v[:, :, e : e + 13])
             nc.gpsimd.dma_start(bqc[:], bq.rearrange("(u p) -> p u", p=P))
 
 
@@ -69,7 +97,7 @@ def tile_list_subsumption_box_features_kernel(
             planes_i[:, 256:1280].rearrange("p (x t Q i) -> p x Q t i", x=8, t=4, i=4),
             wsc_raw[:].bitcast(I32).rearrange("p (x Q i t) -> p x Q t i", x=8, t=4, i=4),
         )
-        nc.vector.tensor_copy(planes_i[:, 0:256], sgath[:].bitcast(I32))
+        nc.vector.tensor_copy(planes_i[:, 0:256], sgath[:, 0 : 2 * S].bitcast(I32))
         for r in range(1, 4):
             nc.scalar.dma_start(planes_i[r:P:32, :], planes_i[8 * r : P : 32, :])
 
@@ -82,32 +110,18 @@ def tile_list_subsumption_box_features_kernel(
                 w2raw[:, :, 256 * g : 256 * (g + 1)].rearrange("p a (q t e) -> p a t q e", t=4, e=2),
             )
             w2p.append(perm)
-        w3raw = tl([P, 2, H], I32, "w3raw", "slotD")
-        nc.sync.dma_start(w3raw[:], w3_words.rearrange("a p n i -> a p (n i)").bitcast(I32).rearrange("a p n -> p a n"))
-
-        v_words = tl([P, 2 * S], U32, "v_words", "sgath")
+        v_words = late_tile([P, 2 * S], U32, "v_words", 7)
         vw = [v_words[:, a * S : (a + 1) * S] for a in range(2)]
         for a in range(2):
             nc.vector.tensor_copy(vw[a], twin[a][:].bitcast(U32).indirect(offsets[:]))
 
-        w1raw = {}
-
-        def load_w1(g, a, tag):
-            raw = tl([P, 4, 512], F32, "w1raw%d%d" % (g, a), tag)
-            nc.sync.dma_start(raw[:], w1[512 * a : 512 * (a + 1), 512 * g : 512 * (g + 1)].rearrange("(p j) c -> p j c", j=4))
-            w1raw[g, a] = raw
-
-        load_w1(0, 0, "slotB")
-        load_w1(0, 1, "slotA")
-
-        for g in range(2):
-            perm = tl([P, 2, 512], I32, "w3p%d" % g)
+        def permute_w3(g):
+            perm = tl([P, 2, 512], I32, "w3p%d" % g, ("w2raw", "b00")[g])
             nc.vector.tensor_copy(
                 perm[:].rearrange("p a (t q e) -> p a t q e", t=4, e=4),
-                w3raw[:, :, 512 * g : 512 * (g + 1)].rearrange("p a (q t e) -> p a t q e", t=4, e=4),
+                w3raw[g][:].rearrange("p a (q t e) -> p a t q e", t=4, e=4),
             )
             w3p.append(perm)
-        load_w1(1, 0, "slotD")
 
         def v_operand(a, j0, n):
             return dict(rhs=vw[a][:, j0 : j0 + n].bitcast(FP8X4), rhs_scale=planes[:, a * S + j0 : a * S + j0 + n])
@@ -153,8 +167,18 @@ def tile_list_subsumption_box_features_kernel(
 
         w1r, w1q = {}, {}
 
+        w1r10 = []
+
+        def w1r_tile(g, a, tp):
+            if (g, a) == (1, 0):
+                if not w1r10:
+                    w1r10.append(tl([P, 2, 1024], BF16, "w1r10", "w2raw"))
+                return w1r10[0][:, tp, :]
+            reuse = {(1, 1, 0): "b01", (1, 1, 1): "wsc_raw"}
+            return tl([P, 1024], BF16, "w1r%d%d%d" % (g, a, tp), reuse.get((g, a, tp)))[:]
+
         def round_w1(g, a, tp, on_vector):
-            rounded = tl([P, 1024], BF16, "w1r%d%d%d" % (g, a, tp))
+            rounded = w1r_tile(g, a, tp)
             src = w1raw[g, a][:].rearrange("p j (q t e) -> p t q j e", t=4, e=4)[:, 2 * tp : 2 * tp + 2]
             cast(on_vector, rounded[:].rearrange("p (t q e j) -> p t q j e", t=2, e=4, j=4), src)
             w1r[g, a, tp] = rounded
@@ -191,64 +215,83 @@ def tile_list_subsumption_box_features_kernel(
         w4raw, w4r, w4q = {}, {}, {}
 
         def load_w4(g, tag):
-            raw = tl([P, 4, N], F32, "w4raw%d" % g, tag)
+            raw = late_tile([P, 4, N], F32, "w4raw%d" % g, tag)
             rows = w4[512 * g : 512 * (g + 1), :].rearrange("(q t e) n -> e q t n", t=4, e=4)
             for e in range(4):
                 nc.sync.dma_start(raw[e:P:4, :, :], rows[e])
             w4raw[g] = raw
 
         def round_w4(g, nh, on_vector):
-            rounded = tl([P, 1024], BF16, "w4r%d%d" % (g, nh))
+            rounded = tl([P, 1024], BF16, "w4r%d%d" % (g, nh), ("b00", "w2raw", "b01", "wsc_raw")[2 * g + nh])
             src = w4raw[g][:, :, 256 * nh : 256 * (nh + 1)].rearrange("p t (c i) -> p c t i", i=4)
             cast(on_vector, rounded[:].rearrange("p (c i t) -> p c t i", i=4, t=4), src)
             w4r[g, nh] = rounded
 
+        load_w1(0, 0, 1)
+        load_w1(0, 1, 2)
+        load_w1(1, 0, 3)
+        load_w3(1, 0)
+        load_w1(1, 1, 4)
+        for g in range(2):
+            load_w4(g, 5 + g)
+
+        permute_w3(0)
         product_b(0)
+        for tp in range(2):
+            round_w1(0, 0, tp, True)
         product_c(0)
-        for a in range(2):
-            for tp in range(2):
-                round_w1(0, a, tp, True)
-            for tp in range(2):
-                quant_w1(0, a, tp)
-        load_w1(1, 1, "slotB")
-        load_w4(0, "slotA")
-        product_b(1)
-        abs0 = [product_a(0, jh) for jh in range(2)]
+        for tp in range(2):
+            quant_w1(0, 0, tp)
+        for tp in range(2):
+            round_w1(0, 1, tp, True)
+        for tp in range(2):
+            quant_w1(0, 1, tp)
+        ab00 = product_a(0, 0)
+        ab01 = product_a(0, 1)
         for tp in range(2):
             round_w1(1, 0, tp, False)
-        load_w4(1, "slotD")
-        product_c(1)
-        hs0 = [make_h(0, jh, abs0[jh]) for jh in range(2)]
+        product_b(1)
+        permute_w3(1)
+        h00 = make_h(0, 0, ab00)
+        h01 = make_h(0, 1, ab01)
         round_w1(1, 1, 0, True)
         round_w1(1, 1, 1, False)
         for a in range(2):
             for tp in range(2):
                 quant_w1(1, a, tp)
-        for jh in range(2):
-            hq[0, jh] = quantize("hq0%d" % jh, hs0[jh])
+        product_c(1)
+        ab10 = product_a(1, 0)
+        hq[0, 0] = quantize("hq00", h00)
+        hq[0, 1] = quantize("hq01", h01)
         for g in range(2):
             for nh in range(2):
                 round_w4(g, nh, False)
-        ab10 = product_a(1, 0)
-        h10 = make_h(1, 0, ab10)
         ab11 = product_a(1, 1)
-        hq[1, 0] = quantize("hq10", h10)
+        h10 = make_h(1, 0, ab10)
         for nh in range(2):
             w4q[0, nh] = quantize("w4q0%d" % nh, w4r[0, nh])
+        hq[1, 0] = quantize("hq10", h10)
+        for nh in range(2):
+            w4q[1, nh] = quantize("w4q1%d" % nh, w4r[1, nh])
         h11 = make_h(1, 1, ab11)
-        w4q[1, 0] = quantize("w4q10", w4r[1, 0])
         hq[1, 1] = quantize("hq11", h11)
-        w4q[1, 1] = quantize("w4q11", w4r[1, 1])
 
+        def out_pass(bank, g, jh, u):
+            cols = slice(P * (u % 2), P * (u % 2 + 1))
+            codes, scales = w4q[g, u // 2]
+            nc.tensor.matmul_mx(
+                bank[:], lhsT=codes[:, cols].bitcast(FP8X4), lhsT_scale=scales[:, cols],
+                rhs=hq[g, jh][0][:].bitcast(FP8X4), rhs_scale=hq[g, jh][1][:], start=(g == 0), stop=(g == 1))
+
+        banks = {}
         for jh in range(2):
             for u in range(4):
-                bank = psum.tile([P, HALF], F32, name="bank", tag="bank")
-                cols = slice(P * (u % 2), P * (u % 2 + 1))
-                for g in range(2):
-                    codes, scales = w4q[g, u // 2]
-                    nc.tensor.matmul_mx(
-                        bank[:], lhsT=codes[:, cols].bitcast(FP8X4), lhsT_scale=scales[:, cols],
-                        rhs=hq[g, jh][0][:].bitcast(FP8X4), rhs_scale=hq[g, jh][1][:], start=(g == 0), stop=(g == 1))
+                banks[jh, u] = psum.tile([P, HALF], F32, name="bank", tag="bank")
+                out_pass(banks[jh, u], 0, jh, u)
+        for jh in range(2):
+            for u in range(4):
+                bank = banks[jh, u]
+                out_pass(bank, 1, jh, u)
                 res = tl([P, HALF], F32, "res%d%d" % (jh, u))
                 if jh == 0 or u % 2 == 0:
                     nc.scalar.activation(res[:], bank[:], ACT.Identity, bias=bqc[:, u : u + 1])

@@ -99,7 +99,7 @@ def tile_list_subsumption_box_features_kernel(
         )
         nc.vector.tensor_copy(planes_i[:, 0:256], sgath[:, 0 : 2 * S].bitcast(I32))
         for r in range(1, 4):
-            nc.scalar.dma_start(planes_i[r:P:32, :], planes_i[8 * r : P : 32, :])
+            nc.sync.dma_start(planes_i[r:P:32, :], planes_i[8 * r : P : 32, :])
 
         w2p, w3p = [], []
         w2perm = tl([P, 2, 2, 256], I32, "w2p", "wsc_raw")
@@ -144,7 +144,7 @@ def tile_list_subsumption_box_features_kernel(
                     nc.scalar.copy(b_sb[g, tp][:, t % 2, :], bank[:])
 
         def product_c(g):
-            c_sb[g] = tl([P, 4, S], F32, "c%d" % g)
+            c_sb[g] = late_tile([P, 4, S], F32, "c1", 4) if g else tl([P, 4, S], F32, "c0")
             for t in range(4):
                 bank = psum.tile([P, S], F32, name="bank", tag="bank")
                 for a in range(2):
@@ -205,7 +205,7 @@ def tile_list_subsumption_box_features_kernel(
 
         def make_h(g, jh, ab):
             js = slice(jh * HALF, (jh + 1) * HALF)
-            h = tl([P, 4 * HALF], BF16, "h%d%d" % (g, jh))
+            h = tl([P, 4 * HALF], BF16, "h%d%d" % (g, jh), "wsc_raw" if (g, jh) == (1, 1) else None)
             nc.vector.tensor_tensor(
                 h[:].rearrange("p (c i t) -> p c t i", i=4, t=4),
                 ab[:].rearrange("p t (c i) -> p c t i", i=4),

@@ -76,12 +76,11 @@ def tile_list_subsumption_box_features_kernel(
         w3raw = {}
 
         def load_w3(g, slot):
-            raw = (early_tile, late_tile)[g]([P, 2, 512], I32, "w3raw%d" % g, slot)
+            raw = late_tile([P, 2, 512], I32, "w3raw%d" % g, slot)
             words = w3_words.rearrange("a p n i -> a p (n i)").bitcast(I32)
             nc.sync.dma_start(raw[:], words[:, :, 512 * g : 512 * (g + 1)].rearrange("a p n -> p a n"))
             w3raw[g] = raw
 
-        load_w3(0, 0)
 
         sgath = late_tile([P, 9 * 8192], U8, "sgath", 0)
         for a in range(2):
@@ -103,13 +102,16 @@ def tile_list_subsumption_box_features_kernel(
 
         w2p, w3p = [], []
         w2perm = tl([P, 2, 2, 256], I32, "w2p", "wsc_raw")
-        for g in range(2):
+
+        def permute_w2(g):
             perm = w2perm[:, g, :, :]
             nc.vector.tensor_copy(
                 perm.rearrange("p a (t q e) -> p a t q e", t=4, e=2),
                 w2raw[:, :, 256 * g : 256 * (g + 1)].rearrange("p a (q t e) -> p a t q e", t=4, e=2),
             )
             w2p.append(perm)
+
+        permute_w2(0)
         v_words = late_tile([P, 2 * S], U32, "v_words", 7)
         vw = [v_words[:, a * S : (a + 1) * S] for a in range(2)]
         for a in range(2):
@@ -227,6 +229,7 @@ def tile_list_subsumption_box_features_kernel(
             cast(on_vector, rounded[:].rearrange("p (c i t) -> p c t i", i=4, t=4), src)
             w4r[g, nh] = rounded
 
+        load_w3(0, 8)
         load_w1(0, 0, 1)
         load_w1(0, 1, 2)
         load_w1(1, 0, 3)
@@ -235,6 +238,7 @@ def tile_list_subsumption_box_features_kernel(
         for g in range(2):
             load_w4(g, 5 + g)
 
+        permute_w2(1)
         permute_w3(0)
         product_b(0)
         for tp in range(2):

@@ -18,6 +18,8 @@ ACT = mybir.ActivationFunctionType
 
 P = 128
 HALF = S // 2
+KB = 1024
+SLOT = 8 * KB
 
 
 def tile_list_subsumption_box_features_kernel(
@@ -26,133 +28,144 @@ def tile_list_subsumption_box_features_kernel(
     nc = tc.nc
     with ExitStack() as ctx:
         keep = ctx.enter_context(tc.tile_pool(name="keep", bufs=1))
-        late = ctx.enter_context(tc.tile_pool(name="late", bufs=1))
-        early = ctx.enter_context(tc.tile_pool(name="early", bufs=1))
+        stage = ctx.enter_context(tc.tile_pool(name="stage", bufs=1))
         psum = ctx.enter_context(tc.psum_pool(name="psum", bufs=8))
 
-        def tl(shape, dtype, name, tag=None):
+        def kept(shape, dtype, name, tag=None):
             return keep.tile(shape, dtype, name=name, tag=tag or name, align_bytes=64)
 
-        def late_tile(shape, dtype, name, slot):
-            return late.tile(shape, dtype, name=name, offset=slot * 8192, align_bytes=64)
-
-        def early_tile(shape, dtype, name, slot):
-            return early.tile(shape, dtype, name=name, offset=slot * 8192, align_bytes=64)
+        def staged(shape, dtype, name, offset):
+            return stage.tile(shape, dtype, name=name, offset=offset, align_bytes=64)
 
         offsets = keep.tile([P, S // 16], U16, name="offsets")
         nc.sync.dma_start(offsets[:], offs)
 
-        w2raw = tl([P, 2, 512], I32, "w2raw")
-        nc.sync.dma_start(w2raw[:], w2_words.bitcast(I32).rearrange("a p n -> p a n"))
-        swin = [tl([P, T], U8, "swin0"), tl([P, T], U8, "swin1")]
-        wsc_raw = tl([P, 4 * H], U8, "wsc_raw")
-        for a in range(2):
-            nc.vector.memset(swin[a][:].bitcast(I32), 0)
-            nc.sync.dma_start(swin[a][:].bitcast(I32)[0:P:8, :], tab_scales[a].bitcast(I32))
-        zeros = early_tile([P, 3 * 2048], I32, "zeros", 0)
-        nc.gpsimd.memset(wsc_raw[:].bitcast(I32)[:, 512:1024], 0)
-        nc.vector.memset(zeros[:, 0:8], 0)
-        nc.vector.tensor_copy(wsc_raw[:].bitcast(I32)[:, 0:512], zeros[:, 0:1].to_broadcast([P, 512]))
-        for x, src in enumerate((w2_scales, w3_scales)):
-            dst = wsc_raw[:].bitcast(I32)[0:P:8, x * 512 : (x + 1) * 512]
-            nc.sync.dma_start(dst.rearrange("q (a n) -> q a n", a=2), src.bitcast(I32).rearrange("a q n -> q a n"))
+        w2view = w2_words.bitcast(I32).rearrange("a p (g n) -> g p a n", g=2)
+        w2raw = [staged([P, 2, 256], I32, "w2raw0", 28 * KB)]
+        nc.sync.dma_start(w2raw[0][:], w2view[0])
 
-        b3c = tl([P, 2, 16], F32, "b3c")
+        swin = [staged([P, T], U8, "swin0", 36 * KB), kept([P, T], U8, "swin1")]
+        wsc_raw = [staged([P, 512], I32, "wsc_raw%d" % x, (30 + 2 * x) * KB) for x in range(2)]
+        zeros = staged([P, 32], I32, "zeros", 10 * KB - 64)
+
+        def load_scale_rows(dst, src):
+            nc.sync.dma_start(dst[0:P:8].rearrange("q (a n) -> q a n", a=2), src.bitcast(I32).rearrange("a q n -> q a n"))
+
+        nc.gpsimd.memset(swin[0][:].bitcast(I32), 0)
+        nc.sync.dma_start(swin[0][:].bitcast(I32)[0:P:8, :], tab_scales[0].bitcast(I32))
+        b3c = kept([P, 2, 16], F32, "b3c")
         b3v = b3.rearrange("(g q s) -> q g s", g=2, s=16)
         for e in range(4):
             nc.gpsimd.dma_start(b3c[e:P:4, :, 0:13], b3v[:, :, e : e + 13])
-        twin = [early_tile([P, T], I32, "twin0", 1)]
-        nc.sync.dma_start(twin[0][:], tab_words[0].rearrange("p t i -> p (t i)").bitcast(I32))
-        twin.append(early_tile([P, T], I32, "twin1", 2))
-        nc.sync.dma_start(twin[1][:], tab_words[1].rearrange("p t i -> p (t i)").bitcast(I32))
-        w1raw = {}
+        bqc = kept([P, 4], F32, "bqc")
+        with nc.allow_non_contiguous_dma(reason="small bias columns"):
+            nc.gpsimd.dma_start(bqc[:], bq.rearrange("(u p) -> p u", p=P))
+        nc.vector.memset(swin[1][:].bitcast(I32), 0)
+        nc.sync.dma_start(swin[1][:].bitcast(I32)[0:P:8, :], tab_scales[1].bitcast(I32))
+        nc.vector.memset(zeros[:], 0)
+        nc.vector.tensor_copy(wsc_raw[0][:], zeros[:, 0:1].to_broadcast([P, 512]))
+        load_scale_rows(wsc_raw[0][:], w2_scales)
+        twin = []
+        for a in range(2):
+            twin.append(staged([P, T], I32, "twin%d" % a, (2 + 8 * a) * KB))
+            nc.sync.dma_start(twin[a][:], tab_words[a].rearrange("p t i -> p (t i)").bitcast(I32))
+        nc.vector.memset(wsc_raw[1][:], 0)
+        load_scale_rows(wsc_raw[1][:], w3_scales)
 
-        def load_w1(g, a, tag):
-            raw = late_tile([P, 4, 512], F32, "w1raw%d%d" % (g, a), tag)
+        w2p = {}
+
+        def permute_w2(g):
+            w2p[g] = staged([P, 2, 256], I32, "w2p1", 10 * KB) if g else kept([P, 2, 256], I32, "w2p0")
+            nc.vector.tensor_copy(
+                w2p[g][:].rearrange("p a (t q e) -> p a t q e", t=4, e=2),
+                w2raw[g][:].rearrange("p a (q t e) -> p a t q e", t=4, e=2),
+            )
+
+        def permute_scales(dst, src):
+            nc.vector.tensor_copy(
+                dst.rearrange("p (x t Q i) -> p x Q t i", x=4, t=4, i=4),
+                src.rearrange("p (x Q i t) -> p x Q t i", x=4, t=4, i=4),
+            )
+
+        def move_rows(plane):
+            for r in range(1, 4):
+                nc.sync.dma_start(plane[r:P:32, :], plane[8 * r : P : 32, :])
+
+        permute_w2(0)
+        sgath = staged([P, 2 * S], U8, "sgath", 20 * KB)
+        for a in range(2):
+            nc.vector.tensor_copy(sgath[:, a * S : (a + 1) * S], swin[a][:].indirect(offsets[:]))
+
+        w2raw.append(staged([P, 2, 256], I32, "w2raw1", 36 * KB))
+        nc.sync.dma_start(w2raw[1][:], w2view[1])
+        planes = kept([P, 2 * S + 2 * H], U8, "planes")
+        planes3 = staged([P, 2 * H], U8, "planes3", 8 * KB)
+        planes_i = planes[:].bitcast(I32)
+        permute_scales(planes_i[:, 256:768], wsc_raw[0][:])
+        nc.vector.tensor_copy(planes_i[:, 0:256], sgath[:].bitcast(I32))
+        move_rows(planes_i)
+
+        v_words = kept([P, 2 * S], U32, "v_words")
+
+        def gather_words(a):
+            nc.vector.tensor_copy(v_words[:, a * S : (a + 1) * S], twin[a][:].bitcast(U32).indirect(offsets[:]))
+
+        w1raw, w3raw, w4raw = {}, {}, {}
+
+        def load_w1(g, a, offset):
+            raw = staged([P, 4, 512], F32, "w1raw%d%d" % (g, a), offset)
             nc.sync.dma_start(raw[:], w1[512 * a : 512 * (a + 1), 512 * g : 512 * (g + 1)].rearrange("(p j) c -> p j c", j=4))
             w1raw[g, a] = raw
 
-
-        w3raw = {}
-
-        def load_w3(g, slot):
-            raw = late_tile([P, 2, 512], I32, "w3raw%d" % g, slot)
+        def load_w3(g):
+            raw = staged([P, 2, 512], I32, "w3raw%d" % g, (30, 36)[g] * KB)
             words = w3_words.rearrange("a p n i -> a p (n i)").bitcast(I32)
             nc.sync.dma_start(raw[:], words[:, :, 512 * g : 512 * (g + 1)].rearrange("a p n -> p a n"))
             w3raw[g] = raw
 
+        def load_w4(g, offset):
+            raw = staged([P, 4, N], F32, "w4raw%d" % g, offset)
+            rows = w4[512 * g : 512 * (g + 1), :].rearrange("(q t e) n -> e q t n", t=4, e=4)
+            for e in range(4):
+                nc.sync.dma_start(raw[e:P:4, :, :], rows[e])
+            w4raw[g] = raw
 
-        sgath = late_tile([P, 9 * 8192], U8, "sgath", 0)
-        for a in range(2):
-            nc.vector.tensor_copy(sgath[:, a * S : (a + 1) * S], swin[a][:].indirect(offsets[:]))
-        bqc = tl([P, 4], F32, "bqc", "swin1")
-        with nc.allow_non_contiguous_dma(reason="small bias columns"):
-            nc.gpsimd.dma_start(bqc[:], bq.rearrange("(u p) -> p u", p=P))
-
-
-        planes = tl([P, 2 * S + 4 * H], U8, "planes")
-        planes_i = planes[:].bitcast(I32)
-        nc.vector.tensor_copy(
-            planes_i[:, 256:1280].rearrange("p (x t Q i) -> p x Q t i", x=8, t=4, i=4),
-            wsc_raw[:].bitcast(I32).rearrange("p (x Q i t) -> p x Q t i", x=8, t=4, i=4),
-        )
-        nc.vector.tensor_copy(planes_i[:, 0:256], sgath[:, 0 : 2 * S].bitcast(I32))
-        for r in range(1, 4):
-            nc.sync.dma_start(planes_i[r:P:32, :], planes_i[8 * r : P : 32, :])
-
-        w2p, w3p = [], []
-        w2perm = tl([P, 2, 2, 256], I32, "w2p", "wsc_raw")
-
-        def permute_w2(g):
-            perm = w2perm[:, g, :, :]
-            nc.vector.tensor_copy(
-                perm.rearrange("p a (t q e) -> p a t q e", t=4, e=2),
-                w2raw[:, :, 256 * g : 256 * (g + 1)].rearrange("p a (q t e) -> p a t q e", t=4, e=2),
-            )
-            w2p.append(perm)
-
-        permute_w2(0)
-        v_words = late_tile([P, 2 * S], U32, "v_words", 7)
-        vw = [v_words[:, a * S : (a + 1) * S] for a in range(2)]
-        for a in range(2):
-            nc.vector.tensor_copy(vw[a], twin[a][:].bitcast(U32).indirect(offsets[:]))
+        w3p = {}
 
         def permute_w3(g):
-            perm = tl([P, 2, 512], I32, "w3p%d" % g, ("w2raw", "b00")[g])
+            w3p[g] = staged([P, 2, 512], I32, "w3p%d" % g, (40, 50)[g] * KB)
             nc.vector.tensor_copy(
-                perm[:].rearrange("p a (t q e) -> p a t q e", t=4, e=4),
+                w3p[g][:].rearrange("p a (t q e) -> p a t q e", t=4, e=4),
                 w3raw[g][:].rearrange("p a (q t e) -> p a t q e", t=4, e=4),
             )
-            w3p.append(perm)
 
-        def v_operand(a, j0, n):
-            return dict(rhs=vw[a][:, j0 : j0 + n].bitcast(FP8X4), rhs_scale=planes[:, a * S + j0 : a * S + j0 + n])
+        def v_operand(a):
+            return dict(rhs=v_words[:, a * S : (a + 1) * S].bitcast(FP8X4), rhs_scale=planes[:, a * S : (a + 1) * S])
 
         def w_scale(x, a, g, t):
-            c0 = 2 * S + 2 * H * x + H * a + 512 * g + P * t
-            return planes[:, c0 : c0 + P]
+            c0 = H * a + 512 * g + P * t
+            return planes3[:, c0 : c0 + P] if x else planes[:, 2 * S + c0 : 2 * S + c0 + P]
 
-        b_sb, c_sb = {}, {}
+        b_sb, c_sb, ab = {}, {}, {}
 
         def product_b(g):
-            for tp in range(2):
-                b_sb[g, tp] = tl([P, 2, S], F32, "b%d%d" % (g, tp))
-                for t in (2 * tp, 2 * tp + 1):
-                    bank = psum.tile([P, S], F32, name="bank", tag="bank")
-                    for a in range(2):
-                        nc.tensor.matmul_mx(
-                            bank[:], lhsT=w2p[g][:, a, 64 * t : 64 * (t + 1)].bitcast(U8).bitcast(FP4X4),
-                            lhsT_scale=w_scale(0, a, g, t), start=(a == 0), stop=(a == 1), **v_operand(a, 0, S))
-                    nc.scalar.copy(b_sb[g, tp][:, t % 2, :], bank[:])
+            for t in range(4):
+                b_sb[g, t] = staged([P, S], F32, "b%d%d" % (g, t), (44 + 10 * g + 2 * t) * KB)
+                bank = psum.tile([P, S], F32, name="bank", tag="bank")
+                for a in range(2):
+                    nc.tensor.matmul_mx(
+                        bank[:], lhsT=w2p[g][:, a, 64 * t : 64 * (t + 1)].bitcast(U8).bitcast(FP4X4),
+                        lhsT_scale=w_scale(0, a, g, t), start=(a == 0), stop=(a == 1), **v_operand(a))
+                nc.scalar.copy(b_sb[g, t][:], bank[:])
 
         def product_c(g):
-            c_sb[g] = late_tile([P, 4, S], F32, "c1", 4) if g else tl([P, 4, S], F32, "c0")
+            c_sb[g] = staged([P, 4, S], F32, "c%d" % g, (12, 20)[g] * KB)
             for t in range(4):
                 bank = psum.tile([P, S], F32, name="bank", tag="bank")
                 for a in range(2):
                     nc.tensor.matmul_mx(
                         bank[:], lhsT=w3p[g][:, a, P * t : P * (t + 1)].bitcast(FP8X4),
-                        lhsT_scale=w_scale(1, a, g, t), start=(a == 0), stop=(a == 1), **v_operand(a, 0, S))
+                        lhsT_scale=w_scale(1, a, g, t), start=(a == 0), stop=(a == 1), **v_operand(a))
                 nc.scalar.activation(c_sb[g][:, t, :], bank[:], ACT.Identity, bias=b3c[:, g, 4 * t : 4 * t + 1])
 
         def cast(on_vector, dst, src):
@@ -161,26 +174,22 @@ def tile_list_subsumption_box_features_kernel(
             else:
                 nc.scalar.copy(dst, src)
 
-        def quantize(name, rounded):
-            codes = tl([P, 256], U32, name + "_codes")
-            scales = tl([P, 256], U8, name + "_scales")
+        def quantize(name, rounded, offset=None):
+            if offset is None:
+                codes = kept([P, 256], U32, name + "_codes")
+            else:
+                codes = staged([P, 256], U32, name + "_codes", offset)
+            scales = kept([P, 256], U8, name + "_scales")
             nc.vector.quantize_mx(codes[:].bitcast(FP8X4), scales[:], rounded[:])
             return codes, scales
 
         w1r, w1q = {}, {}
 
-        w1r10 = []
-
-        def w1r_tile(g, a, tp):
-            if (g, a) == (1, 0):
-                if not w1r10:
-                    w1r10.append(tl([P, 2, 1024], BF16, "w1r10", "w2raw"))
-                return w1r10[0][:, tp, :]
-            reuse = {(1, 1, 0): "b01", (1, 1, 1): "wsc_raw"}
-            return tl([P, 1024], BF16, "w1r%d%d%d" % (g, a, tp), reuse.get((g, a, tp)))[:]
-
         def round_w1(g, a, tp, on_vector):
-            rounded = w1r_tile(g, a, tp)
+            if g:
+                rounded = staged([P, 1024], BF16, "w1r1%d%d" % (a, tp), ((10, 74), (10, 74))[a][tp] * KB)
+            else:
+                rounded = staged([P, 1024], BF16, "w1r0%d%d" % (a, tp), (70 - 8 * a + 2 * tp) * KB)
             src = w1raw[g, a][:].rearrange("p j (q t e) -> p t q j e", t=4, e=4)[:, 2 * tp : 2 * tp + 2]
             cast(on_vector, rounded[:].rearrange("p (t q e j) -> p t q j e", t=2, e=4, j=4), src)
             w1r[g, a, tp] = rounded
@@ -188,117 +197,123 @@ def tile_list_subsumption_box_features_kernel(
         def quant_w1(g, a, tp):
             w1q[g, a, tp] = quantize("w1q%d%d%d" % (g, a, tp), w1r[g, a, tp])
 
-        hq = {}
+        def product_a(g):
+            ab[g] = kept([P, 4, S], F32, "ab1") if g else staged([P, 4, S], F32, "ab0", 28 * KB)
+            for t in range(4):
+                bank = psum.tile([P, S], F32, name="bank", tag="bank")
+                cols = slice(P * (t % 2), P * (t % 2 + 1))
+                for a in range(2):
+                    codes, scales = w1q[g, a, t // 2]
+                    nc.tensor.matmul_mx(
+                        bank[:], lhsT=codes[:, cols].bitcast(FP8X4), lhsT_scale=scales[:, cols],
+                        start=(a == 0), stop=(a == 1), **v_operand(a))
+                nc.vector.tensor_tensor(ab[g][:, t, :], bank[:], b_sb[g, t][:], ALU.mult)
 
-        def product_a(g, jh):
-            js = slice(jh * HALF, (jh + 1) * HALF)
-            ab = tl([P, 4, HALF], F32, "ab%d%d" % (g, jh))
-            for tp in range(2):
-                bank = psum.tile([P, 2, HALF], F32, name="bank", tag="bank")
-                for t2 in range(2):
-                    for a in range(2):
-                        codes, scales = w1q[g, a, tp]
-                        nc.tensor.matmul_mx(
-                            bank[:, t2, :], lhsT=codes[:, P * t2 : P * (t2 + 1)].bitcast(FP8X4),
-                            lhsT_scale=scales[:, P * t2 : P * (t2 + 1)], start=(a == 0), stop=(a == 1),
-                            **v_operand(a, jh * HALF, HALF))
-                nc.vector.tensor_tensor(ab[:, 2 * tp : 2 * tp + 2, :], bank[:], b_sb[g, tp][:, :, js], ALU.mult)
-            return ab
+        h, hq = {}, {}
 
-        def make_h(g, jh, ab):
+        def make_h(g, jh):
             js = slice(jh * HALF, (jh + 1) * HALF)
-            h = tl([P, 4 * HALF], BF16, "h%d%d" % (g, jh), "wsc_raw" if (g, jh) == (1, 1) else None)
+            h[g, jh] = staged([P, 4 * HALF], BF16, "h%d%d" % (g, jh), ((10, 74), (52, 8))[g][jh] * KB)
             nc.vector.tensor_tensor(
-                h[:].rearrange("p (c i t) -> p c t i", i=4, t=4),
-                ab[:].rearrange("p t (c i) -> p c t i", i=4),
+                h[g, jh][:].rearrange("p (c i t) -> p c t i", i=4, t=4),
+                ab[g][:, :, js].rearrange("p t (c i) -> p c t i", i=4),
                 c_sb[g][:, :, js].rearrange("p t (c i) -> p c t i", i=4), ALU.max)
-            return h
 
-        w4raw, w4r, w4q = {}, {}, {}
+        def quant_h(g, jh):
+            hq[g, jh] = quantize("hq%d%d" % (g, jh), h[g, jh], offset=None if g else (56 + 2 * jh) * KB)
 
-        def load_w4(g, tag):
-            raw = late_tile([P, 4, N], F32, "w4raw%d" % g, tag)
-            rows = w4[512 * g : 512 * (g + 1), :].rearrange("(q t e) n -> e q t n", t=4, e=4)
-            for e in range(4):
-                nc.sync.dma_start(raw[e:P:4, :, :], rows[e])
-            w4raw[g] = raw
+        w4r, w4q = {}, {}
 
         def round_w4(g, nh, on_vector):
-            rounded = tl([P, 1024], BF16, "w4r%d%d" % (g, nh), ("b00", "w2raw", "b01", "wsc_raw")[2 * g + nh])
+            if g == 0:
+                rounded = staged([P, 1024], BF16, "w4r0%d" % nh, (50 + 2 * nh) * KB)[:]
+            else:
+                if nh == 0:
+                    w4r[1] = staged([P, 2, 1024], BF16, "w4r1", 8 * KB)
+                rounded = w4r[1][:, nh, :]
             src = w4raw[g][:, :, 256 * nh : 256 * (nh + 1)].rearrange("p t (c i) -> p c t i", i=4)
             cast(on_vector, rounded[:].rearrange("p (c i t) -> p c t i", i=4, t=4), src)
             w4r[g, nh] = rounded
 
-        load_w3(0, 8)
-        load_w1(0, 0, 1)
-        load_w1(0, 1, 2)
-        load_w1(1, 0, 3)
-        load_w3(1, 0)
-        load_w1(1, 1, 4)
-        for g in range(2):
-            load_w4(g, 5 + g)
+        def quant_w4(g, nh):
+            w4q[g, nh] = quantize("w4q%d%d" % (g, nh), w4r[g, nh], offset=((60, 61), (59, 57))[g][nh] * KB)
 
-        permute_w2(1)
-        permute_w3(0)
-        product_b(0)
-        for tp in range(2):
-            round_w1(0, 0, tp, True)
-        product_c(0)
-        for tp in range(2):
-            quant_w1(0, 0, tp)
-        for tp in range(2):
-            round_w1(0, 1, tp, True)
-        for tp in range(2):
-            quant_w1(0, 1, tp)
-        ab00 = product_a(0, 0)
-        ab01 = product_a(0, 1)
-        for tp in range(2):
-            round_w1(1, 0, tp, False)
-        product_b(1)
-        permute_w3(1)
-        h00 = make_h(0, 0, ab00)
-        h01 = make_h(0, 1, ab01)
-        round_w1(1, 1, 0, True)
-        round_w1(1, 1, 1, False)
-        for a in range(2):
-            for tp in range(2):
-                quant_w1(1, a, tp)
-        product_c(1)
-        ab10 = product_a(1, 0)
-        hq[0, 0] = quantize("hq00", h00)
-        hq[0, 1] = quantize("hq01", h01)
-        for g in range(2):
-            for nh in range(2):
-                round_w4(g, nh, False)
-        ab11 = product_a(1, 1)
-        h10 = make_h(1, 0, ab10)
-        for nh in range(2):
-            w4q[0, nh] = quantize("w4q0%d" % nh, w4r[0, nh])
-        hq[1, 0] = quantize("hq10", h10)
-        for nh in range(2):
-            w4q[1, nh] = quantize("w4q1%d" % nh, w4r[1, nh])
-        h11 = make_h(1, 1, ab11)
-        hq[1, 1] = quantize("hq11", h11)
+        out_banks = {}
 
-        def out_pass(bank, g, jh, u):
+        def out_pass(g, jh, u):
+            if g == 0:
+                out_banks[jh, u] = psum.tile([P, HALF], F32, name="bank", tag="bank")
             cols = slice(P * (u % 2), P * (u % 2 + 1))
             codes, scales = w4q[g, u // 2]
             nc.tensor.matmul_mx(
-                bank[:], lhsT=codes[:, cols].bitcast(FP8X4), lhsT_scale=scales[:, cols],
+                out_banks[jh, u][:], lhsT=codes[:, cols].bitcast(FP8X4), lhsT_scale=scales[:, cols],
                 rhs=hq[g, jh][0][:].bitcast(FP8X4), rhs_scale=hq[g, jh][1][:], start=(g == 0), stop=(g == 1))
 
-        banks = {}
-        for jh in range(2):
+        def out_half(jh):
             for u in range(4):
-                banks[jh, u] = psum.tile([P, HALF], F32, name="bank", tag="bank")
-                out_pass(banks[jh, u], 0, jh, u)
-        for jh in range(2):
-            for u in range(4):
-                bank = banks[jh, u]
-                out_pass(bank, 1, jh, u)
-                res = tl([P, HALF], F32, "res%d%d" % (jh, u))
+                out_pass(1, jh, u)
+                bank = out_banks[jh, u]
+                res = kept([P, HALF], F32, "res%d%d" % (jh, u))
                 if jh == 0 or u % 2 == 0:
                     nc.scalar.activation(res[:], bank[:], ACT.Identity, bias=bqc[:, u : u + 1])
                 else:
                     nc.vector.tensor_scalar(res[:], bank[:], bqc[:, u : u + 1], None, ALU.add)
                 nc.sync.dma_start(out[P * u : P * (u + 1), jh * HALF : (jh + 1) * HALF], res[:])
+
+        load_w1(0, 0, 20 * KB)
+        gather_words(0)
+        load_w1(0, 1, 0)
+        permute_scales(planes3[:].bitcast(I32), wsc_raw[1][:])
+        move_rows(planes3[:].bitcast(I32))
+        load_w3(0)
+        gather_words(1)
+        load_w1(1, 0, 12 * KB)
+        permute_w2(1)
+        load_w3(1)
+        product_b(0)
+        product_b(1)
+        for tp in range(2):
+            round_w1(0, 0, tp, True)
+        load_w1(1, 1, 20 * KB)
+        for tp in range(2):
+            quant_w1(0, 0, tp)
+        for tp in range(2):
+            round_w1(0, 1, tp, True)
+        load_w4(0, 0)
+        for tp in range(2):
+            quant_w1(0, 1, tp)
+        load_w4(1, 62 * KB)
+        permute_w3(0)
+        product_a(0)
+        round_w1(1, 0, 0, False)
+        round_w1(1, 0, 1, False)
+        product_c(0)
+        permute_w3(1)
+        for tp in range(2):
+            quant_w1(1, 0, tp)
+        round_w1(1, 1, 0, True)
+        round_w1(1, 1, 1, True)
+        product_c(1)
+        quant_w1(1, 1, 0)
+        quant_w1(1, 1, 1)
+        make_h(0, 0)
+        make_h(0, 1)
+        product_a(1)
+        for g in range(2):
+            for nh in range(2):
+                round_w4(g, nh, False)
+        quant_h(0, 0)
+        quant_h(0, 1)
+        for nh in range(2):
+            quant_w4(0, nh)
+        for jh in range(2):
+            for u in range(4):
+                out_pass(0, jh, u)
+        make_h(1, 0)
+        quant_w4(1, 0)
+        quant_h(1, 0)
+        quant_w4(1, 1)
+        make_h(1, 1)
+        quant_h(1, 1)
+        out_half(0)
+        out_half(1)

@@ -125,9 +125,9 @@ def tile_list_subsumption_box_features_kernel(
 
         def load_w4(g, offset):
             raw = staged([P, 4, N], F32, "w4raw%d" % g, offset)
-            rows = w4[512 * g : 512 * (g + 1), :].rearrange("(q t e) n -> e q t n", t=4, e=4)
-            for e in range(4):
-                nc.sync.dma_start(raw[e:P:4, :, :], rows[e])
+            rows = w4[512 * g : 512 * (g + 1), :].rearrange("(q t e) n -> t q e n", t=4, e=4)
+            for t in range(4):
+                nc.sync.dma_start(raw[:, t, :], rows[t])
             w4raw[g] = raw
 
         w3p = {}
@@ -213,7 +213,7 @@ def tile_list_subsumption_box_features_kernel(
 
         def make_h(g, jh):
             js = slice(jh * HALF, (jh + 1) * HALF)
-            h[g, jh] = staged([P, 4 * HALF], BF16, "h%d%d" % (g, jh), ((10, 74), (52, 8))[g][jh] * KB)
+            h[g, jh] = staged([P, 4 * HALF], BF16, "h%d%d" % (g, jh), ((10, 74), (52, 40))[g][jh] * KB)
             nc.vector.tensor_tensor(
                 h[g, jh][:].rearrange("p (c i t) -> p c t i", i=4, t=4),
                 ab[g][:, :, js].rearrange("p t (c i) -> p c t i", i=4),
@@ -229,7 +229,7 @@ def tile_list_subsumption_box_features_kernel(
                 rounded = staged([P, 1024], BF16, "w4r0%d" % nh, (50 + 2 * nh) * KB)[:]
             else:
                 if nh == 0:
-                    w4r[1] = staged([P, 2, 1024], BF16, "w4r1", 8 * KB)
+                    w4r[1] = staged([P, 2, 1024], BF16, "w4r1", 40 * KB)
                 rounded = w4r[1][:, nh, :]
             src = w4raw[g][:, :, 256 * nh : 256 * (nh + 1)].rearrange("p t (c i) -> p c t i", i=4)
             cast(on_vector, rounded[:].rearrange("p (c i t) -> p c t i", i=4, t=4), src)

@@ -40,11 +40,10 @@ def tile_list_subsumption_box_features_kernel(
         offsets = keep.tile([P, S // 16], U16, name="offsets")
         nc.sync.dma_start(offsets[:], offs)
 
-        w2view = w2_words.bitcast(I32).rearrange("a p (g n) -> g p a n", g=2)
-        w2raw = [staged([P, 2, 256], I32, "w2raw0", 28 * KB)]
-        nc.sync.dma_start(w2raw[0][:], w2view[0])
+        w2raw = staged([P, 2, 512], I32, "w2raw", 36 * KB)
+        nc.sync.dma_start(w2raw[:], w2_words.bitcast(I32).rearrange("a p n -> p a n"))
 
-        swin = [staged([P, T], U8, "swin0", 36 * KB), kept([P, T], U8, "swin1")]
+        swin = [kept([P, T], U8, "swin0"), kept([P, T], U8, "swin1")]
         wsc_raw = [staged([P, 512], I32, "wsc_raw%d" % x, (30 + 2 * x) * KB) for x in range(2)]
         zeros = staged([P, 32], I32, "zeros", 10 * KB - 64)
 
@@ -57,9 +56,6 @@ def tile_list_subsumption_box_features_kernel(
         b3v = b3.rearrange("(g q s) -> q g s", g=2, s=16)
         for e in range(4):
             nc.gpsimd.dma_start(b3c[e:P:4, :, 0:13], b3v[:, :, e : e + 13])
-        bqc = kept([P, 4], F32, "bqc")
-        with nc.allow_non_contiguous_dma(reason="small bias columns"):
-            nc.gpsimd.dma_start(bqc[:], bq.rearrange("(u p) -> p u", p=P))
         nc.vector.memset(swin[1][:].bitcast(I32), 0)
         nc.sync.dma_start(swin[1][:].bitcast(I32)[0:P:8, :], tab_scales[1].bitcast(I32))
         nc.vector.memset(zeros[:], 0)
@@ -78,7 +74,7 @@ def tile_list_subsumption_box_features_kernel(
             w2p[g] = staged([P, 2, 256], I32, "w2p1", 10 * KB) if g else kept([P, 2, 256], I32, "w2p0")
             nc.vector.tensor_copy(
                 w2p[g][:].rearrange("p a (t q e) -> p a t q e", t=4, e=2),
-                w2raw[g][:].rearrange("p a (q t e) -> p a t q e", t=4, e=2),
+                w2raw[:, :, 256 * g : 256 * (g + 1)].rearrange("p a (q t e) -> p a t q e", t=4, e=2),
             )
 
         def permute_scales(dst, src):
@@ -87,23 +83,21 @@ def tile_list_subsumption_box_features_kernel(
                 src.rearrange("p (x Q i t) -> p x Q t i", x=4, t=4, i=4),
             )
 
-        def move_rows(plane):
+        def move_rows(queue, plane):
             for r in range(1, 4):
-                nc.sync.dma_start(plane[r:P:32, :], plane[8 * r : P : 32, :])
+                queue.dma_start(plane[r:P:32, :], plane[8 * r : P : 32, :])
 
         permute_w2(0)
-        sgath = staged([P, 2 * S], U8, "sgath", 20 * KB)
+        sgath = staged([P, 2 * S], U8, "sgath", 80 * KB - S)
         for a in range(2):
             nc.vector.tensor_copy(sgath[:, a * S : (a + 1) * S], swin[a][:].indirect(offsets[:]))
 
-        w2raw.append(staged([P, 2, 256], I32, "w2raw1", 36 * KB))
-        nc.sync.dma_start(w2raw[1][:], w2view[1])
         planes = kept([P, 2 * S + 2 * H], U8, "planes")
         planes3 = staged([P, 2 * H], U8, "planes3", 8 * KB)
         planes_i = planes[:].bitcast(I32)
         permute_scales(planes_i[:, 256:768], wsc_raw[0][:])
         nc.vector.tensor_copy(planes_i[:, 0:256], sgath[:].bitcast(I32))
-        move_rows(planes_i)
+        move_rows(nc.sync, planes_i)
 
         v_words = kept([P, 2 * S], U32, "v_words")
 
@@ -159,7 +153,7 @@ def tile_list_subsumption_box_features_kernel(
                 nc.scalar.copy(b_sb[g, t][:], bank[:])
 
         def product_c(g):
-            c_sb[g] = staged([P, 4, S], F32, "c%d" % g, (12, 20)[g] * KB)
+            c_sb[g] = staged([P, 4, S], F32, "c%d" % g, (12, 80)[g] * KB)
             for t in range(4):
                 bank = psum.tile([P, S], F32, name="bank", tag="bank")
                 for a in range(2):
@@ -258,23 +252,27 @@ def tile_list_subsumption_box_features_kernel(
                     nc.scalar.activation(res[:], bank[:], ACT.Identity, bias=bqc[:, u : u + 1])
                 else:
                     nc.vector.tensor_scalar(res[:], bank[:], bqc[:, u : u + 1], None, ALU.add)
-                nc.sync.dma_start(out[P * u : P * (u + 1), jh * HALF : (jh + 1) * HALF], res[:])
+                queue = nc.scalar if (jh, u) == (1, 2) else nc.sync
+                queue.dma_start(out[P * u : P * (u + 1), jh * HALF : (jh + 1) * HALF], res[:])
 
-        load_w1(0, 0, 20 * KB)
+        load_w1(0, 0, 80 * KB)
         gather_words(0)
         load_w1(0, 1, 0)
         permute_scales(planes3[:].bitcast(I32), wsc_raw[1][:])
-        move_rows(planes3[:].bitcast(I32))
+        move_rows(nc.gpsimd, planes3[:].bitcast(I32))
         load_w3(0)
         gather_words(1)
         load_w1(1, 0, 12 * KB)
         permute_w2(1)
         load_w3(1)
         product_b(0)
+        bqc = kept([P, 4], F32, "bqc", "w2p0")
+        with nc.allow_non_contiguous_dma(reason="small bias columns"):
+            nc.gpsimd.dma_start(bqc[:], bq.rearrange("(u p) -> p u", p=P))
         product_b(1)
         for tp in range(2):
             round_w1(0, 0, tp, True)
-        load_w1(1, 1, 20 * KB)
+        load_w1(1, 1, 80 * KB)
         for tp in range(2):
             quant_w1(0, 0, tp)
         for tp in range(2):

@@ -52,10 +52,6 @@ def tile_list_subsumption_box_features_kernel(
 
         nc.gpsimd.memset(swin[0][:].bitcast(I32), 0)
         nc.sync.dma_start(swin[0][:].bitcast(I32)[0:P:8, :], tab_scales[0].bitcast(I32))
-        b3c = kept([P, 2, 16], F32, "b3c")
-        b3v = b3.rearrange("(g q s) -> q g s", g=2, s=16)
-        for e in range(4):
-            nc.gpsimd.dma_start(b3c[e:P:4, :, 0:13], b3v[:, :, e : e + 13])
         nc.vector.memset(swin[1][:].bitcast(I32), 0)
         nc.sync.dma_start(swin[1][:].bitcast(I32)[0:P:8, :], tab_scales[1].bitcast(I32))
         nc.vector.memset(zeros[:], 0)
@@ -153,7 +149,7 @@ def tile_list_subsumption_box_features_kernel(
                 nc.scalar.copy(b_sb[g, t][:], bank[:])
 
         def product_c(g):
-            c_sb[g] = staged([P, 4, S], F32, "c%d" % g, (12, 80)[g] * KB)
+            c_sb[g] = staged([P, 4, S], F32, "c%d" % g, (12 * KB + 128, 80 * KB)[g])
             for t in range(4):
                 bank = psum.tile([P, S], F32, name="bank", tag="bank")
                 for a in range(2):
@@ -183,7 +179,7 @@ def tile_list_subsumption_box_features_kernel(
             if g:
                 rounded = staged([P, 1024], BF16, "w1r1%d%d" % (a, tp), ((10, 74), (10, 74))[a][tp] * KB)
             else:
-                rounded = staged([P, 1024], BF16, "w1r0%d%d" % (a, tp), (70 - 8 * a + 2 * tp) * KB)
+                rounded = staged([P, 1024], BF16, "w1r0%d%d" % (a, tp), ((88, 62)[a] + 2 * tp) * KB)
             src = w1raw[g, a][:].rearrange("p j (q t e) -> p t q j e", t=4, e=4)[:, 2 * tp : 2 * tp + 2]
             cast(on_vector, rounded[:].rearrange("p (t q e j) -> p t q j e", t=2, e=4, j=4), src)
             w1r[g, a, tp] = rounded
@@ -259,16 +255,17 @@ def tile_list_subsumption_box_features_kernel(
         gather_words(0)
         load_w1(0, 1, 0)
         permute_scales(planes3[:].bitcast(I32), wsc_raw[1][:])
-        move_rows(nc.gpsimd, planes3[:].bitcast(I32))
+        move_rows(nc.sync, planes3[:].bitcast(I32))
         load_w3(0)
         gather_words(1)
-        load_w1(1, 0, 12 * KB)
+        load_w1(1, 0, 12 * KB + 128)
+        b3c = staged([P, 2, 16], F32, "b3c", 12 * KB)
+        b3v = b3.rearrange("(g q s) -> q g s", g=2, s=16)
+        for e in range(4):
+            nc.sync.dma_start(b3c[e:P:4, :, 0:13], b3v[:, :, e : e + 13])
         permute_w2(1)
         load_w3(1)
         product_b(0)
-        bqc = kept([P, 4], F32, "bqc", "w2p0")
-        with nc.allow_non_contiguous_dma(reason="small bias columns"):
-            nc.gpsimd.dma_start(bqc[:], bq.rearrange("(u p) -> p u", p=P))
         product_b(1)
         for tp in range(2):
             round_w1(0, 0, tp, True)
@@ -280,7 +277,10 @@ def tile_list_subsumption_box_features_kernel(
         load_w4(0, 0)
         for tp in range(2):
             quant_w1(0, 1, tp)
-        load_w4(1, 62 * KB)
+        load_w4(1, 62 * KB + 64)
+        bqc = staged([P, 4], F32, "bqc", 62 * KB)
+        with nc.allow_non_contiguous_dma(reason="small bias columns"):
+            nc.sync.dma_start(bqc[:], bq.rearrange("(u p) -> p u", p=P))
         permute_w3(0)
         product_a(0)
         round_w1(1, 0, 0, False)

@@ -188,7 +188,7 @@ def tile_list_subsumption_box_features_kernel(
             w1q[g, a, tp] = quantize("w1q%d%d%d" % (g, a, tp), w1r[g, a, tp])
 
         def product_a(g):
-            ab[g] = kept([P, 4, S], F32, "ab1") if g else staged([P, 4, S], F32, "ab0", 28 * KB)
+            ab[g] = kept([P, 4, S], F32, "ab1") if g else staged([P, 4, S], F32, "ab0", 23 * KB)
             for t in range(4):
                 bank = psum.tile([P, S], F32, name="bank", tag="bank")
                 cols = slice(P * (t % 2), P * (t % 2 + 1))
@@ -203,14 +203,14 @@ def tile_list_subsumption_box_features_kernel(
 
         def make_h(g, jh):
             js = slice(jh * HALF, (jh + 1) * HALF)
-            h[g, jh] = staged([P, 4 * HALF], BF16, "h%d%d" % (g, jh), ((10, 74), (52, 40))[g][jh] * KB)
+            h[g, jh] = staged([P, 4 * HALF], BF16, "h%d%d" % (g, jh), ((10, 75), (52, 40))[g][jh] * KB)
             nc.vector.tensor_tensor(
-                h[g, jh][:].rearrange("p (c i t) -> p c t i", i=4, t=4),
-                ab[g][:, :, js].rearrange("p t (c i) -> p c t i", i=4),
-                c_sb[g][:, :, js].rearrange("p t (c i) -> p c t i", i=4), ALU.max)
+                h[g, jh][:].rearrange("p (c i t) -> p c t i", i=2, t=4),
+                ab[g][:, :, js].rearrange("p t (c i) -> p c t i", i=2),
+                c_sb[g][:, :, js].rearrange("p t (c i) -> p c t i", i=2), ALU.max)
 
         def quant_h(g, jh):
-            hq[g, jh] = quantize("hq%d%d" % (g, jh), h[g, jh], offset=None if g else (56 + 2 * jh) * KB)
+            hq[g, jh] = quantize("hq%d%d" % (g, jh), h[g, jh], offset=None if g else (74, 58)[jh] * KB)
 
         w4r, w4q = {}, {}
 
@@ -221,8 +221,8 @@ def tile_list_subsumption_box_features_kernel(
                 if nh == 0:
                     w4r[1] = staged([P, 2, 1024], BF16, "w4r1", 40 * KB)
                 rounded = w4r[1][:, nh, :]
-            src = w4raw[g][:, :, 256 * nh : 256 * (nh + 1)].rearrange("p t (c i) -> p c t i", i=4)
-            cast(on_vector, rounded[:].rearrange("p (c i t) -> p c t i", i=4, t=4), src)
+            src = w4raw[g][:, :, 256 * nh : 256 * (nh + 1)].rearrange("p t (c i) -> p c t i", i=2)
+            cast(on_vector, rounded[:].rearrange("p (c i t) -> p c t i", i=2, t=4), src)
             w4r[g, nh] = rounded
 
         def quant_w4(g, nh):
@@ -277,11 +277,11 @@ def tile_list_subsumption_box_features_kernel(
         load_w4(0, 0)
         for tp in range(2):
             quant_w1(0, 1, tp)
-        load_w4(1, 62 * KB + 64)
-        bqc = staged([P, 4], F32, "bqc", 62 * KB)
+        load_w4(1, 62 * KB)
+        permute_w3(0)
+        bqc = staged([P, 4], F32, "bqc", 33 * KB)
         with nc.allow_non_contiguous_dma(reason="small bias columns"):
             nc.sync.dma_start(bqc[:], bq.rearrange("(u p) -> p u", p=P))
-        permute_w3(0)
         product_a(0)
         round_w1(1, 0, 0, False)
         round_w1(1, 0, 1, False)
@@ -296,11 +296,11 @@ def tile_list_subsumption_box_features_kernel(
         quant_w1(1, 1, 1)
         make_h(0, 0)
         make_h(0, 1)
+        quant_h(0, 0)
         product_a(1)
         for g in range(2):
             for nh in range(2):
                 round_w4(g, nh, False)
-        quant_h(0, 0)
         quant_h(0, 1)
         for nh in range(2):
             quant_w4(0, nh)

@@ -19,7 +19,28 @@ ACT = mybir.ActivationFunctionType
 P = 128
 HALF = S // 2
 KB = 1024
-SLOT = 8 * KB
+
+AT_TABLE = (2 * KB, 10 * KB)
+AT_ZEROS = 10 * KB - 64
+AT_W2_RAW = 36 * KB
+AT_SCALE_ROWS = (30 * KB, 32 * KB)
+AT_GATHERED_SCALES = 80 * KB - S
+AT_W1_RAW = {(0, 0): 80 * KB, (0, 1): 0, (1, 0): 12 * KB + 128, (1, 1): 80 * KB}
+AT_W3_RAW = (30 * KB, 36 * KB)
+AT_B3 = 12 * KB
+AT_W4_RAW = (0, 62 * KB)
+AT_BQ = 33 * KB
+AT_W3_PLANES = 8 * KB
+AT_W2_GROUP1 = 10 * KB
+AT_B = (44 * KB, 54 * KB)
+AT_W3 = (40 * KB, 50 * KB)
+AT_AB0 = 23 * KB
+AT_C = (12 * KB + 128, 80 * KB)
+AT_W1_ROUNDED = {(0, 0): (88 * KB, 90 * KB), (0, 1): (62 * KB, 64 * KB), (1, 0): (10 * KB, 74 * KB), (1, 1): (10 * KB, 74 * KB)}
+AT_H = ((10 * KB, 75 * KB), (52 * KB, 40 * KB))
+AT_H0_CODES = (74 * KB, 58 * KB)
+AT_W4_ROUNDED = (50 * KB, 40 * KB)
+AT_W4_CODES = ((59 * KB, 61 * KB), (60 * KB, 57 * KB))
 
 
 def tile_list_subsumption_box_features_kernel(
@@ -28,290 +49,280 @@ def tile_list_subsumption_box_features_kernel(
     nc = tc.nc
     with ExitStack() as ctx:
         keep = ctx.enter_context(tc.tile_pool(name="keep", bufs=1))
-        stage = ctx.enter_context(tc.tile_pool(name="stage", bufs=1))
+        shared = ctx.enter_context(tc.tile_pool(name="shared", bufs=1))
         psum = ctx.enter_context(tc.psum_pool(name="psum", bufs=8))
 
-        def kept(shape, dtype, name, tag=None):
-            return keep.tile(shape, dtype, name=name, tag=tag or name, align_bytes=64)
+        def kept(shape, dtype, name):
+            return keep.tile(shape, dtype, name=name, align_bytes=64)
 
-        def staged(shape, dtype, name, offset):
-            return stage.tile(shape, dtype, name=name, offset=offset, align_bytes=64)
+        def placed(shape, dtype, name, offset):
+            return shared.tile(shape, dtype, name=name, offset=offset, align_bytes=64)
 
         offsets = keep.tile([P, S // 16], U16, name="offsets")
         nc.sync.dma_start(offsets[:], offs)
 
-        w2raw = staged([P, 2, 512], I32, "w2raw", 36 * KB)
-        nc.sync.dma_start(w2raw[:], w2_words.bitcast(I32).rearrange("a p n -> p a n"))
+        w2_raw = placed([P, 2, 512], I32, "w2_raw", AT_W2_RAW)
+        nc.sync.dma_start(w2_raw[:], w2_words.bitcast(I32).rearrange("a p n -> p a n"))
 
-        swin = [kept([P, T], U8, "swin0"), kept([P, T], U8, "swin1")]
-        wsc_raw = [staged([P, 512], I32, "wsc_raw%d" % x, (30 + 2 * x) * KB) for x in range(2)]
-        zeros = staged([P, 32], I32, "zeros", 10 * KB - 64)
+        scale_window = [kept([P, T], U8, "scale_window0"), kept([P, T], U8, "scale_window1")]
+        scale_rows = [placed([P, 512], I32, "scale_rows%d" % x, AT_SCALE_ROWS[x]) for x in range(2)]
+        zeros = placed([P, 32], I32, "zeros", AT_ZEROS)
 
         def load_scale_rows(dst, src):
-            nc.sync.dma_start(dst[0:P:8].rearrange("q (a n) -> q a n", a=2), src.bitcast(I32).rearrange("a q n -> q a n"))
+            nc.sync.dma_start(dst[0:P:8].rearrange("m (a n) -> m a n", a=2), src.bitcast(I32).rearrange("a m n -> m a n"))
 
-        nc.gpsimd.memset(swin[0][:].bitcast(I32), 0)
-        nc.sync.dma_start(swin[0][:].bitcast(I32)[0:P:8, :], tab_scales[0].bitcast(I32))
-        nc.vector.memset(swin[1][:].bitcast(I32), 0)
-        nc.sync.dma_start(swin[1][:].bitcast(I32)[0:P:8, :], tab_scales[1].bitcast(I32))
+        nc.gpsimd.memset(scale_window[0][:].bitcast(I32), 0)
+        nc.sync.dma_start(scale_window[0][:].bitcast(I32)[0:P:8, :], tab_scales[0].bitcast(I32))
+        nc.vector.memset(scale_window[1][:].bitcast(I32), 0)
+        nc.sync.dma_start(scale_window[1][:].bitcast(I32)[0:P:8, :], tab_scales[1].bitcast(I32))
         nc.vector.memset(zeros[:], 0)
-        nc.vector.tensor_copy(wsc_raw[0][:], zeros[:, 0:1].to_broadcast([P, 512]))
-        load_scale_rows(wsc_raw[0][:], w2_scales)
-        twin = []
+        nc.vector.tensor_copy(
+            scale_rows[0][:].rearrange("p (n w) -> p n w", w=32), zeros[:].unsqueeze(1).to_broadcast([P, 16, 32]))
+        load_scale_rows(scale_rows[0][:], w2_scales)
+        table = []
         for a in range(2):
-            twin.append(staged([P, T], I32, "twin%d" % a, (2 + 8 * a) * KB))
-            nc.sync.dma_start(twin[a][:], tab_words[a].rearrange("p t i -> p (t i)").bitcast(I32))
-        nc.vector.memset(wsc_raw[1][:], 0)
-        load_scale_rows(wsc_raw[1][:], w3_scales)
+            table.append(placed([P, T], I32, "table%d" % a, AT_TABLE[a]))
+            nc.sync.dma_start(table[a][:], tab_words[a].rearrange("p t i -> p (t i)").bitcast(I32))
+        nc.vector.memset(scale_rows[1][:], 0)
+        load_scale_rows(scale_rows[1][:], w3_scales)
 
-        w2p = {}
+        w2_cols, w3_cols = {}, {}
 
-        def permute_w2(g):
-            w2p[g] = staged([P, 2, 256], I32, "w2p1", 10 * KB) if g else kept([P, 2, 256], I32, "w2p0")
+        def reorder_w2(g):
+            w2_cols[g] = placed([P, 2, 256], I32, "w2_cols1", AT_W2_GROUP1) if g else kept([P, 2, 256], I32, "w2_cols0")
             nc.vector.tensor_copy(
-                w2p[g][:].rearrange("p a (t q e) -> p a t q e", t=4, e=2),
-                w2raw[:, :, 256 * g : 256 * (g + 1)].rearrange("p a (q t e) -> p a t q e", t=4, e=2),
+                w2_cols[g][:].rearrange("p a (t q e) -> p a t q e", t=4, e=2),
+                w2_raw[:, :, 256 * g : 256 * (g + 1)].rearrange("p a (q t e) -> p a t q e", t=4, e=2),
             )
 
-        def permute_scales(dst, src):
+        def reorder_scales(dst, src):
             nc.vector.tensor_copy(
-                dst.rearrange("p (x t Q i) -> p x Q t i", x=4, t=4, i=4),
-                src.rearrange("p (x Q i t) -> p x Q t i", x=4, t=4, i=4),
+                dst.rearrange("p (x t qh ql) -> p x qh t ql", x=4, t=4, ql=4),
+                src.rearrange("p (x qh ql t) -> p x qh t ql", x=4, t=4, ql=4),
             )
 
-        def move_rows(queue, plane):
-            for r in range(1, 4):
-                queue.dma_start(plane[r:P:32, :], plane[8 * r : P : 32, :])
+        def move_rows(plane):
+            for i in range(1, 4):
+                nc.sync.dma_start(plane[i:P:32, :], plane[8 * i : P : 32, :])
 
-        permute_w2(0)
-        sgath = staged([P, 2 * S], U8, "sgath", 80 * KB - S)
+        reorder_w2(0)
+        gathered_scales = placed([P, 2 * S], U8, "gathered_scales", AT_GATHERED_SCALES)
         for a in range(2):
-            nc.vector.tensor_copy(sgath[:, a * S : (a + 1) * S], swin[a][:].indirect(offsets[:]))
+            nc.vector.tensor_copy(gathered_scales[:, a * S : (a + 1) * S], scale_window[a][:].indirect(offsets[:]))
 
         planes = kept([P, 2 * S + 2 * H], U8, "planes")
-        planes3 = staged([P, 2 * H], U8, "planes3", 8 * KB)
-        planes_i = planes[:].bitcast(I32)
-        permute_scales(planes_i[:, 256:768], wsc_raw[0][:])
-        nc.vector.tensor_copy(planes_i[:, 0:256], sgath[:].bitcast(I32))
-        move_rows(nc.sync, planes_i)
+        w3_planes = placed([P, 2 * H], U8, "w3_planes", AT_W3_PLANES)
+        planes_i32 = planes[:].bitcast(I32)
+        reorder_scales(planes_i32[:, 256:768], scale_rows[0][:])
+        nc.vector.tensor_copy(planes_i32[:, 0:256], gathered_scales[:].bitcast(I32))
+        move_rows(planes_i32)
 
         v_words = kept([P, 2 * S], U32, "v_words")
 
         def gather_words(a):
-            nc.vector.tensor_copy(v_words[:, a * S : (a + 1) * S], twin[a][:].bitcast(U32).indirect(offsets[:]))
-
-        w1raw, w3raw, w4raw = {}, {}, {}
-
-        def load_w1(g, a, offset):
-            raw = staged([P, 4, 512], F32, "w1raw%d%d" % (g, a), offset)
-            nc.sync.dma_start(raw[:], w1[512 * a : 512 * (a + 1), 512 * g : 512 * (g + 1)].rearrange("(p j) c -> p j c", j=4))
-            w1raw[g, a] = raw
-
-        def load_w3(g):
-            raw = staged([P, 2, 512], I32, "w3raw%d" % g, (30, 36)[g] * KB)
-            words = w3_words.rearrange("a p n i -> a p (n i)").bitcast(I32)
-            nc.sync.dma_start(raw[:], words[:, :, 512 * g : 512 * (g + 1)].rearrange("a p n -> p a n"))
-            w3raw[g] = raw
-
-        def load_w4(g, offset):
-            raw = staged([P, 4, N], F32, "w4raw%d" % g, offset)
-            rows = w4[512 * g : 512 * (g + 1), :].rearrange("(q t e) n -> t q e n", t=4, e=4)
-            for t in range(4):
-                nc.sync.dma_start(raw[:, t, :], rows[t])
-            w4raw[g] = raw
-
-        w3p = {}
-
-        def permute_w3(g):
-            w3p[g] = staged([P, 2, 512], I32, "w3p%d" % g, (40, 50)[g] * KB)
-            nc.vector.tensor_copy(
-                w3p[g][:].rearrange("p a (t q e) -> p a t q e", t=4, e=4),
-                w3raw[g][:].rearrange("p a (q t e) -> p a t q e", t=4, e=4),
-            )
+            nc.vector.tensor_copy(v_words[:, a * S : (a + 1) * S], table[a][:].bitcast(U32).indirect(offsets[:]))
 
         def v_operand(a):
             return dict(rhs=v_words[:, a * S : (a + 1) * S].bitcast(FP8X4), rhs_scale=planes[:, a * S : (a + 1) * S])
 
-        def w_scale(x, a, g, t):
-            c0 = H * a + 512 * g + P * t
-            return planes3[:, c0 : c0 + P] if x else planes[:, 2 * S + c0 : 2 * S + c0 + P]
+        w1_raw, w3_raw, w4_raw = {}, {}, {}
+
+        def load_w1(g, a):
+            w1_raw[g, a] = placed([P, 4, 512], F32, "w1_raw%d%d" % (g, a), AT_W1_RAW[g, a])
+            chunk = w1[512 * a : 512 * (a + 1), 512 * g : 512 * (g + 1)]
+            nc.sync.dma_start(w1_raw[g, a][:], chunk.rearrange("(p i) c -> p i c", i=4))
+
+        def load_w3(g):
+            w3_raw[g] = placed([P, 2, 512], I32, "w3_raw%d" % g, AT_W3_RAW[g])
+            words = w3_words.rearrange("a p n i -> a p (n i)").bitcast(I32)
+            nc.sync.dma_start(w3_raw[g][:], words[:, :, 512 * g : 512 * (g + 1)].rearrange("a p n -> p a n"))
+
+        def load_w4(g):
+            w4_raw[g] = placed([P, 4, N], F32, "w4_raw%d" % g, AT_W4_RAW[g])
+            rows = w4[512 * g : 512 * (g + 1), :].rearrange("(q t e) n -> t q e n", t=4, e=4)
+            for t in range(4):
+                nc.sync.dma_start(w4_raw[g][:, t, :], rows[t])
+
+        def reorder_w3(g):
+            w3_cols[g] = placed([P, 2, 512], I32, "w3_cols%d" % g, AT_W3[g])
+            nc.vector.tensor_copy(
+                w3_cols[g][:].rearrange("p a (t q e) -> p a t q e", t=4, e=4),
+                w3_raw[g][:].rearrange("p a (q t e) -> p a t q e", t=4, e=4),
+            )
 
         b_sb, c_sb, ab = {}, {}, {}
 
         def product_b(g):
             for t in range(4):
-                b_sb[g, t] = staged([P, S], F32, "b%d%d" % (g, t), (44 + 10 * g + 2 * t) * KB)
+                b_sb[g, t] = placed([P, S], F32, "b%d%d" % (g, t), AT_B[g] + 2 * KB * t)
                 bank = psum.tile([P, S], F32, name="bank", tag="bank")
                 for a in range(2):
+                    c0 = 2 * S + H * a + 512 * g + P * t
                     nc.tensor.matmul_mx(
-                        bank[:], lhsT=w2p[g][:, a, 64 * t : 64 * (t + 1)].bitcast(U8).bitcast(FP4X4),
-                        lhsT_scale=w_scale(0, a, g, t), start=(a == 0), stop=(a == 1), **v_operand(a))
+                        bank[:], lhsT=w2_cols[g][:, a, 64 * t : 64 * (t + 1)].bitcast(U8).bitcast(FP4X4),
+                        lhsT_scale=planes[:, c0 : c0 + P], start=(a == 0), stop=(a == 1), **v_operand(a))
                 nc.scalar.copy(b_sb[g, t][:], bank[:])
 
         def product_c(g):
-            c_sb[g] = staged([P, 4, S], F32, "c%d" % g, (12 * KB + 128, 80 * KB)[g])
+            c_sb[g] = placed([P, 4, S], F32, "c%d" % g, AT_C[g])
             for t in range(4):
                 bank = psum.tile([P, S], F32, name="bank", tag="bank")
                 for a in range(2):
+                    c0 = H * a + 512 * g + P * t
                     nc.tensor.matmul_mx(
-                        bank[:], lhsT=w3p[g][:, a, P * t : P * (t + 1)].bitcast(FP8X4),
-                        lhsT_scale=w_scale(1, a, g, t), start=(a == 0), stop=(a == 1), **v_operand(a))
-                nc.scalar.activation(c_sb[g][:, t, :], bank[:], ACT.Identity, bias=b3c[:, g, 4 * t : 4 * t + 1])
-
-        def cast(on_vector, dst, src):
-            if on_vector:
-                nc.vector.tensor_copy(dst, src)
-            else:
-                nc.scalar.copy(dst, src)
+                        bank[:], lhsT=w3_cols[g][:, a, P * t : P * (t + 1)].bitcast(FP8X4),
+                        lhsT_scale=w3_planes[:, c0 : c0 + P], start=(a == 0), stop=(a == 1), **v_operand(a))
+                nc.scalar.activation(c_sb[g][:, t, :], bank[:], ACT.Identity, bias=b3_cols[:, g, 4 * t : 4 * t + 1])
 
         def quantize(name, rounded, offset=None):
-            if offset is None:
-                codes = kept([P, 256], U32, name + "_codes")
-            else:
-                codes = staged([P, 256], U32, name + "_codes", offset)
+            codes = kept([P, 256], U32, name) if offset is None else placed([P, 256], U32, name, offset)
             scales = kept([P, 256], U8, name + "_scales")
-            nc.vector.quantize_mx(codes[:].bitcast(FP8X4), scales[:], rounded[:])
+            nc.vector.quantize_mx(codes[:].bitcast(FP8X4), scales[:], rounded)
             return codes, scales
 
-        w1r, w1q = {}, {}
+        w1_rounded, w1_mx = {}, {}
 
-        def round_w1(g, a, tp, on_vector):
-            if g:
-                rounded = staged([P, 1024], BF16, "w1r1%d%d" % (a, tp), ((10, 74), (10, 74))[a][tp] * KB)
+        def round_w1(g, a, tp):
+            rounded = placed([P, 1024], BF16, "w1_rounded%d%d%d" % (g, a, tp), AT_W1_ROUNDED[g, a][tp])
+            src = w1_raw[g, a][:].rearrange("p i (q t e) -> p t q i e", t=4, e=4)[:, 2 * tp : 2 * tp + 2]
+            dst = rounded[:].rearrange("p (t q e i) -> p t q i e", t=2, e=4, i=4)
+            if (g, a) == (1, 0):
+                nc.scalar.copy(dst, src)
             else:
-                rounded = staged([P, 1024], BF16, "w1r0%d%d" % (a, tp), ((88, 62)[a] + 2 * tp) * KB)
-            src = w1raw[g, a][:].rearrange("p j (q t e) -> p t q j e", t=4, e=4)[:, 2 * tp : 2 * tp + 2]
-            cast(on_vector, rounded[:].rearrange("p (t q e j) -> p t q j e", t=2, e=4, j=4), src)
-            w1r[g, a, tp] = rounded
+                nc.vector.tensor_copy(dst, src)
+            w1_rounded[g, a, tp] = rounded
 
-        def quant_w1(g, a, tp):
-            w1q[g, a, tp] = quantize("w1q%d%d%d" % (g, a, tp), w1r[g, a, tp])
+        def quantize_w1(g, a, tp):
+            w1_mx[g, a, tp] = quantize("w1_mx%d%d%d" % (g, a, tp), w1_rounded[g, a, tp][:])
 
-        def product_a(g):
-            ab[g] = kept([P, 4, S], F32, "ab1") if g else staged([P, 4, S], F32, "ab0", 23 * KB)
-            for t in range(4):
-                bank = psum.tile([P, S], F32, name="bank", tag="bank")
-                cols = slice(P * (t % 2), P * (t % 2 + 1))
-                for a in range(2):
-                    codes, scales = w1q[g, a, t // 2]
-                    nc.tensor.matmul_mx(
-                        bank[:], lhsT=codes[:, cols].bitcast(FP8X4), lhsT_scale=scales[:, cols],
-                        start=(a == 0), stop=(a == 1), **v_operand(a))
-                nc.vector.tensor_tensor(ab[g][:, t, :], bank[:], b_sb[g, t][:], ALU.mult)
+        def product_a(g, t):
+            bank = psum.tile([P, S], F32, name="bank", tag="bank")
+            cols = slice(P * (t % 2), P * (t % 2 + 1))
+            for a in range(2):
+                codes, scales = w1_mx[g, a, t // 2]
+                nc.tensor.matmul_mx(
+                    bank[:], lhsT=codes[:, cols].bitcast(FP8X4), lhsT_scale=scales[:, cols],
+                    start=(a == 0), stop=(a == 1), **v_operand(a))
+            return bank
 
-        h, hq = {}, {}
+        def multiply(g, t, bank):
+            nc.vector.tensor_tensor(ab[g][:, t, :], bank[:], b_sb[g, t][:], ALU.mult)
 
-        def make_h(g, jh):
-            js = slice(jh * HALF, (jh + 1) * HALF)
-            h[g, jh] = staged([P, 4 * HALF], BF16, "h%d%d" % (g, jh), ((10, 75), (52, 40))[g][jh] * KB)
+        h, h_mx, w4_rounded, w4_mx = {}, {}, {}, {}
+
+        def make_h(g, half):
+            js = slice(half * HALF, (half + 1) * HALF)
+            h[g, half] = placed([P, 4 * HALF], BF16, "h%d%d" % (g, half), AT_H[g][half])
             nc.vector.tensor_tensor(
-                h[g, jh][:].rearrange("p (c i t) -> p c t i", i=2, t=4),
-                ab[g][:, :, js].rearrange("p t (c i) -> p c t i", i=2),
-                c_sb[g][:, :, js].rearrange("p t (c i) -> p c t i", i=2), ALU.max)
+                h[g, half][:].rearrange("p (c j t) -> p c t j", j=2, t=4),
+                ab[g][:, :, js].rearrange("p t (c j) -> p c t j", j=2),
+                c_sb[g][:, :, js].rearrange("p t (c j) -> p c t j", j=2), ALU.max)
 
-        def quant_h(g, jh):
-            hq[g, jh] = quantize("hq%d%d" % (g, jh), h[g, jh], offset=None if g else (74, 58)[jh] * KB)
+        def quantize_h(g, half):
+            h_mx[g, half] = quantize("h_mx%d%d" % (g, half), h[g, half][:], None if g else AT_H0_CODES[half])
 
-        w4r, w4q = {}, {}
+        def round_w4(g, nh, rounded):
+            src = w4_raw[g][:, :, 256 * nh : 256 * (nh + 1)].rearrange("p t (c n) -> p c t n", n=2)
+            nc.scalar.copy(rounded.rearrange("p (c n t) -> p c t n", n=2, t=4), src)
+            w4_rounded[g, nh] = rounded
 
-        def round_w4(g, nh, on_vector):
-            if g == 0:
-                rounded = staged([P, 1024], BF16, "w4r0%d" % nh, (50 + 2 * nh) * KB)[:]
-            else:
-                if nh == 0:
-                    w4r[1] = staged([P, 2, 1024], BF16, "w4r1", 40 * KB)
-                rounded = w4r[1][:, nh, :]
-            src = w4raw[g][:, :, 256 * nh : 256 * (nh + 1)].rearrange("p t (c i) -> p c t i", i=2)
-            cast(on_vector, rounded[:].rearrange("p (c i t) -> p c t i", i=2, t=4), src)
-            w4r[g, nh] = rounded
-
-        def quant_w4(g, nh):
-            w4q[g, nh] = quantize("w4q%d%d" % (g, nh), w4r[g, nh], offset=((60, 61), (59, 57))[g][nh] * KB)
+        def quantize_w4(g, nh):
+            w4_mx[g, nh] = quantize("w4_mx%d%d" % (g, nh), w4_rounded[g, nh], AT_W4_CODES[g][nh])
 
         out_banks = {}
 
-        def out_pass(g, jh, u):
+        def out_pass(g, half, u):
             if g == 0:
-                out_banks[jh, u] = psum.tile([P, HALF], F32, name="bank", tag="bank")
+                out_banks[half, u] = psum.tile([P, HALF], F32, name="bank", tag="bank")
             cols = slice(P * (u % 2), P * (u % 2 + 1))
-            codes, scales = w4q[g, u // 2]
+            codes, scales = w4_mx[g, u // 2]
             nc.tensor.matmul_mx(
-                out_banks[jh, u][:], lhsT=codes[:, cols].bitcast(FP8X4), lhsT_scale=scales[:, cols],
-                rhs=hq[g, jh][0][:].bitcast(FP8X4), rhs_scale=hq[g, jh][1][:], start=(g == 0), stop=(g == 1))
+                out_banks[half, u][:], lhsT=codes[:, cols].bitcast(FP8X4), lhsT_scale=scales[:, cols],
+                rhs=h_mx[g, half][0][:].bitcast(FP8X4), rhs_scale=h_mx[g, half][1][:], start=(g == 0), stop=(g == 1))
 
-        def out_half(jh):
+        def finish_half(half):
             for u in range(4):
-                out_pass(1, jh, u)
-                bank = out_banks[jh, u]
-                res = kept([P, HALF], F32, "res%d%d" % (jh, u))
-                if jh == 0 or u % 2 == 0:
-                    nc.scalar.activation(res[:], bank[:], ACT.Identity, bias=bqc[:, u : u + 1])
+                out_pass(1, half, u)
+                result = kept([P, HALF], F32, "result%d%d" % (half, u))
+                if half == 0 or u % 2 == 0:
+                    nc.scalar.activation(result[:], out_banks[half, u][:], ACT.Identity, bias=bq_cols[:, u : u + 1])
                 else:
-                    nc.vector.tensor_scalar(res[:], bank[:], bqc[:, u : u + 1], None, ALU.add)
-                queue = nc.scalar if (jh, u) == (1, 2) else nc.sync
-                queue.dma_start(out[P * u : P * (u + 1), jh * HALF : (jh + 1) * HALF], res[:])
+                    nc.vector.tensor_scalar(result[:], out_banks[half, u][:], bq_cols[:, u : u + 1], None, ALU.add)
+                queue = nc.scalar if (half, u) == (1, 2) else nc.sync
+                queue.dma_start(out[P * u : P * (u + 1), half * HALF : (half + 1) * HALF], result[:])
 
-        load_w1(0, 0, 80 * KB)
+        load_w1(0, 0)
         gather_words(0)
-        load_w1(0, 1, 0)
-        permute_scales(planes3[:].bitcast(I32), wsc_raw[1][:])
-        move_rows(nc.sync, planes3[:].bitcast(I32))
+        load_w1(0, 1)
+        reorder_scales(w3_planes[:].bitcast(I32), scale_rows[1][:])
+        move_rows(w3_planes[:].bitcast(I32))
         load_w3(0)
         gather_words(1)
-        load_w1(1, 0, 12 * KB + 128)
-        b3c = staged([P, 2, 16], F32, "b3c", 12 * KB)
-        b3v = b3.rearrange("(g q s) -> q g s", g=2, s=16)
+        load_w1(1, 0)
+        b3_cols = placed([P, 2, 16], F32, "b3_cols", AT_B3)
+        b3_runs = b3.rearrange("(g q s) -> q g s", g=2, s=16)
         for e in range(4):
-            nc.sync.dma_start(b3c[e:P:4, :, 0:13], b3v[:, :, e : e + 13])
-        permute_w2(1)
+            nc.sync.dma_start(b3_cols[e:P:4, :, 0:13], b3_runs[:, :, e : e + 13])
+        reorder_w2(1)
         load_w3(1)
         product_b(0)
         product_b(1)
         for tp in range(2):
-            round_w1(0, 0, tp, True)
-        load_w1(1, 1, 80 * KB)
+            round_w1(0, 0, tp)
+        load_w1(1, 1)
         for tp in range(2):
-            quant_w1(0, 0, tp)
+            quantize_w1(0, 0, tp)
         for tp in range(2):
-            round_w1(0, 1, tp, True)
-        load_w4(0, 0)
+            round_w1(0, 1, tp)
+        load_w4(0)
         for tp in range(2):
-            quant_w1(0, 1, tp)
-        load_w4(1, 62 * KB)
-        permute_w3(0)
-        bqc = staged([P, 4], F32, "bqc", 33 * KB)
-        with nc.allow_non_contiguous_dma(reason="small bias columns"):
-            nc.sync.dma_start(bqc[:], bq.rearrange("(u p) -> p u", p=P))
-        product_a(0)
-        round_w1(1, 0, 0, False)
-        round_w1(1, 0, 1, False)
+            quantize_w1(0, 1, tp)
+        load_w4(1)
+        reorder_w3(0)
+        bq_cols = placed([P, 4], F32, "bq_cols", AT_BQ)
+        with nc.allow_non_contiguous_dma(reason="one bias value a partition and output tile"):
+            nc.sync.dma_start(bq_cols[:], bq.rearrange("(u p) -> p u", p=P))
+
+        ab[0] = placed([P, 4, S], F32, "ab0", AT_AB0)
+        for t in range(4):
+            multiply(0, t, product_a(0, t))
+        for tp in range(2):
+            round_w1(1, 0, tp)
         product_c(0)
-        permute_w3(1)
+        reorder_w3(1)
         for tp in range(2):
-            quant_w1(1, 0, tp)
-        round_w1(1, 1, 0, True)
-        round_w1(1, 1, 1, True)
+            quantize_w1(1, 0, tp)
+        for tp in range(2):
+            round_w1(1, 1, tp)
         product_c(1)
-        quant_w1(1, 1, 0)
-        quant_w1(1, 1, 1)
-        make_h(0, 0)
-        make_h(0, 1)
-        quant_h(0, 0)
-        product_a(1)
-        for g in range(2):
-            for nh in range(2):
-                round_w4(g, nh, False)
-        quant_h(0, 1)
+        for tp in range(2):
+            quantize_w1(1, 1, tp)
+        for half in range(2):
+            make_h(0, half)
+        quantize_h(0, 0)
+
         for nh in range(2):
-            quant_w4(0, nh)
-        for jh in range(2):
+            round_w4(0, nh, placed([P, 1024], BF16, "w4_rounded0%d" % nh, AT_W4_ROUNDED[0] + 2 * KB * nh)[:])
+        w4_group1 = placed([P, 2, 1024], BF16, "w4_rounded1", AT_W4_ROUNDED[1])
+        for nh in range(2):
+            round_w4(1, nh, w4_group1[:, nh, :])
+
+        ab[1] = kept([P, 4, S], F32, "ab1")
+        for t in range(3):
+            multiply(1, t, product_a(1, t))
+        last_bank = product_a(1, 3)
+        quantize_h(0, 1)
+        quantize_w4(0, 0)
+        multiply(1, 3, last_bank)
+        quantize_w4(0, 1)
+        for half in range(2):
             for u in range(4):
-                out_pass(0, jh, u)
+                out_pass(0, half, u)
         make_h(1, 0)
-        quant_w4(1, 0)
-        quant_h(1, 0)
-        quant_w4(1, 1)
+        quantize_w4(1, 0)
+        quantize_h(1, 0)
+        quantize_w4(1, 1)
         make_h(1, 1)
-        quant_h(1, 1)
-        out_half(0)
-        out_half(1)
+        quantize_h(1, 1)
+        for half in range(2):
+            finish_half(half)

@@ -19,28 +19,32 @@ ACT = mybir.ActivationFunctionType
 P = 128
 HALF = S // 2
 KB = 1024
+CHUNK = 2048
 
-AT_TABLE = (2 * KB, 10 * KB)
-AT_ZEROS = 10 * KB - 64
-AT_W2_RAW = 36 * KB
-AT_SCALE_ROWS = (30 * KB, 32 * KB)
-AT_GATHERED_SCALES = 80 * KB - S
-AT_W1_RAW = {(0, 0): 80 * KB, (0, 1): 0, (1, 0): 12 * KB + 128, (1, 1): 80 * KB}
-AT_W3_RAW = (30 * KB, 36 * KB)
-AT_B3 = 12 * KB
-AT_W4_RAW = (0, 62 * KB)
-AT_BQ = 33 * KB
-AT_W3_PLANES = 8 * KB
-AT_W2_GROUP1 = 10 * KB
-AT_B = (44 * KB, 54 * KB)
-AT_W3 = (40 * KB, 50 * KB)
-AT_AB0 = 23 * KB
-AT_C = (12 * KB + 128, 80 * KB)
-AT_W1_ROUNDED = {(0, 0): (88 * KB, 90 * KB), (0, 1): (62 * KB, 64 * KB), (1, 0): (10 * KB, 74 * KB), (1, 1): (10 * KB, 74 * KB)}
-AT_H = ((10 * KB, 75 * KB), (52 * KB, 40 * KB))
-AT_H0_CODES = (74 * KB, 58 * KB)
-AT_W4_ROUNDED = (50 * KB, 40 * KB)
-AT_W4_CODES = ((59 * KB, 61 * KB), (60 * KB, 57 * KB))
+AT = {
+    "table0": 0,
+    "table1": 8 * KB,
+    "zeros": 8 * KB - 64,
+    "w3_raw": 16 * KB,
+    "gathered_scales": 24 * KB - S,
+    "staging": 24 * KB,
+    "b11": 16 * KB,
+    "w4_rounded11": 16 * KB,
+    "w3_cols0": 94 * KB,
+    "b12": 94 * KB,
+    "b03": 90 * KB,
+    "w1_rounded100": 89 * KB,
+    "w1_rounded101": 91 * KB,
+    "h00": 89 * KB,
+    "w4_rounded01": 89 * KB,
+    "w1_rounded111": 80 * KB,
+    "c1": 73 * KB,
+    "w4_rounded00": 81 * KB,
+    "w1_rounded110": 84 * KB,
+    "b13": 83 * KB,
+    "h01": 85 * KB,
+    "w4_rounded10": 85 * KB,
+}
 
 
 def tile_list_subsumption_box_features_kernel(
@@ -50,279 +54,299 @@ def tile_list_subsumption_box_features_kernel(
     with ExitStack() as ctx:
         keep = ctx.enter_context(tc.tile_pool(name="keep", bufs=1))
         shared = ctx.enter_context(tc.tile_pool(name="shared", bufs=1))
-        psum = ctx.enter_context(tc.psum_pool(name="psum", bufs=8))
+        psum = ctx.enter_context(tc.psum_pool(name="psum", bufs=1))
 
-        def kept(shape, dtype, name):
+        def new(shape, dtype, name):
+            if name in AT:
+                return shared.tile(shape, dtype, name=name, offset=AT[name], align_bytes=64)
             return keep.tile(shape, dtype, name=name, align_bytes=64)
 
-        def placed(shape, dtype, name, offset):
-            return shared.tile(shape, dtype, name=name, offset=offset, align_bytes=64)
+        def bank(letter):
+            return psum.tile([P, S], F32, name="bank" + letter, tag="bank" + letter)
+
+        def clock(name, src):
+            tick = new([P, 1], src.dtype, name)
+            nc.gpsimd.tensor_copy(tick[:], src)
+
+        on_vector, on_scalar = nc.vector.tensor_copy, nc.scalar.copy
 
         offsets = keep.tile([P, S // 16], U16, name="offsets")
+        w2_raw = new([P, 2, 512], I32, "w2_raw")
+        scale_window = [new([P, T], U8, "scale_window0"), new([P, T], U8, "scale_window1")]
+        scale_rows = new([P, 1024], I32, "scale_rows")
+        table, w2_cols, w3_raw, w3_cols, v_words = {}, {}, {}, {}, {}
+
+        def load_table(a):
+            table[a] = new([P, T], I32, "table%d" % a)
+            nc.sync.dma_start(table[a][:], tab_words[a].rearrange("p t i -> p (t i)").bitcast(I32))
+
+        def reorder_w2(g, engine):
+            w2_cols[g] = new([P, 2, 256], U32, "w2_cols%d" % g)
+            engine(
+                w2_cols[g][:].rearrange("p a (t q e) -> p a t q e", t=4, e=2),
+                w2_raw[:].bitcast(U32)[:, :, 256 * g : 256 * (g + 1)].rearrange("p a (q t e) -> p a t q e", t=4, e=2),
+            )
+
+        def load_w3(g):
+            w3_raw[g] = w3_both[:, 1024 * g : 1024 * (g + 1)].rearrange("p (a n) -> p a n", a=2)
+            words = w3_words.rearrange("a p n i -> a p (n i)").bitcast(I32)
+            nc.sync.dma_start(w3_raw[g], words[:, :, 512 * g : 512 * (g + 1)].rearrange("a p n -> p a n"))
+
+        def reorder_w3(g, engine):
+            w3_cols[g] = new([P, 2, 512], U32, "w3_cols%d" % g)
+            engine(
+                w3_cols[g][:].rearrange("p a (t q e) -> p a t q e", t=4, e=4),
+                w3_raw[g].bitcast(U32).rearrange("p a (q t e) -> p a t q e", t=4, e=4),
+            )
+
+        def gather_words(a):
+            v_words[a] = new([P, S], U32, "v_words%d" % a)
+            nc.vector.tensor_copy(v_words[a][:], table[a][:].bitcast(U32).indirect(offsets[:]))
+
         nc.sync.dma_start(offsets[:], offs)
-
-        w2_raw = placed([P, 2, 512], I32, "w2_raw", AT_W2_RAW)
         nc.sync.dma_start(w2_raw[:], w2_words.bitcast(I32).rearrange("a p n -> p a n"))
-
-        scale_window = [kept([P, T], U8, "scale_window0"), kept([P, T], U8, "scale_window1")]
-        scale_rows = [placed([P, 512], I32, "scale_rows%d" % x, AT_SCALE_ROWS[x]) for x in range(2)]
-        zeros = placed([P, 32], I32, "zeros", AT_ZEROS)
-
-        def load_scale_rows(dst, src):
-            nc.sync.dma_start(dst[0:P:8].rearrange("m (a n) -> m a n", a=2), src.bitcast(I32).rearrange("a m n -> m a n"))
-
+        zeros = new([P, 32], I32, "zeros")
         nc.gpsimd.memset(scale_window[0][:].bitcast(I32), 0)
         nc.sync.dma_start(scale_window[0][:].bitcast(I32)[0:P:8, :], tab_scales[0].bitcast(I32))
         nc.vector.memset(scale_window[1][:].bitcast(I32), 0)
         nc.sync.dma_start(scale_window[1][:].bitcast(I32)[0:P:8, :], tab_scales[1].bitcast(I32))
         nc.vector.memset(zeros[:], 0)
         nc.vector.tensor_copy(
-            scale_rows[0][:].rearrange("p (n w) -> p n w", w=32), zeros[:].unsqueeze(1).to_broadcast([P, 16, 32]))
-        load_scale_rows(scale_rows[0][:], w2_scales)
-        table = []
-        for a in range(2):
-            table.append(placed([P, T], I32, "table%d" % a, AT_TABLE[a]))
-            nc.sync.dma_start(table[a][:], tab_words[a].rearrange("p t i -> p (t i)").bitcast(I32))
-        nc.vector.memset(scale_rows[1][:], 0)
-        load_scale_rows(scale_rows[1][:], w3_scales)
+            scale_rows[:].rearrange("p (n w) -> p n w", w=32), zeros[:].unsqueeze(1).to_broadcast([P, 32, 32]))
+        for x, src in enumerate((w2_scales, w3_scales)):
+            nc.sync.dma_start(
+                scale_rows[0:P:8, 512 * x : 512 * (x + 1)].rearrange("m (a n) -> m a n", a=2),
+                src.bitcast(I32).rearrange("a m n -> m a n"))
+        load_table(0)
+        load_table(1)
 
-        w2_cols, w3_cols = {}, {}
-
-        def reorder_w2(g):
-            w2_cols[g] = placed([P, 2, 256], I32, "w2_cols1", AT_W2_GROUP1) if g else kept([P, 2, 256], I32, "w2_cols0")
-            nc.vector.tensor_copy(
-                w2_cols[g][:].rearrange("p a (t q e) -> p a t q e", t=4, e=2),
-                w2_raw[:, :, 256 * g : 256 * (g + 1)].rearrange("p a (q t e) -> p a t q e", t=4, e=2),
-            )
-
-        def reorder_scales(dst, src):
-            nc.vector.tensor_copy(
-                dst.rearrange("p (x t qh ql) -> p x qh t ql", x=4, t=4, ql=4),
-                src.rearrange("p (x qh ql t) -> p x qh t ql", x=4, t=4, ql=4),
-            )
-
-        def move_rows(plane):
-            for i in range(1, 4):
-                nc.sync.dma_start(plane[i:P:32, :], plane[8 * i : P : 32, :])
-
-        reorder_w2(0)
-        gathered_scales = placed([P, 2 * S], U8, "gathered_scales", AT_GATHERED_SCALES)
+        planes = new([P, 2 * S + 4 * H], U8, "planes")
+        reorder_w2(0, on_scalar)
+        nc.scalar.copy(
+            planes[:].bitcast(U32)[:, 256:1280].rearrange("p (x t qh ql) -> p x qh t ql", x=8, t=4, ql=4),
+            scale_rows[:].bitcast(U32).rearrange("p (x qh ql t) -> p x qh t ql", x=8, t=4, ql=4),
+        )
+        reorder_w2(1, on_scalar)
+        gathered_scales = new([P, 2 * S], U8, "gathered_scales")
         for a in range(2):
             nc.vector.tensor_copy(gathered_scales[:, a * S : (a + 1) * S], scale_window[a][:].indirect(offsets[:]))
-
-        planes = kept([P, 2 * S + 2 * H], U8, "planes")
-        w3_planes = placed([P, 2 * H], U8, "w3_planes", AT_W3_PLANES)
         planes_i32 = planes[:].bitcast(I32)
-        reorder_scales(planes_i32[:, 256:768], scale_rows[0][:])
         nc.vector.tensor_copy(planes_i32[:, 0:256], gathered_scales[:].bitcast(I32))
-        move_rows(planes_i32)
-
-        v_words = kept([P, 2 * S], U32, "v_words")
-
-        def gather_words(a):
-            nc.vector.tensor_copy(v_words[:, a * S : (a + 1) * S], table[a][:].bitcast(U32).indirect(offsets[:]))
+        for i in range(1, 4):
+            nc.sync.dma_start(planes_i32[i:P:32, :], planes_i32[8 * i : P : 32, :])
+        gather_words(0)
+        gather_words(1)
 
         def v_operand(a):
-            return dict(rhs=v_words[:, a * S : (a + 1) * S].bitcast(FP8X4), rhs_scale=planes[:, a * S : (a + 1) * S])
+            return dict(rhs=v_words[a][:].bitcast(FP8X4), rhs_scale=planes[:, a * S : (a + 1) * S])
 
-        w1_raw, w3_raw, w4_raw = {}, {}, {}
+        staging = new([P, 6 * CHUNK + 64], F32, "staging")
+
+        def staged(slot):
+            return staging[:, slot * CHUNK : (slot + 1) * CHUNK].rearrange("p (i c) -> p i c", i=4)
+
+        w1_raw = {(g, a): staged(2 * g + a) for g in range(2) for a in range(2)}
+        w4_raw = {g: staged(4 + g) for g in range(2)}
+        b3_cols = staging[:, 6 * CHUNK : 6 * CHUNK + 32].rearrange("p (g s) -> p g s", g=2)
+        bq_cols = staging[:, 6 * CHUNK + 32 : 6 * CHUNK + 36]
 
         def load_w1(g, a):
-            w1_raw[g, a] = placed([P, 4, 512], F32, "w1_raw%d%d" % (g, a), AT_W1_RAW[g, a])
             chunk = w1[512 * a : 512 * (a + 1), 512 * g : 512 * (g + 1)]
-            nc.sync.dma_start(w1_raw[g, a][:], chunk.rearrange("(p i) c -> p i c", i=4))
-
-        def load_w3(g):
-            w3_raw[g] = placed([P, 2, 512], I32, "w3_raw%d" % g, AT_W3_RAW[g])
-            words = w3_words.rearrange("a p n i -> a p (n i)").bitcast(I32)
-            nc.sync.dma_start(w3_raw[g][:], words[:, :, 512 * g : 512 * (g + 1)].rearrange("a p n -> p a n"))
+            nc.sync.dma_start(w1_raw[g, a], chunk.rearrange("(p i) c -> p i c", i=4))
 
         def load_w4(g):
-            w4_raw[g] = placed([P, 4, N], F32, "w4_raw%d" % g, AT_W4_RAW[g])
             rows = w4[512 * g : 512 * (g + 1), :].rearrange("(q t e) n -> t q e n", t=4, e=4)
             for t in range(4):
                 nc.sync.dma_start(w4_raw[g][:, t, :], rows[t])
 
-        def reorder_w3(g):
-            w3_cols[g] = placed([P, 2, 512], I32, "w3_cols%d" % g, AT_W3[g])
-            nc.vector.tensor_copy(
-                w3_cols[g][:].rearrange("p a (t q e) -> p a t q e", t=4, e=4),
-                w3_raw[g][:].rearrange("p a (q t e) -> p a t q e", t=4, e=4),
-            )
+        def load_b3():
+            b3_runs = b3.rearrange("(g q s) -> q g s", g=2, s=16)
+            for e in range(4):
+                nc.sync.dma_start(b3_cols[e:P:4, :, 0:13], b3_runs[:, :, e : e + 13])
 
-        b_sb, c_sb, ab = {}, {}, {}
+        def load_bq():
+            with nc.allow_non_contiguous_dma(reason="one bias value a partition and output tile"):
+                nc.sync.dma_start(bq_cols, bq.rearrange("(u p) -> p u", p=P))
 
-        def product_b(g):
-            for t in range(4):
-                b_sb[g, t] = placed([P, S], F32, "b%d%d" % (g, t), AT_B[g] + 2 * KB * t)
-                bank = psum.tile([P, S], F32, name="bank", tag="bank")
-                for a in range(2):
-                    c0 = 2 * S + H * a + 512 * g + P * t
-                    nc.tensor.matmul_mx(
-                        bank[:], lhsT=w2_cols[g][:, a, 64 * t : 64 * (t + 1)].bitcast(U8).bitcast(FP4X4),
-                        lhsT_scale=planes[:, c0 : c0 + P], start=(a == 0), stop=(a == 1), **v_operand(a))
-                nc.scalar.copy(b_sb[g, t][:], bank[:])
+        w3_both = new([P, 2048], I32, "w3_raw")
+        load_w1(0, 0)
+        load_w1(0, 1)
+        load_w3(0)
+        load_w3(1)
+        load_b3()
+        load_w1(1, 0)
+        load_w1(1, 1)
+        load_w4(0)
+        load_w4(1)
+        load_bq()
 
-        def product_c(g):
-            c_sb[g] = placed([P, 4, S], F32, "c%d" % g, AT_C[g])
-            for t in range(4):
-                bank = psum.tile([P, S], F32, name="bank", tag="bank")
-                for a in range(2):
-                    c0 = H * a + 512 * g + P * t
-                    nc.tensor.matmul_mx(
-                        bank[:], lhsT=w3_cols[g][:, a, P * t : P * (t + 1)].bitcast(FP8X4),
-                        lhsT_scale=w3_planes[:, c0 : c0 + P], start=(a == 0), stop=(a == 1), **v_operand(a))
-                nc.scalar.activation(c_sb[g][:, t, :], bank[:], ACT.Identity, bias=b3_cols[:, g, 4 * t : 4 * t + 1])
+        banks, b_sb, w1_rounded, w1_mx = {}, {}, {}, {}
+        c_sb = [new([P, 4, S], F32, "c0"), new([P, 4, S], F32, "c1")]
+        ab = [new([P, 4, S], F32, "ab0"), new([P, 4, S], F32, "ab1")]
 
-        def quantize(name, rounded, offset=None):
-            codes = kept([P, 256], U32, name) if offset is None else placed([P, 256], U32, name, offset)
-            scales = kept([P, 256], U8, name + "_scales")
+        def first_stage_pass(x, g, t, a, letter=None):
+            if letter:
+                banks[x, g, t] = bank(letter)
+            cols = slice(P * t, P * (t + 1))
+            if x == "a":
+                codes, scales = w1_mx[g, a, t // 2]
+                lhsT, lhsT_scale = codes[:, P * (t % 2) : P * (t % 2 + 1)].bitcast(FP8X4), scales[:, P * (t % 2) : P * (t % 2 + 1)]
+            elif x == "b":
+                c0 = 2 * S + H * a + 512 * g + P * t
+                lhsT, lhsT_scale = w2_cols[g][:, a, 64 * t : 64 * (t + 1)].bitcast(U8).bitcast(FP4X4), planes[:, c0 : c0 + P]
+            else:
+                c0 = 2 * S + 2 * H + H * a + 512 * g + P * t
+                lhsT, lhsT_scale = w3_cols[g][:, a, cols].bitcast(FP8X4), planes[:, c0 : c0 + P]
+            nc.tensor.matmul_mx(
+                banks[x, g, t][:], lhsT=lhsT, lhsT_scale=lhsT_scale, start=bool(letter), stop=not letter, **v_operand(a))
+
+        def product(x, g, t, letter):
+            first_stage_pass(x, g, t, 1, letter)
+            first_stage_pass(x, g, t, 0)
+
+        def empty_b(g, t, engine=on_scalar):
+            b_sb[g, t] = new([P, S], F32, "b%d%d" % (g, t))
+            engine(b_sb[g, t][:], banks["b", g, t][:])
+
+        def empty_c(g, t):
+            nc.scalar.activation(c_sb[g][:, t, :], banks["c", g, t][:], ACT.Identity, bias=b3_cols[:, g, 4 * t : 4 * t + 1])
+
+        def multiply(g, t):
+            nc.vector.tensor_tensor(ab[g][:, t, :], banks["a", g, t][:], b_sb[g, t][:], ALU.mult)
+
+        def quantize(name, rounded):
+            codes = new([P, 256], U32, name)
+            scales = new([P, 256], U8, name + "_scales")
             nc.vector.quantize_mx(codes[:].bitcast(FP8X4), scales[:], rounded)
             return codes, scales
 
-        w1_rounded, w1_mx = {}, {}
-
-        def round_w1(g, a, tp):
-            rounded = placed([P, 1024], BF16, "w1_rounded%d%d%d" % (g, a, tp), AT_W1_ROUNDED[g, a][tp])
-            src = w1_raw[g, a][:].rearrange("p i (q t e) -> p t q i e", t=4, e=4)[:, 2 * tp : 2 * tp + 2]
+        def round_w1(g, a, tp, engine):
+            rounded = new([P, 1024], BF16, "w1_rounded%d%d%d" % (g, a, tp))
+            src = w1_raw[g, a].rearrange("p i (q t e) -> p t q i e", t=4, e=4)[:, 2 * tp : 2 * tp + 2]
             dst = rounded[:].rearrange("p (t q e i) -> p t q i e", t=2, e=4, i=4)
-            if (g, a) == (1, 0):
-                nc.scalar.copy(dst, src)
-            else:
-                nc.vector.tensor_copy(dst, src)
+            engine(dst, src)
             w1_rounded[g, a, tp] = rounded
 
         def quantize_w1(g, a, tp):
             w1_mx[g, a, tp] = quantize("w1_mx%d%d%d" % (g, a, tp), w1_rounded[g, a, tp][:])
 
-        def product_a(g, t):
-            bank = psum.tile([P, S], F32, name="bank", tag="bank")
-            cols = slice(P * (t % 2), P * (t % 2 + 1))
-            for a in range(2):
-                codes, scales = w1_mx[g, a, t // 2]
-                nc.tensor.matmul_mx(
-                    bank[:], lhsT=codes[:, cols].bitcast(FP8X4), lhsT_scale=scales[:, cols],
-                    start=(a == 0), stop=(a == 1), **v_operand(a))
-            return bank
-
-        def multiply(g, t, bank):
-            nc.vector.tensor_tensor(ab[g][:, t, :], bank[:], b_sb[g, t][:], ALU.mult)
-
-        h, h_mx, w4_rounded, w4_mx = {}, {}, {}, {}
+        h, w4_rounded, w4_mx, out_banks = {}, {}, {}, {}
+        h_codes = [new([P, S], U32, "h_codes0"), new([P, S], U32, "h_codes1")]
+        h_scales = [new([P, S], U8, "h_scales0"), new([P, S], U8, "h_scales1")]
 
         def make_h(g, half):
             js = slice(half * HALF, (half + 1) * HALF)
-            h[g, half] = placed([P, 4 * HALF], BF16, "h%d%d" % (g, half), AT_H[g][half])
+            h[g, half] = new([P, 4 * HALF], BF16, "h%d%d" % (g, half))
             nc.vector.tensor_tensor(
                 h[g, half][:].rearrange("p (c j t) -> p c t j", j=2, t=4),
                 ab[g][:, :, js].rearrange("p t (c j) -> p c t j", j=2),
                 c_sb[g][:, :, js].rearrange("p t (c j) -> p c t j", j=2), ALU.max)
 
         def quantize_h(g, half):
-            h_mx[g, half] = quantize("h_mx%d%d" % (g, half), h[g, half][:], None if g else AT_H0_CODES[half])
+            js = slice(half * HALF, (half + 1) * HALF)
+            nc.vector.quantize_mx(h_codes[g][:, js].bitcast(FP8X4), h_scales[g][:, js], h[g, half][:])
 
-        def round_w4(g, nh, rounded):
+        def round_w4(g, nh, engine):
+            rounded = new([P, 1024], BF16, "w4_rounded%d%d" % (g, nh))
             src = w4_raw[g][:, :, 256 * nh : 256 * (nh + 1)].rearrange("p t (c n) -> p c t n", n=2)
-            nc.scalar.copy(rounded.rearrange("p (c n t) -> p c t n", n=2, t=4), src)
+            engine(rounded[:].rearrange("p (c n t) -> p c t n", n=2, t=4), src)
             w4_rounded[g, nh] = rounded
 
         def quantize_w4(g, nh):
-            w4_mx[g, nh] = quantize("w4_mx%d%d" % (g, nh), w4_rounded[g, nh], AT_W4_CODES[g][nh])
+            w4_mx[g, nh] = quantize("w4_mx%d%d" % (g, nh), w4_rounded[g, nh][:])
 
-        out_banks = {}
-
-        def out_pass(g, half, u):
-            if g == 0:
-                out_banks[half, u] = psum.tile([P, HALF], F32, name="bank", tag="bank")
-            cols = slice(P * (u % 2), P * (u % 2 + 1))
+        def out_pass(g, half, u, letter=None):
+            if letter:
+                out_banks[half, u] = bank(letter)
+            cols, js = slice(P * (u % 2), P * (u % 2 + 1)), slice(half * HALF, (half + 1) * HALF)
             codes, scales = w4_mx[g, u // 2]
             nc.tensor.matmul_mx(
-                out_banks[half, u][:], lhsT=codes[:, cols].bitcast(FP8X4), lhsT_scale=scales[:, cols],
-                rhs=h_mx[g, half][0][:].bitcast(FP8X4), rhs_scale=h_mx[g, half][1][:], start=(g == 0), stop=(g == 1))
+                out_banks[half, u][:, 0:HALF], lhsT=codes[:, cols].bitcast(FP8X4), lhsT_scale=scales[:, cols],
+                rhs=h_codes[g][:, js].bitcast(FP8X4), rhs_scale=h_scales[g][:, js], start=bool(letter), stop=not letter)
 
-        def finish_half(half):
-            for u in range(4):
-                out_pass(1, half, u)
-                result = kept([P, HALF], F32, "result%d%d" % (half, u))
-                if half == 0 or u % 2 == 0:
-                    nc.scalar.activation(result[:], out_banks[half, u][:], ACT.Identity, bias=bq_cols[:, u : u + 1])
-                else:
-                    nc.vector.tensor_scalar(result[:], out_banks[half, u][:], bq_cols[:, u : u + 1], None, ALU.add)
-                queue = nc.scalar if (half, u) == (1, 2) else nc.sync
-                queue.dma_start(out[P * u : P * (u + 1), half * HALF : (half + 1) * HALF], result[:])
+        def finish(half, u, on_scalar_engine, queue=nc.sync):
+            result = new([P, HALF], F32, "result%d%d" % (half, u))
+            sums = out_banks[half, u][:, 0:HALF]
+            if on_scalar_engine:
+                nc.scalar.activation(result[:], sums, ACT.Identity, bias=bq_cols[:, u : u + 1])
+            else:
+                nc.vector.tensor_scalar(result[:], sums, bq_cols[:, u : u + 1], None, ALU.add)
+            queue.dma_start(out[P * u : P * (u + 1), half * HALF : (half + 1) * HALF], result[:])
 
-        load_w1(0, 0)
-        gather_words(0)
-        load_w1(0, 1)
-        reorder_scales(w3_planes[:].bitcast(I32), scale_rows[1][:])
-        move_rows(w3_planes[:].bitcast(I32))
-        load_w3(0)
-        gather_words(1)
-        load_w1(1, 0)
-        b3_cols = placed([P, 2, 16], F32, "b3_cols", AT_B3)
-        b3_runs = b3.rearrange("(g q s) -> q g s", g=2, s=16)
-        for e in range(4):
-            nc.sync.dma_start(b3_cols[e:P:4, :, 0:13], b3_runs[:, :, e : e + 13])
-        reorder_w2(1)
-        load_w3(1)
-        product_b(0)
-        product_b(1)
+        for a in range(2):
+            for t in range(2):
+                first_stage_pass("b", 0, t, a, "" if a else "AB"[t])
+        for t in range(2):
+            empty_b(0, t)
+        for t in range(2, 4):
+            first_stage_pass("b", 0, t, 0, "ABCD"[t])
+            first_stage_pass("b", 0, t, 1)
+            empty_b(0, t)
+        for t in range(4):
+            product("b", 1, t, "EFGH"[t])
+        empty_b(1, 0)
         for tp in range(2):
-            round_w1(0, 0, tp)
-        load_w1(1, 1)
+            round_w1(0, 0, tp, on_vector)
         for tp in range(2):
             quantize_w1(0, 0, tp)
-        for tp in range(2):
-            round_w1(0, 1, tp)
-        load_w4(0)
+        round_w1(0, 1, 0, on_vector)
+        round_w1(0, 1, 1, on_scalar)
         for tp in range(2):
             quantize_w1(0, 1, tp)
-        load_w4(1)
-        reorder_w3(0)
-        bq_cols = placed([P, 4], F32, "bq_cols", AT_BQ)
-        with nc.allow_non_contiguous_dma(reason="one bias value a partition and output tile"):
-            nc.sync.dma_start(bq_cols[:], bq.rearrange("(u p) -> p u", p=P))
-
-        ab[0] = placed([P, 4, S], F32, "ab0", AT_AB0)
+        reorder_w3(0, on_scalar)
+        reorder_w3(1, on_scalar)
+        empty_b(1, 1)
         for t in range(4):
-            multiply(0, t, product_a(0, t))
+            product("a", 0, t, "ABCD"[t])
+            multiply(0, t)
+        for t in range(4):
+            product("c", 0, t, "ABCD"[t])
+            empty_c(0, t)
+        empty_b(1, 2)
         for tp in range(2):
-            round_w1(1, 0, tp)
-        product_c(0)
-        reorder_w3(1)
+            round_w1(1, 0, tp, on_vector)
         for tp in range(2):
             quantize_w1(1, 0, tp)
         for tp in range(2):
-            round_w1(1, 1, tp)
-        product_c(1)
-        for tp in range(2):
-            quantize_w1(1, 1, tp)
-        for half in range(2):
-            make_h(0, half)
+            round_w1(1, 1, tp, on_scalar)
+        empty_b(1, 3)
+        for t in range(4):
+            product("c", 1, t, "EABC"[t])
+            empty_c(1, t)
+        make_h(0, 0)
+        quantize_w1(1, 1, 0)
+        make_h(0, 1)
+        quantize_w1(1, 1, 1)
         quantize_h(0, 0)
-
-        for nh in range(2):
-            round_w4(0, nh, placed([P, 1024], BF16, "w4_rounded0%d" % nh, AT_W4_ROUNDED[0] + 2 * KB * nh)[:])
-        w4_group1 = placed([P, 2, 1024], BF16, "w4_rounded1", AT_W4_ROUNDED[1])
-        for nh in range(2):
-            round_w4(1, nh, w4_group1[:, nh, :])
-
-        ab[1] = kept([P, 4, S], F32, "ab1")
-        for t in range(3):
-            multiply(1, t, product_a(1, t))
-        last_bank = product_a(1, 3)
-        quantize_h(0, 1)
+        for g in range(2):
+            for nh in range(2):
+                round_w4(g, nh, on_scalar)
+        for t in range(4):
+            product("a", 1, t, "DFGH"[t])
+            multiply(1, t)
+            if t == 1:
+                quantize_h(0, 1)
+        make_h(1, 0)
         quantize_w4(0, 0)
-        multiply(1, 3, last_bank)
+        for half in range(2):
+            for u in range(2):
+                out_pass(0, half, u, "EABC"[2 * half + u])
+        quantize_h(1, 0)
         quantize_w4(0, 1)
         for half in range(2):
-            for u in range(4):
-                out_pass(0, half, u)
-        make_h(1, 0)
-        quantize_w4(1, 0)
-        quantize_h(1, 0)
-        quantize_w4(1, 1)
+            for u in range(2, 4):
+                out_pass(0, half, u, "DFGH"[2 * half + u - 2])
         make_h(1, 1)
+        quantize_w4(1, 0)
+        for u in range(2):
+            out_pass(1, 0, u)
+            finish(0, u, True)
         quantize_h(1, 1)
-        for half in range(2):
-            finish_half(half)
+        for u in range(2):
+            out_pass(1, 1, u)
+            finish(1, u, True)
+        quantize_w4(1, 1)
+        for u in range(2, 4):
+            for half in range(2):
+                out_pass(1, half, u)
+                finish(half, u, (half, u) == (1, 3))

@@ -23,27 +23,34 @@ CHUNK = 2048
 
 AT = {
     "table0": 0,
-    "table1": 8 * KB,
+    "w1_last": 0,
+    "c1": 0,
     "zeros": 8 * KB - 64,
-    "w3_raw": 16 * KB,
-    "gathered_scales": 24 * KB - S,
-    "staging": 24 * KB,
-    "b11": 16 * KB,
-    "w4_rounded11": 16 * KB,
-    "w3_cols0": 94 * KB,
-    "b12": 94 * KB,
-    "b03": 90 * KB,
-    "w1_rounded100": 89 * KB,
-    "w1_rounded101": 91 * KB,
-    "h00": 89 * KB,
-    "w4_rounded01": 89 * KB,
-    "w1_rounded111": 80 * KB,
-    "c1": 73 * KB,
-    "w4_rounded00": 81 * KB,
-    "w1_rounded110": 84 * KB,
-    "b13": 83 * KB,
-    "h01": 85 * KB,
-    "w4_rounded10": 85 * KB,
+    "table1": 8 * KB,
+    "w4_staging": 8 * KB,
+    "w3_raw": 25 * KB,
+    "gathered_scales": 33 * KB - S,
+    "staging": 33 * KB,
+    "w1_rounded011": 61 * KB,
+    "b10": 60 * KB,
+    "b11": 62 * KB,
+    "w4_rounded11": 60 * KB,
+    "w3_cols0": 64 * KB,
+    "w3_cols1": 64 * KB,
+    "b03": 69 * KB,
+    "w1_rounded100": 68 * KB,
+    "w1_rounded101": 70 * KB,
+    "h00": 68 * KB,
+    "w1_rounded111": 73 * KB,
+    "w4_rounded00": 72 * KB,
+    "w4_rounded01": 74 * KB,
+    "w1_rounded110": 77 * KB,
+    "b12": 76 * KB,
+    "b13": 78 * KB,
+    "h01": 80 * KB,
+    "w4_rounded10": 80 * KB,
+    "h10": 72 * KB,
+    "h11": 74 * KB,
 }
 
 
@@ -73,7 +80,7 @@ def tile_list_subsumption_box_features_kernel(
         offsets = keep.tile([P, S // 16], U16, name="offsets")
         w2_raw = new([P, 2, 512], I32, "w2_raw")
         scale_window = [new([P, T], U8, "scale_window0"), new([P, T], U8, "scale_window1")]
-        scale_rows = new([P, 1024], I32, "scale_rows")
+        scale_rows = new([P, 512], I32, "scale_rows")
         table, w2_cols, w3_raw, w3_cols, v_words = {}, {}, {}, {}, {}
 
         def load_table(a):
@@ -112,25 +119,26 @@ def tile_list_subsumption_box_features_kernel(
         nc.sync.dma_start(scale_window[1][:].bitcast(I32)[0:P:8, :], tab_scales[1].bitcast(I32))
         nc.vector.memset(zeros[:], 0)
         nc.vector.tensor_copy(
-            scale_rows[:].rearrange("p (n w) -> p n w", w=32), zeros[:].unsqueeze(1).to_broadcast([P, 32, 32]))
-        for x, src in enumerate((w2_scales, w3_scales)):
+            scale_rows[:].rearrange("p (n w) -> p n w", w=32), zeros[:].unsqueeze(1).to_broadcast([P, 16, 32]))
+        for first, src in ((0, w2_scales), (4, w3_scales)):
             nc.sync.dma_start(
-                scale_rows[0:P:8, 512 * x : 512 * (x + 1)].rearrange("m (a n) -> m a n", a=2),
-                src.bitcast(I32).rearrange("a m n -> m a n"))
+                scale_rows[first:P:8, :].rearrange("m (a n) -> m a n", a=2), src.bitcast(I32).rearrange("a m n -> m a n"))
         load_table(0)
         load_table(1)
 
-        planes = new([P, 2 * S + 4 * H], U8, "planes")
+        planes = new([P, 2 * S + 2 * H], U8, "planes")
+        planes_i32 = planes[:].bitcast(I32)
         reorder_w2(0, on_scalar)
         nc.scalar.copy(
-            planes[:].bitcast(U32)[:, 256:1280].rearrange("p (x t qh ql) -> p x qh t ql", x=8, t=4, ql=4),
-            scale_rows[:].bitcast(U32).rearrange("p (x qh ql t) -> p x qh t ql", x=8, t=4, ql=4),
+            planes[:].bitcast(U32)[:, 256:768].rearrange("p (x t qh ql) -> p x qh t ql", x=4, t=4, ql=4),
+            scale_rows[:].bitcast(U32).rearrange("p (x qh ql t) -> p x qh t ql", x=4, t=4, ql=4),
         )
         reorder_w2(1, on_scalar)
+        for i in range(1, 4):
+            nc.sync.dma_start(planes_i32[4 + i : P : 32, 256:768], planes_i32[4 + 8 * i : P : 32, 256:768])
         gathered_scales = new([P, 2 * S], U8, "gathered_scales")
         for a in range(2):
             nc.vector.tensor_copy(gathered_scales[:, a * S : (a + 1) * S], scale_window[a][:].indirect(offsets[:]))
-        planes_i32 = planes[:].bitcast(I32)
         nc.vector.tensor_copy(planes_i32[:, 0:256], gathered_scales[:].bitcast(I32))
         for i in range(1, 4):
             nc.sync.dma_start(planes_i32[i:P:32, :], planes_i32[8 * i : P : 32, :])
@@ -140,15 +148,17 @@ def tile_list_subsumption_box_features_kernel(
         def v_operand(a):
             return dict(rhs=v_words[a][:].bitcast(FP8X4), rhs_scale=planes[:, a * S : (a + 1) * S])
 
-        staging = new([P, 6 * CHUNK + 64], F32, "staging")
+        staging = new([P, 3 * CHUNK + 32], F32, "staging")
+        w1_last = new([P, CHUNK], F32, "w1_last")
+        w4_staging = new([P, 2 * CHUNK + 8], F32, "w4_staging")
 
-        def staged(slot):
-            return staging[:, slot * CHUNK : (slot + 1) * CHUNK].rearrange("p (i c) -> p i c", i=4)
+        def chunk_of(tile, slot):
+            return tile[:, slot * CHUNK : (slot + 1) * CHUNK].rearrange("p (i c) -> p i c", i=4)
 
-        w1_raw = {(g, a): staged(2 * g + a) for g in range(2) for a in range(2)}
-        w4_raw = {g: staged(4 + g) for g in range(2)}
-        b3_cols = staging[:, 6 * CHUNK : 6 * CHUNK + 32].rearrange("p (g s) -> p g s", g=2)
-        bq_cols = staging[:, 6 * CHUNK + 32 : 6 * CHUNK + 36]
+        w1_raw = {(0, 0): chunk_of(staging, 0), (0, 1): chunk_of(staging, 1), (1, 0): chunk_of(staging, 2), (1, 1): chunk_of(w1_last, 0)}
+        w4_raw = {g: chunk_of(w4_staging, g) for g in range(2)}
+        b3_cols = staging[:, 3 * CHUNK : 3 * CHUNK + 32].rearrange("p (g s) -> p g s", g=2)
+        bq_cols = w4_staging[:, 2 * CHUNK : 2 * CHUNK + 4]
 
         def load_w1(g, a):
             chunk = w1[512 * a : 512 * (a + 1), 512 * g : 512 * (g + 1)]
@@ -172,9 +182,9 @@ def tile_list_subsumption_box_features_kernel(
         load_w1(0, 0)
         load_w1(0, 1)
         load_w3(0)
-        load_w3(1)
         load_b3()
         load_w1(1, 0)
+        load_w3(1)
         load_w1(1, 1)
         load_w4(0)
         load_w4(1)
@@ -195,8 +205,8 @@ def tile_list_subsumption_box_features_kernel(
                 c0 = 2 * S + H * a + 512 * g + P * t
                 lhsT, lhsT_scale = w2_cols[g][:, a, 64 * t : 64 * (t + 1)].bitcast(U8).bitcast(FP4X4), planes[:, c0 : c0 + P]
             else:
-                c0 = 2 * S + 2 * H + H * a + 512 * g + P * t
-                lhsT, lhsT_scale = w3_cols[g][:, a, cols].bitcast(FP8X4), planes[:, c0 : c0 + P]
+                c0 = 2 * S + H * a + 512 * g + P * t
+                lhsT, lhsT_scale = w3_cols[g][:, a, cols].bitcast(FP8X4), planes[4:P, c0 : c0 + P]
             nc.tensor.matmul_mx(
                 banks[x, g, t][:], lhsT=lhsT, lhsT_scale=lhsT_scale, start=bool(letter), stop=not letter, **v_operand(a))
 
@@ -252,6 +262,12 @@ def tile_list_subsumption_box_features_kernel(
             engine(rounded[:].rearrange("p (c n t) -> p c t n", n=2, t=4), src)
             w4_rounded[g, nh] = rounded
 
+        def round_w4_on_gpsimd(g, nh):
+            rounded = new([P, 1024], BF16, "w4_rounded%d%d" % (g, nh))
+            src = w4_raw[g][:, :, 256 * nh : 256 * (nh + 1)].rearrange("p t n -> p n t")
+            nc.gpsimd.tensor_scalar(rounded[:].rearrange("p (n t) -> p n t", t=4), src, 1.0, 0.0, ALU.mult, ALU.add)
+            w4_rounded[g, nh] = rounded
+
         def quantize_w4(g, nh):
             w4_mx[g, nh] = quantize("w4_mx%d%d" % (g, nh), w4_rounded[g, nh][:])
 
@@ -282,9 +298,8 @@ def tile_list_subsumption_box_features_kernel(
             first_stage_pass("b", 0, t, 0, "ABCD"[t])
             first_stage_pass("b", 0, t, 1)
             empty_b(0, t)
-        for t in range(4):
-            product("b", 1, t, "EFGH"[t])
-        empty_b(1, 0)
+        for t in range(2):
+            product("b", 1, t, "EF"[t])
         for tp in range(2):
             round_w1(0, 0, tp, on_vector)
         for tp in range(2):
@@ -294,59 +309,58 @@ def tile_list_subsumption_box_features_kernel(
         for tp in range(2):
             quantize_w1(0, 1, tp)
         reorder_w3(0, on_scalar)
-        reorder_w3(1, on_scalar)
-        empty_b(1, 1)
+        for t in range(2):
+            empty_b(1, t)
         for t in range(4):
             product("a", 0, t, "ABCD"[t])
             multiply(0, t)
         for t in range(4):
             product("c", 0, t, "ABCD"[t])
             empty_c(0, t)
-        empty_b(1, 2)
+        for t in range(2, 4):
+            product("b", 1, t, "..AB"[t])
+        reorder_w3(1, on_scalar)
         for tp in range(2):
             round_w1(1, 0, tp, on_vector)
         for tp in range(2):
             quantize_w1(1, 0, tp)
         for tp in range(2):
             round_w1(1, 1, tp, on_scalar)
-        empty_b(1, 3)
+        for t in range(2, 4):
+            empty_b(1, t)
         for t in range(4):
-            product("c", 1, t, "EABC"[t])
+            product("c", 1, t, "CDGH"[t])
             empty_c(1, t)
-        make_h(0, 0)
+        for half in range(2):
+            make_h(0, half)
         quantize_w1(1, 1, 0)
-        make_h(0, 1)
+        for half in range(2):
+            quantize_h(0, half)
         quantize_w1(1, 1, 1)
-        quantize_h(0, 0)
-        for g in range(2):
-            for nh in range(2):
-                round_w4(g, nh, on_scalar)
         for t in range(4):
-            product("a", 1, t, "DFGH"[t])
+            product("a", 1, t, "EFAB"[t])
             multiply(1, t)
-            if t == 1:
-                quantize_h(0, 1)
+        for nh in range(2):
+            round_w4_on_gpsimd(0, nh)
+        for nh in range(2):
+            round_w4(1, nh, on_scalar)
+        for nh in range(2):
+            quantize_w4(0, nh)
+            for half in range(2):
+                for u in range(2 * nh, 2 * nh + 2):
+                    out_pass(0, half, u, ("EFAB", "CDGH")[nh][2 * half + u % 2])
         make_h(1, 0)
-        quantize_w4(0, 0)
-        for half in range(2):
-            for u in range(2):
-                out_pass(0, half, u, "EABC"[2 * half + u])
-        quantize_h(1, 0)
-        quantize_w4(0, 1)
-        for half in range(2):
-            for u in range(2, 4):
-                out_pass(0, half, u, "DFGH"[2 * half + u - 2])
-        make_h(1, 1)
         quantize_w4(1, 0)
+        quantize_h(1, 0)
         for u in range(2):
             out_pass(1, 0, u)
             finish(0, u, True)
-        quantize_h(1, 1)
-        for u in range(2):
-            out_pass(1, 1, u)
-            finish(1, u, True)
+        make_h(1, 1)
         quantize_w4(1, 1)
         for u in range(2, 4):
-            for half in range(2):
-                out_pass(1, half, u)
-                finish(half, u, (half, u) == (1, 3))
+            out_pass(1, 0, u)
+            finish(0, u, True)
+        quantize_h(1, 1)
+        for u in range(4):
+            out_pass(1, 1, u)
+            finish(1, u, u % 2 == 1)

@@ -24,33 +24,43 @@ CHUNK = 2048
 AT = {
     "table0": 0,
     "w1_last": 0,
-    "c1": 0,
     "zeros": 8 * KB - 64,
     "table1": 8 * KB,
-    "w4_staging": 8 * KB,
-    "w3_raw": 25 * KB,
+    "w3_raw1": 8 * KB,
+    "w4_staging": 12 * KB,
+    "w3_raw0": 29 * KB,
+    "w1_rounded010": 93 * KB,
+    "b10": 92 * KB,
+    "b11": 94 * KB,
     "gathered_scales": 33 * KB - S,
     "staging": 33 * KB,
-    "w1_rounded011": 61 * KB,
-    "b10": 60 * KB,
-    "b11": 62 * KB,
-    "w4_rounded11": 60 * KB,
-    "w3_cols0": 64 * KB,
-    "w3_cols1": 64 * KB,
-    "b03": 69 * KB,
-    "w1_rounded100": 68 * KB,
-    "w1_rounded101": 70 * KB,
-    "h00": 68 * KB,
-    "w1_rounded111": 73 * KB,
-    "w4_rounded00": 72 * KB,
-    "w4_rounded01": 74 * KB,
-    "w1_rounded110": 77 * KB,
-    "b12": 76 * KB,
-    "b13": 78 * KB,
-    "h01": 80 * KB,
-    "w4_rounded10": 80 * KB,
-    "h10": 72 * KB,
-    "h11": 74 * KB,
+    "w4_rounded01": 8 * KB,
+    "ab1": 98 * KB,
+    "w1_rounded11": 105 * KB,
+    "h00": 106 * KB,
+    "h01": 108 * KB,
+    "w3_cols1": 0,
+    "h_rows01": 114 * KB,
+    "c10": 114 * KB,
+    "c11": 118 * KB,
+    "w4_mx01": 114 * KB,
+    "w4_mx00": 29 * KB,
+    "h_rows00": 82 * KB,
+    "w4_rounded00": 82 * KB,
+    "w1_rounded011": 87 * KB,
+    "w3_cols0": 88 * KB,
+    "b12": 86 * KB,
+    "h_mx00": 86 * KB,
+    "h_mx01": 87 * KB,
+    "w4_rounded10": 0,
+    "w4_rounded11": 2 * KB,
+    "ab0": 60 * KB,
+    "w1_mx110": 60 * KB,
+    "w1_mx101": 61 * KB,
+    "w1_mx111": 62 * KB,
+    "b03": 96 * KB,
+    "w1_mx100": 96 * KB,
+    "b13": 29 * KB,
 }
 
 
@@ -95,7 +105,7 @@ def tile_list_subsumption_box_features_kernel(
             )
 
         def load_w3(g):
-            w3_raw[g] = w3_both[:, 1024 * g : 1024 * (g + 1)].rearrange("p (a n) -> p a n", a=2)
+            w3_raw[g] = new([P, 2, 512], I32, "w3_raw%d" % g)[:]
             words = w3_words.rearrange("a p n i -> a p (n i)").bitcast(I32)
             nc.sync.dma_start(w3_raw[g], words[:, :, 512 * g : 512 * (g + 1)].rearrange("a p n -> p a n"))
 
@@ -178,20 +188,19 @@ def tile_list_subsumption_box_features_kernel(
             with nc.allow_non_contiguous_dma(reason="one bias value a partition and output tile"):
                 nc.sync.dma_start(bq_cols, bq.rearrange("(u p) -> p u", p=P))
 
-        w3_both = new([P, 2048], I32, "w3_raw")
         load_w1(0, 0)
         load_w1(0, 1)
         load_w3(0)
         load_b3()
         load_w1(1, 0)
-        load_w3(1)
         load_w1(1, 1)
+        load_w3(1)
         load_w4(0)
         load_w4(1)
         load_bq()
 
         banks, b_sb, w1_rounded, w1_mx = {}, {}, {}, {}
-        c_sb = [new([P, 4, S], F32, "c0"), new([P, 4, S], F32, "c1")]
+        c_sb = {}
         ab = [new([P, 4, S], F32, "ab0"), new([P, 4, S], F32, "ab1")]
 
         def first_stage_pass(x, g, t, a, letter=None):
@@ -230,19 +239,25 @@ def tile_list_subsumption_box_features_kernel(
             nc.vector.quantize_mx(codes[:].bitcast(FP8X4), scales[:], rounded)
             return codes, scales
 
+        last_rounded = new([P, 2048], BF16, "w1_rounded11")
+
+        def rounded_half(g, a, tp):
+            if (g, a) == (1, 1):
+                return last_rounded[:, 1024 * tp : 1024 * (tp + 1)]
+            return new([P, 1024], BF16, "w1_rounded%d%d%d" % (g, a, tp))[:]
+
         def round_w1(g, a, tp, engine):
-            rounded = new([P, 1024], BF16, "w1_rounded%d%d%d" % (g, a, tp))
+            rounded = rounded_half(g, a, tp)
             src = w1_raw[g, a].rearrange("p i (q t e) -> p t q i e", t=4, e=4)[:, 2 * tp : 2 * tp + 2]
-            dst = rounded[:].rearrange("p (t q e i) -> p t q i e", t=2, e=4, i=4)
+            dst = rounded.rearrange("p (t q e i) -> p t q i e", t=2, e=4, i=4)
             engine(dst, src)
             w1_rounded[g, a, tp] = rounded
 
         def quantize_w1(g, a, tp):
-            w1_mx[g, a, tp] = quantize("w1_mx%d%d%d" % (g, a, tp), w1_rounded[g, a, tp][:])
+            w1_mx[g, a, tp] = quantize("w1_mx%d%d%d" % (g, a, tp), w1_rounded[g, a, tp])
 
         h, w4_rounded, w4_mx, out_banks = {}, {}, {}, {}
-        h_codes = [new([P, S], U32, "h_codes0"), new([P, S], U32, "h_codes1")]
-        h_scales = [new([P, S], U8, "h_scales0"), new([P, S], U8, "h_scales1")]
+        h_mx = {}
 
         def make_h(g, half):
             js = slice(half * HALF, (half + 1) * HALF)
@@ -250,11 +265,10 @@ def tile_list_subsumption_box_features_kernel(
             nc.vector.tensor_tensor(
                 h[g, half][:].rearrange("p (c j t) -> p c t j", j=2, t=4),
                 ab[g][:, :, js].rearrange("p t (c j) -> p c t j", j=2),
-                c_sb[g][:, :, js].rearrange("p t (c j) -> p c t j", j=2), ALU.max)
+                c_sb[g, half][:].rearrange("p t (c j) -> p c t j", j=2), ALU.max)
 
         def quantize_h(g, half):
-            js = slice(half * HALF, (half + 1) * HALF)
-            nc.vector.quantize_mx(h_codes[g][:, js].bitcast(FP8X4), h_scales[g][:, js], h[g, half][:])
+            h_mx[g, half] = quantize("h_mx%d%d" % (g, half), h[g, half][:])
 
         def round_w4(g, nh, engine):
             rounded = new([P, 1024], BF16, "w4_rounded%d%d" % (g, nh))
@@ -262,11 +276,60 @@ def tile_list_subsumption_box_features_kernel(
             engine(rounded[:].rearrange("p (c n t) -> p c t n", n=2, t=4), src)
             w4_rounded[g, nh] = rounded
 
+        def interleave_on_gpsimd(dst, src):
+            nc.gpsimd.tensor_scalar(
+                dst.rearrange("p (n t) -> p n t", t=4), src.rearrange("p t n -> p n t"), 1.0, 0.0, ALU.mult, ALU.add)
+
         def round_w4_on_gpsimd(g, nh):
-            rounded = new([P, 1024], BF16, "w4_rounded%d%d" % (g, nh))
-            src = w4_raw[g][:, :, 256 * nh : 256 * (nh + 1)].rearrange("p t n -> p n t")
-            nc.gpsimd.tensor_scalar(rounded[:].rearrange("p (n t) -> p n t", t=4), src, 1.0, 0.0, ALU.mult, ALU.add)
-            w4_rounded[g, nh] = rounded
+            w4_rounded[g, nh] = new([P, 1024], BF16, "w4_rounded%d%d" % (g, nh))
+            interleave_on_gpsimd(w4_rounded[g, nh][:], w4_raw[g][:, :, 256 * nh : 256 * (nh + 1)])
+
+        h_rows, c_halves = {}, {}
+
+        def product_c_half(g, half, letters):
+            js = slice(half * HALF, (half + 1) * HALF)
+            for t in range(4):
+                if t % 2 == 0:
+                    pair = bank(letters[t // 2])
+                c_halves[g, half, t] = pair[:, HALF * (t % 2) : HALF * (t % 2 + 1)]
+                for a in range(2):
+                    c0 = 2 * S + H * a + 512 * g + P * t
+                    nc.tensor.matmul_mx(
+                        c_halves[g, half, t], lhsT=w3_cols[g][:, a, P * t : P * (t + 1)].bitcast(FP8X4),
+                        lhsT_scale=planes[4:P, c0 : c0 + P], rhs=v_words[a][:, js].bitcast(FP8X4),
+                        rhs_scale=planes[:, a * S + half * HALF : a * S + (half + 1) * HALF], start=(a == 0), stop=(a == 1))
+
+        def make_h_rows(g, half):
+            js = slice(half * HALF, (half + 1) * HALF)
+            h_rows[g, half] = new([P, 4, HALF], BF16, "h_rows%d%d" % (g, half))
+            for t in range(4):
+                nc.vector.scalar_tensor_tensor(
+                    h_rows[g, half][:, t, :], c_halves[g, half, t], b3_cols[:, g, 4 * t : 4 * t + 1],
+                    ab[g][:, t, js], ALU.add, ALU.max)
+
+        def empty_c_half(g, half):
+            c_sb[g, half] = new([P, 4, HALF], F32, "c%d%d" % (g, half))
+            for t in range(4):
+                nc.scalar.activation(
+                    c_sb[g, half][:, t, :], c_halves[g, half, t], ACT.Identity, bias=b3_cols[:, g, 4 * t : 4 * t + 1])
+
+        def round_w1_on_gpsimd(g, a, tp):
+            rounded = rounded_half(g, a, tp)
+            src = w1_raw[g, a].rearrange("p i (q t e) -> p t q e i", t=4, e=4)
+            for t in range(2):
+                nc.gpsimd.tensor_scalar(
+                    rounded[:, 512 * t : 512 * (t + 1)].rearrange("p (q e i) -> p q e i", e=4, i=4), src[:, 2 * tp + t],
+                    1.0, 0.0, ALU.mult, ALU.add)
+            w1_rounded[g, a, tp] = rounded
+
+        def interleave_h(g, half, on_gpsimd=True):
+            h[g, half] = new([P, 4 * HALF], BF16, "h%d%d" % (g, half))
+            if on_gpsimd:
+                interleave_on_gpsimd(h[g, half][:], h_rows[g, half][:])
+            else:
+                nc.scalar.copy(
+                    h[g, half][:].rearrange("p (c j t) -> p c t j", j=4, t=4),
+                    h_rows[g, half][:].rearrange("p t (c j) -> p c t j", j=4))
 
         def quantize_w4(g, nh):
             w4_mx[g, nh] = quantize("w4_mx%d%d" % (g, nh), w4_rounded[g, nh][:])
@@ -274,11 +337,11 @@ def tile_list_subsumption_box_features_kernel(
         def out_pass(g, half, u, letter=None):
             if letter:
                 out_banks[half, u] = bank(letter)
-            cols, js = slice(P * (u % 2), P * (u % 2 + 1)), slice(half * HALF, (half + 1) * HALF)
+            cols = slice(P * (u % 2), P * (u % 2 + 1))
             codes, scales = w4_mx[g, u // 2]
             nc.tensor.matmul_mx(
                 out_banks[half, u][:, 0:HALF], lhsT=codes[:, cols].bitcast(FP8X4), lhsT_scale=scales[:, cols],
-                rhs=h_codes[g][:, js].bitcast(FP8X4), rhs_scale=h_scales[g][:, js], start=bool(letter), stop=not letter)
+                rhs=h_mx[g, half][0][:].bitcast(FP8X4), rhs_scale=h_mx[g, half][1][:], start=bool(letter), stop=not letter)
 
         def finish(half, u, on_scalar_engine, queue=nc.sync):
             result = new([P, HALF], F32, "result%d%d" % (half, u))
@@ -298,8 +361,8 @@ def tile_list_subsumption_box_features_kernel(
             first_stage_pass("b", 0, t, 0, "ABCD"[t])
             first_stage_pass("b", 0, t, 1)
             empty_b(0, t)
-        for t in range(2):
-            product("b", 1, t, "EF"[t])
+        for t in range(4):
+            product("b", 1, t, "EFGH"[t])
         for tp in range(2):
             round_w1(0, 0, tp, on_vector)
         for tp in range(2):
@@ -308,59 +371,64 @@ def tile_list_subsumption_box_features_kernel(
         round_w1(0, 1, 1, on_scalar)
         for tp in range(2):
             quantize_w1(0, 1, tp)
-        reorder_w3(0, on_scalar)
-        for t in range(2):
+        reorder_w3(0, nc.gpsimd.tensor_copy)
+        for t in range(4):
             empty_b(1, t)
         for t in range(4):
             product("a", 0, t, "ABCD"[t])
             multiply(0, t)
-        for t in range(4):
-            product("c", 0, t, "ABCD"[t])
-            empty_c(0, t)
-        for t in range(2, 4):
-            product("b", 1, t, "..AB"[t])
-        reorder_w3(1, on_scalar)
-        for tp in range(2):
-            round_w1(1, 0, tp, on_vector)
-        for tp in range(2):
-            quantize_w1(1, 0, tp)
-        for tp in range(2):
-            round_w1(1, 1, tp, on_scalar)
-        for t in range(2, 4):
-            empty_b(1, t)
-        for t in range(4):
-            product("c", 1, t, "CDGH"[t])
-            empty_c(1, t)
-        for half in range(2):
-            make_h(0, half)
+        round_w1(1, 0, 0, on_scalar)
+        round_w1_on_gpsimd(1, 0, 1)
+        product_c_half(0, 0, "AB")
+        product_c_half(0, 1, "CD")
+        make_h_rows(0, 0)
+        quantize_w1(1, 0, 0)
+        for t in range(2):
+            first_stage_pass("a", 1, t, 0, "AB"[t])
+        make_h_rows(0, 1)
+        round_w1(1, 1, 0, on_scalar)
+        round_w1_on_gpsimd(1, 1, 1)
         quantize_w1(1, 1, 0)
-        for half in range(2):
-            quantize_h(0, half)
+        quantize_w1(1, 0, 1)
         quantize_w1(1, 1, 1)
+        reorder_w3(1, on_scalar)
+        interleave_h(0, 0)
+        interleave_h(0, 1, False)
+        round_w4_on_gpsimd(0, 0)
+        round_w4(0, 1, on_scalar)
         for t in range(4):
-            product("a", 1, t, "EFAB"[t])
+            if t >= 2:
+                first_stage_pass("a", 1, t, 0, "ABCD"[t])
+            first_stage_pass("a", 1, t, 1)
             multiply(1, t)
-        for nh in range(2):
-            round_w4_on_gpsimd(0, nh)
+        for half in range(2):
+            product_c_half(1, half, ("FG", "HE")[half])
+            empty_c_half(1, half)
         for nh in range(2):
             round_w4(1, nh, on_scalar)
-        for nh in range(2):
-            quantize_w4(0, nh)
-            for half in range(2):
-                for u in range(2 * nh, 2 * nh + 2):
-                    out_pass(0, half, u, ("EFAB", "CDGH")[nh][2 * half + u % 2])
+        for half in range(2):
+            quantize_h(0, half)
+        quantize_w4(0, 0)
+        for half in range(2):
+            for u in range(2):
+                out_pass(0, half, u, "ABCD"[2 * half + u])
         make_h(1, 0)
-        quantize_w4(1, 0)
+        quantize_w4(0, 1)
+        for half in range(2):
+            for u in range(2, 4):
+                out_pass(0, half, u, "FGHE"[2 * half + u % 2])
         quantize_h(1, 0)
+        make_h(1, 1)
+        quantize_w4(1, 0)
         for u in range(2):
             out_pass(1, 0, u)
             finish(0, u, True)
-        make_h(1, 1)
+        quantize_h(1, 1)
+        for u in range(2):
+            out_pass(1, 1, u)
+            finish(1, u, True)
         quantize_w4(1, 1)
         for u in range(2, 4):
-            out_pass(1, 0, u)
-            finish(0, u, True)
-        quantize_h(1, 1)
-        for u in range(4):
-            out_pass(1, 1, u)
-            finish(1, u, u % 2 == 1)
+            for half in range(2):
+                out_pass(1, half, u)
+                finish(half, u, (half, u) == (0, 3))

@@ -22,45 +22,44 @@ KB = 1024
 CHUNK = 2048
 
 AT = {
-    "table0": 0,
-    "w1_last": 0,
-    "zeros": 8 * KB - 64,
-    "table1": 8 * KB,
-    "w3_raw1": 8 * KB,
-    "w4_staging": 12 * KB,
-    "w3_raw0": 29 * KB,
-    "w1_rounded010": 93 * KB,
-    "b10": 92 * KB,
-    "b11": 94 * KB,
-    "gathered_scales": 33 * KB - S,
-    "staging": 33 * KB,
-    "w4_rounded01": 8 * KB,
-    "ab1": 98 * KB,
-    "w1_rounded11": 105 * KB,
-    "h00": 106 * KB,
-    "h01": 108 * KB,
-    "w3_cols1": 0,
-    "h_rows01": 114 * KB,
-    "c10": 114 * KB,
-    "c11": 118 * KB,
-    "w4_mx01": 114 * KB,
-    "w4_mx00": 29 * KB,
-    "h_rows00": 82 * KB,
-    "w4_rounded00": 82 * KB,
-    "w1_rounded011": 87 * KB,
-    "w3_cols0": 88 * KB,
-    "b12": 86 * KB,
-    "h_mx00": 86 * KB,
-    "h_mx01": 87 * KB,
-    "w4_rounded10": 0,
-    "w4_rounded11": 2 * KB,
+    "table0": 4 * KB,
+    "w1_last0": 1 * KB,
+    "w1_last1": 5 * KB,
+    "w3_cols1": 5 * KB,
+    "w4_rounded10": 5 * KB,
+    "w4_rounded11": 7 * KB,
+    "w3_raw1": 9 * KB,
+    "h_rows": 114 * KB,
+    "w4_rounded01": 114 * KB,
+    "h10": 114 * KB,
+    "zeros": 12 * KB - 64,
+    "table1": 12 * KB,
+    "w4_first": 13 * KB,
+    "c10": 13 * KB,
+    "w1_rounded000": 21 * KB,
+    "w4_last": 21 * KB,
+    "w3_raw0": 30 * KB,
+    "b13": 30 * KB,
+    "w4_mx00": 30 * KB,
+    "gathered_scales": 34 * KB - S,
+    "staging": 34 * KB,
     "ab0": 60 * KB,
     "w1_mx110": 60 * KB,
     "w1_mx101": 61 * KB,
     "w1_mx111": 62 * KB,
     "b03": 96 * KB,
     "w1_mx100": 96 * KB,
-    "b13": 29 * KB,
+    "b12": 86 * KB,
+    "h_mx0": 86 * KB,
+    "w1_rounded011": 87 * KB,
+    "w3_cols0": 88 * KB,
+    "b10": 92 * KB,
+    "w1_rounded010": 93 * KB,
+    "b11": 94 * KB,
+    "ab1": 98 * KB,
+    "w1_rounded11": 105 * KB,
+    "w4_rounded00": 106 * KB,
+    "h0": 108 * KB,
 }
 
 
@@ -81,47 +80,16 @@ def tile_list_subsumption_box_features_kernel(
         def bank(letter):
             return psum.tile([P, S], F32, name="bank" + letter, tag="bank" + letter)
 
-        def clock(name, src):
-            tick = new([P, 1], src.dtype, name)
-            nc.gpsimd.tensor_copy(tick[:], src)
-
-        on_vector, on_scalar = nc.vector.tensor_copy, nc.scalar.copy
+        def gpsimd_round(dst, src):
+            nc.gpsimd.tensor_scalar(dst, src, 1.0, 0.0, ALU.mult, ALU.add)
 
         offsets = keep.tile([P, S // 16], U16, name="offsets")
+        nc.sync.dma_start(offsets[:], offs)
         w2_raw = new([P, 2, 512], I32, "w2_raw")
+        nc.sync.dma_start(w2_raw[:], w2_words.bitcast(I32).rearrange("a p n -> p a n"))
+
         scale_window = [new([P, T], U8, "scale_window0"), new([P, T], U8, "scale_window1")]
         scale_rows = new([P, 512], I32, "scale_rows")
-        table, w2_cols, w3_raw, w3_cols, v_words = {}, {}, {}, {}, {}
-
-        def load_table(a):
-            table[a] = new([P, T], I32, "table%d" % a)
-            nc.sync.dma_start(table[a][:], tab_words[a].rearrange("p t i -> p (t i)").bitcast(I32))
-
-        def reorder_w2(g, engine):
-            w2_cols[g] = new([P, 2, 256], U32, "w2_cols%d" % g)
-            engine(
-                w2_cols[g][:].rearrange("p a (t q e) -> p a t q e", t=4, e=2),
-                w2_raw[:].bitcast(U32)[:, :, 256 * g : 256 * (g + 1)].rearrange("p a (q t e) -> p a t q e", t=4, e=2),
-            )
-
-        def load_w3(g):
-            w3_raw[g] = new([P, 2, 512], I32, "w3_raw%d" % g)[:]
-            words = w3_words.rearrange("a p n i -> a p (n i)").bitcast(I32)
-            nc.sync.dma_start(w3_raw[g], words[:, :, 512 * g : 512 * (g + 1)].rearrange("a p n -> p a n"))
-
-        def reorder_w3(g, engine):
-            w3_cols[g] = new([P, 2, 512], U32, "w3_cols%d" % g)
-            engine(
-                w3_cols[g][:].rearrange("p a (t q e) -> p a t q e", t=4, e=4),
-                w3_raw[g].bitcast(U32).rearrange("p a (q t e) -> p a t q e", t=4, e=4),
-            )
-
-        def gather_words(a):
-            v_words[a] = new([P, S], U32, "v_words%d" % a)
-            nc.vector.tensor_copy(v_words[a][:], table[a][:].bitcast(U32).indirect(offsets[:]))
-
-        nc.sync.dma_start(offsets[:], offs)
-        nc.sync.dma_start(w2_raw[:], w2_words.bitcast(I32).rearrange("a p n -> p a n"))
         zeros = new([P, 32], I32, "zeros")
         nc.gpsimd.memset(scale_window[0][:].bitcast(I32), 0)
         nc.sync.dma_start(scale_window[0][:].bitcast(I32)[0:P:8, :], tab_scales[0].bitcast(I32))
@@ -133,17 +101,28 @@ def tile_list_subsumption_box_features_kernel(
         for first, src in ((0, w2_scales), (4, w3_scales)):
             nc.sync.dma_start(
                 scale_rows[first:P:8, :].rearrange("m (a n) -> m a n", a=2), src.bitcast(I32).rearrange("a m n -> m a n"))
-        load_table(0)
-        load_table(1)
+        table = []
+        for a in range(2):
+            table.append(new([P, T], I32, "table%d" % a))
+            nc.sync.dma_start(table[a][:], tab_words[a].rearrange("p t i -> p (t i)").bitcast(I32))
+
+        w2_cols, w3_raw, w3_cols, v_words = {}, {}, {}, {}
+
+        def reorder_w2(g):
+            w2_cols[g] = new([P, 2, 256], U32, "w2_cols%d" % g)
+            nc.scalar.copy(
+                w2_cols[g][:].rearrange("p a (t q e) -> p a t q e", t=4, e=2),
+                w2_raw[:].bitcast(U32)[:, :, 256 * g : 256 * (g + 1)].rearrange("p a (q t e) -> p a t q e", t=4, e=2),
+            )
 
         planes = new([P, 2 * S + 2 * H], U8, "planes")
         planes_i32 = planes[:].bitcast(I32)
-        reorder_w2(0, on_scalar)
+        reorder_w2(0)
         nc.scalar.copy(
             planes[:].bitcast(U32)[:, 256:768].rearrange("p (x t qh ql) -> p x qh t ql", x=4, t=4, ql=4),
             scale_rows[:].bitcast(U32).rearrange("p (x qh ql t) -> p x qh t ql", x=4, t=4, ql=4),
         )
-        reorder_w2(1, on_scalar)
+        reorder_w2(1)
         for i in range(1, 4):
             nc.sync.dma_start(planes_i32[4 + i : P : 32, 256:768], planes_i32[4 + 8 * i : P : 32, 256:768])
         gathered_scales = new([P, 2 * S], U8, "gathered_scales")
@@ -152,223 +131,223 @@ def tile_list_subsumption_box_features_kernel(
         nc.vector.tensor_copy(planes_i32[:, 0:256], gathered_scales[:].bitcast(I32))
         for i in range(1, 4):
             nc.sync.dma_start(planes_i32[i:P:32, :], planes_i32[8 * i : P : 32, :])
-        gather_words(0)
-        gather_words(1)
-
-        def v_operand(a):
-            return dict(rhs=v_words[a][:].bitcast(FP8X4), rhs_scale=planes[:, a * S : (a + 1) * S])
+        for a in range(2):
+            v_words[a] = new([P, S], U32, "v_words%d" % a)
+            nc.vector.tensor_copy(v_words[a][:], table[a][:].bitcast(U32).indirect(offsets[:]))
 
         staging = new([P, 3 * CHUNK + 32], F32, "staging")
-        w1_last = new([P, CHUNK], F32, "w1_last")
-        w4_staging = new([P, 2 * CHUNK + 8], F32, "w4_staging")
+        w1_last = [new([P, 4, 256], F32, "w1_last0"), new([P, 4, 256], F32, "w1_last1")]
+        w4_first = new([P, CHUNK], F32, "w4_first")
+        w4_last = new([P, CHUNK + 8], F32, "w4_last")
 
         def chunk_of(tile, slot):
             return tile[:, slot * CHUNK : (slot + 1) * CHUNK].rearrange("p (i c) -> p i c", i=4)
 
-        w1_raw = {(0, 0): chunk_of(staging, 0), (0, 1): chunk_of(staging, 1), (1, 0): chunk_of(staging, 2), (1, 1): chunk_of(w1_last, 0)}
-        w4_raw = {g: chunk_of(w4_staging, g) for g in range(2)}
+        w1_raw = {(0, 0): chunk_of(staging, 0), (0, 1): chunk_of(staging, 1), (1, 0): chunk_of(staging, 2)}
+        w4_raw = [chunk_of(w4_first, 0), chunk_of(w4_last, 0)]
         b3_cols = staging[:, 3 * CHUNK : 3 * CHUNK + 32].rearrange("p (g s) -> p g s", g=2)
-        bq_cols = w4_staging[:, 2 * CHUNK : 2 * CHUNK + 4]
+        bq_cols = w4_last[:, CHUNK : CHUNK + 4]
 
         def load_w1(g, a):
             chunk = w1[512 * a : 512 * (a + 1), 512 * g : 512 * (g + 1)]
             nc.sync.dma_start(w1_raw[g, a], chunk.rearrange("(p i) c -> p i c", i=4))
+
+        def load_w3(g):
+            w3_raw[g] = new([P, 2, 512], I32, "w3_raw%d" % g)
+            words = w3_words.rearrange("a p n i -> a p (n i)").bitcast(I32)
+            nc.sync.dma_start(w3_raw[g][:], words[:, :, 512 * g : 512 * (g + 1)].rearrange("a p n -> p a n"))
 
         def load_w4(g):
             rows = w4[512 * g : 512 * (g + 1), :].rearrange("(q t e) n -> t q e n", t=4, e=4)
             for t in range(4):
                 nc.sync.dma_start(w4_raw[g][:, t, :], rows[t])
 
-        def load_b3():
-            b3_runs = b3.rearrange("(g q s) -> q g s", g=2, s=16)
-            for e in range(4):
-                nc.sync.dma_start(b3_cols[e:P:4, :, 0:13], b3_runs[:, :, e : e + 13])
-
-        def load_bq():
-            with nc.allow_non_contiguous_dma(reason="one bias value a partition and output tile"):
-                nc.sync.dma_start(bq_cols, bq.rearrange("(u p) -> p u", p=P))
-
         load_w1(0, 0)
         load_w1(0, 1)
         load_w3(0)
-        load_b3()
+        b3_runs = b3.rearrange("(g q s) -> q g s", g=2, s=16)
+        for e in range(4):
+            nc.sync.dma_start(b3_cols[e:P:4, :, 0:13], b3_runs[:, :, e : e + 13])
         load_w1(1, 0)
-        load_w1(1, 1)
+        for qh in range(2):
+            columns = w1[512:1024, 512 + 256 * qh : 512 + 256 * (qh + 1)]
+            nc.sync.dma_start(w1_last[qh][:], columns.rearrange("(p i) c -> p i c", i=4))
         load_w3(1)
         load_w4(0)
-        load_w4(1)
-        load_bq()
 
-        banks, b_sb, w1_rounded, w1_mx = {}, {}, {}, {}
-        c_sb = {}
+        def reorder_w3(g, copy):
+            w3_cols[g] = new([P, 2, 512], U32, "w3_cols%d" % g)
+            copy(
+                w3_cols[g][:].rearrange("p a (t q e) -> p a t q e", t=4, e=4),
+                w3_raw[g][:].bitcast(U32).rearrange("p a (q t e) -> p a t q e", t=4, e=4),
+            )
+
+        sums, b_sb, c_sb, w1_rounded, w1_mx = {}, {}, {}, {}, {}
         ab = [new([P, 4, S], F32, "ab0"), new([P, 4, S], F32, "ab1")]
 
-        def first_stage_pass(x, g, t, a, letter=None):
-            if letter:
-                banks[x, g, t] = bank(letter)
-            cols = slice(P * t, P * (t + 1))
+        def stationary(x, g, t, a):
+            c0 = 2 * S + H * a + 512 * g + P * t
             if x == "a":
                 codes, scales = w1_mx[g, a, t // 2]
-                lhsT, lhsT_scale = codes[:, P * (t % 2) : P * (t % 2 + 1)].bitcast(FP8X4), scales[:, P * (t % 2) : P * (t % 2 + 1)]
-            elif x == "b":
-                c0 = 2 * S + H * a + 512 * g + P * t
-                lhsT, lhsT_scale = w2_cols[g][:, a, 64 * t : 64 * (t + 1)].bitcast(U8).bitcast(FP4X4), planes[:, c0 : c0 + P]
-            else:
-                c0 = 2 * S + H * a + 512 * g + P * t
-                lhsT, lhsT_scale = w3_cols[g][:, a, cols].bitcast(FP8X4), planes[4:P, c0 : c0 + P]
+                cols = slice(P * (t % 2), P * (t % 2 + 1))
+                return dict(lhsT=codes[:, cols].bitcast(FP8X4), lhsT_scale=scales[:, cols])
+            if x == "b":
+                words = w2_cols[g][:, a, 64 * t : 64 * (t + 1)].bitcast(U8)
+                return dict(lhsT=words.bitcast(FP4X4), lhsT_scale=planes[:, c0 : c0 + P])
+            return dict(lhsT=w3_cols[g][:, a, P * t : P * (t + 1)].bitcast(FP8X4), lhsT_scale=planes[4:P, c0 : c0 + P])
+
+        def one_pass(key, a, first, j0=0, width=S):
+            x, g, t = key[:3]
             nc.tensor.matmul_mx(
-                banks[x, g, t][:], lhsT=lhsT, lhsT_scale=lhsT_scale, start=bool(letter), stop=not letter, **v_operand(a))
+                sums[key], rhs=v_words[a][:, j0 : j0 + width].bitcast(FP8X4),
+                rhs_scale=planes[:, a * S + j0 : a * S + j0 + width], start=first, stop=not first, **stationary(x, g, t, a))
 
-        def product(x, g, t, letter):
-            first_stage_pass(x, g, t, 1, letter)
-            first_stage_pass(x, g, t, 0)
+        def open_sum(x, g, t, a, letter):
+            sums[x, g, t] = bank(letter)[:]
+            one_pass((x, g, t), a, True)
 
-        def empty_b(g, t, engine=on_scalar):
+        def close_sum(x, g, t, a):
+            one_pass((x, g, t), a, False)
+
+        def product(x, g, t, letter, first=1):
+            open_sum(x, g, t, first, letter)
+            close_sum(x, g, t, 1 - first)
+
+        def product_c1(half, letters):
+            c_sb[half] = new([P, 4, HALF], F32, "c1%d" % half)
+            for t in range(4):
+                if t % 2 == 0:
+                    pair = bank(letters[t // 2])
+                sums["c", 1, t, half] = pair[:, HALF * (t % 2) : HALF * (t % 2 + 1)]
+                for a in range(2):
+                    one_pass(("c", 1, t, half), a, a == 0, half * HALF, HALF)
+            for t in range(4):
+                nc.scalar.activation(
+                    c_sb[half][:, t, :], sums["c", 1, t, half], ACT.Identity, bias=b3_cols[:, 1, 4 * t : 4 * t + 1])
+
+        def empty_b(g, t):
             b_sb[g, t] = new([P, S], F32, "b%d%d" % (g, t))
-            engine(b_sb[g, t][:], banks["b", g, t][:])
-
-        def empty_c(g, t):
-            nc.scalar.activation(c_sb[g][:, t, :], banks["c", g, t][:], ACT.Identity, bias=b3_cols[:, g, 4 * t : 4 * t + 1])
+            nc.scalar.copy(b_sb[g, t][:], sums["b", g, t])
 
         def multiply(g, t):
-            nc.vector.tensor_tensor(ab[g][:, t, :], banks["a", g, t][:], b_sb[g, t][:], ALU.mult)
+            nc.vector.tensor_tensor(ab[g][:, t, :], sums["a", g, t], b_sb[g, t][:], ALU.mult)
 
-        def quantize(name, rounded):
-            codes = new([P, 256], U32, name)
-            scales = new([P, 256], U8, name + "_scales")
+        def quantize(name, rounded, width=256):
+            codes = new([P, width], U32, name)
+            scales = new([P, width], U8, name + "_scales")
             nc.vector.quantize_mx(codes[:].bitcast(FP8X4), scales[:], rounded)
-            return codes, scales
+            return codes[:], scales[:]
 
         last_rounded = new([P, 2048], BF16, "w1_rounded11")
 
         def rounded_half(g, a, tp):
             if (g, a) == (1, 1):
-                return last_rounded[:, 1024 * tp : 1024 * (tp + 1)]
-            return new([P, 1024], BF16, "w1_rounded%d%d%d" % (g, a, tp))[:]
+                w1_rounded[g, a, tp] = last_rounded[:, 1024 * tp : 1024 * (tp + 1)]
+            else:
+                w1_rounded[g, a, tp] = new([P, 1024], BF16, "w1_rounded%d%d%d" % (g, a, tp))[:]
+            return w1_rounded[g, a, tp]
 
-        def round_w1(g, a, tp, engine):
-            rounded = rounded_half(g, a, tp)
+        def round_w1(g, a, tp, copy):
             src = w1_raw[g, a].rearrange("p i (q t e) -> p t q i e", t=4, e=4)[:, 2 * tp : 2 * tp + 2]
-            dst = rounded.rearrange("p (t q e i) -> p t q i e", t=2, e=4, i=4)
-            engine(dst, src)
-            w1_rounded[g, a, tp] = rounded
+            copy(rounded_half(g, a, tp).rearrange("p (t q e i) -> p t q i e", t=2, e=4, i=4), src)
+
+        def round_w1_on_gpsimd(g, a, tp):
+            src = w1_raw[g, a].rearrange("p i (q t e) -> p t q e i", t=4, e=4)
+            dst = rounded_half(g, a, tp).rearrange("p (t q e i) -> p t q e i", t=2, e=4, i=4)
+            for t in range(2):
+                gpsimd_round(dst[:, t], src[:, 2 * tp + t])
 
         def quantize_w1(g, a, tp):
             w1_mx[g, a, tp] = quantize("w1_mx%d%d%d" % (g, a, tp), w1_rounded[g, a, tp])
 
-        h, w4_rounded, w4_mx, out_banks = {}, {}, {}, {}
-        h_mx = {}
+        h1, h_mx, w4_rounded, w4_mx = {}, {}, {}, {}
+        h_rows = new([P, 4, S], BF16, "h_rows")
+        h0 = new([P, 4 * S], BF16, "h0")
 
-        def make_h(g, half):
-            js = slice(half * HALF, (half + 1) * HALF)
-            h[g, half] = new([P, 4 * HALF], BF16, "h%d%d" % (g, half))
+        def make_h0_row(t):
+            nc.vector.scalar_tensor_tensor(
+                h_rows[:, t, :], sums["c", 0, t], b3_cols[:, 0, 4 * t : 4 * t + 1], ab[0][:, t, :], ALU.add, ALU.max)
+
+        def h0_half(half):
+            return h0[:, 4 * HALF * half : 4 * HALF * (half + 1)], h_rows[:, :, HALF * half : HALF * (half + 1)]
+
+        def interleave_h0_on_gpsimd(half):
+            dst, src = h0_half(half)
+            gpsimd_round(dst.rearrange("p (j t) -> p j t", t=4), src.rearrange("p t j -> p j t"))
+
+        def interleave_h0_on_scalar(half):
+            dst, src = h0_half(half)
+            nc.scalar.copy(dst.rearrange("p (c j t) -> p c t j", j=4, t=4), src.rearrange("p t (c j) -> p c t j", j=4))
+
+        def quantize_h0():
+            codes, scales = quantize("h_mx0", h0[:], S)
+            for half in range(2):
+                h_mx[0, half] = codes[:, HALF * half : HALF * (half + 1)], scales[:, HALF * half : HALF * (half + 1)]
+
+        def make_h1(half):
+            h1[half] = new([P, 4 * HALF], BF16, "h1%d" % half)
             nc.vector.tensor_tensor(
-                h[g, half][:].rearrange("p (c j t) -> p c t j", j=2, t=4),
-                ab[g][:, :, js].rearrange("p t (c j) -> p c t j", j=2),
-                c_sb[g, half][:].rearrange("p t (c j) -> p c t j", j=2), ALU.max)
+                h1[half][:].rearrange("p (c j t) -> p c t j", j=2, t=4),
+                ab[1][:, :, half * HALF : (half + 1) * HALF].rearrange("p t (c j) -> p c t j", j=2),
+                c_sb[half][:].rearrange("p t (c j) -> p c t j", j=2), ALU.max)
 
-        def quantize_h(g, half):
-            h_mx[g, half] = quantize("h_mx%d%d" % (g, half), h[g, half][:])
+        def quantize_h1(half):
+            h_mx[1, half] = quantize("h_mx1%d" % half, h1[half][:])
 
-        def round_w4(g, nh, engine):
-            rounded = new([P, 1024], BF16, "w4_rounded%d%d" % (g, nh))
-            src = w4_raw[g][:, :, 256 * nh : 256 * (nh + 1)].rearrange("p t (c n) -> p c t n", n=2)
-            engine(rounded[:].rearrange("p (c n t) -> p c t n", n=2, t=4), src)
-            w4_rounded[g, nh] = rounded
+        def w4_quarter(g, nh):
+            w4_rounded[g, nh] = new([P, 1024], BF16, "w4_rounded%d%d" % (g, nh))
+            return w4_rounded[g, nh][:], w4_raw[g][:, :, 256 * nh : 256 * (nh + 1)]
 
-        def interleave_on_gpsimd(dst, src):
-            nc.gpsimd.tensor_scalar(
-                dst.rearrange("p (n t) -> p n t", t=4), src.rearrange("p t n -> p n t"), 1.0, 0.0, ALU.mult, ALU.add)
+        def round_w4(g, nh, copy):
+            dst, src = w4_quarter(g, nh)
+            copy(dst.rearrange("p (c n t) -> p c t n", n=2, t=4), src.rearrange("p t (c n) -> p c t n", n=2))
 
         def round_w4_on_gpsimd(g, nh):
-            w4_rounded[g, nh] = new([P, 1024], BF16, "w4_rounded%d%d" % (g, nh))
-            interleave_on_gpsimd(w4_rounded[g, nh][:], w4_raw[g][:, :, 256 * nh : 256 * (nh + 1)])
-
-        h_rows, c_halves = {}, {}
-
-        def product_c_half(g, half, letters):
-            js = slice(half * HALF, (half + 1) * HALF)
-            for t in range(4):
-                if t % 2 == 0:
-                    pair = bank(letters[t // 2])
-                c_halves[g, half, t] = pair[:, HALF * (t % 2) : HALF * (t % 2 + 1)]
-                for a in range(2):
-                    c0 = 2 * S + H * a + 512 * g + P * t
-                    nc.tensor.matmul_mx(
-                        c_halves[g, half, t], lhsT=w3_cols[g][:, a, P * t : P * (t + 1)].bitcast(FP8X4),
-                        lhsT_scale=planes[4:P, c0 : c0 + P], rhs=v_words[a][:, js].bitcast(FP8X4),
-                        rhs_scale=planes[:, a * S + half * HALF : a * S + (half + 1) * HALF], start=(a == 0), stop=(a == 1))
-
-        def make_h_rows(g, half):
-            js = slice(half * HALF, (half + 1) * HALF)
-            h_rows[g, half] = new([P, 4, HALF], BF16, "h_rows%d%d" % (g, half))
-            for t in range(4):
-                nc.vector.scalar_tensor_tensor(
-                    h_rows[g, half][:, t, :], c_halves[g, half, t], b3_cols[:, g, 4 * t : 4 * t + 1],
-                    ab[g][:, t, js], ALU.add, ALU.max)
-
-        def empty_c_half(g, half):
-            c_sb[g, half] = new([P, 4, HALF], F32, "c%d%d" % (g, half))
-            for t in range(4):
-                nc.scalar.activation(
-                    c_sb[g, half][:, t, :], c_halves[g, half, t], ACT.Identity, bias=b3_cols[:, g, 4 * t : 4 * t + 1])
-
-        def round_w1_on_gpsimd(g, a, tp):
-            rounded = rounded_half(g, a, tp)
-            src = w1_raw[g, a].rearrange("p i (q t e) -> p t q e i", t=4, e=4)
-            for t in range(2):
-                nc.gpsimd.tensor_scalar(
-                    rounded[:, 512 * t : 512 * (t + 1)].rearrange("p (q e i) -> p q e i", e=4, i=4), src[:, 2 * tp + t],
-                    1.0, 0.0, ALU.mult, ALU.add)
-            w1_rounded[g, a, tp] = rounded
-
-        def interleave_h(g, half, on_gpsimd=True):
-            h[g, half] = new([P, 4 * HALF], BF16, "h%d%d" % (g, half))
-            if on_gpsimd:
-                interleave_on_gpsimd(h[g, half][:], h_rows[g, half][:])
-            else:
-                nc.scalar.copy(
-                    h[g, half][:].rearrange("p (c j t) -> p c t j", j=4, t=4),
-                    h_rows[g, half][:].rearrange("p t (c j) -> p c t j", j=4))
+            dst, src = w4_quarter(g, nh)
+            gpsimd_round(dst.rearrange("p (n t) -> p n t", t=4), src.rearrange("p t n -> p n t"))
 
         def quantize_w4(g, nh):
             w4_mx[g, nh] = quantize("w4_mx%d%d" % (g, nh), w4_rounded[g, nh][:])
 
+        out_sums, results = {}, {}
+
         def out_pass(g, half, u, letter=None):
             if letter:
-                out_banks[half, u] = bank(letter)
+                out_sums[half, u] = bank(letter)[:, 0:HALF]
             cols = slice(P * (u % 2), P * (u % 2 + 1))
             codes, scales = w4_mx[g, u // 2]
             nc.tensor.matmul_mx(
-                out_banks[half, u][:, 0:HALF], lhsT=codes[:, cols].bitcast(FP8X4), lhsT_scale=scales[:, cols],
-                rhs=h_mx[g, half][0][:].bitcast(FP8X4), rhs_scale=h_mx[g, half][1][:], start=bool(letter), stop=not letter)
+                out_sums[half, u], lhsT=codes[:, cols].bitcast(FP8X4), lhsT_scale=scales[:, cols],
+                rhs=h_mx[g, half][0].bitcast(FP8X4), rhs_scale=h_mx[g, half][1], start=(g == 0), stop=(g == 1))
 
-        def finish(half, u, on_scalar_engine, queue=nc.sync):
-            result = new([P, HALF], F32, "result%d%d" % (half, u))
-            sums = out_banks[half, u][:, 0:HALF]
-            if on_scalar_engine:
-                nc.scalar.activation(result[:], sums, ACT.Identity, bias=bq_cols[:, u : u + 1])
+        def finish(half, u, on_scalar, queue=nc.sync):
+            out_pass(1, half, u)
+            results[half, u] = new([P, HALF], F32, "result%d%d" % (half, u))
+            if on_scalar:
+                nc.scalar.activation(results[half, u][:], out_sums[half, u], ACT.Identity, bias=bq_cols[:, u : u + 1])
             else:
-                nc.vector.tensor_scalar(result[:], sums, bq_cols[:, u : u + 1], None, ALU.add)
-            queue.dma_start(out[P * u : P * (u + 1), half * HALF : (half + 1) * HALF], result[:])
+                nc.vector.tensor_scalar(results[half, u][:], out_sums[half, u], bq_cols[:, u : u + 1], None, ALU.add)
+            queue.dma_start(out[P * u : P * (u + 1), half * HALF : (half + 1) * HALF], results[half, u][:])
 
-        for a in range(2):
-            for t in range(2):
-                first_stage_pass("b", 0, t, a, "" if a else "AB"[t])
         for t in range(2):
+            open_sum("b", 0, t, 0, "AB"[t])
+        for t in range(2):
+            close_sum("b", 0, t, 1)
             empty_b(0, t)
         for t in range(2, 4):
-            first_stage_pass("b", 0, t, 0, "ABCD"[t])
-            first_stage_pass("b", 0, t, 1)
+            product("b", 0, t, "ABCD"[t], first=0)
             empty_b(0, t)
         for t in range(4):
             product("b", 1, t, "EFGH"[t])
         for tp in range(2):
-            round_w1(0, 0, tp, on_vector)
+            round_w1(0, 0, tp, nc.vector.tensor_copy)
         for tp in range(2):
             quantize_w1(0, 0, tp)
-        round_w1(0, 1, 0, on_vector)
-        round_w1(0, 1, 1, on_scalar)
+        load_w4(1)
+        with nc.allow_non_contiguous_dma(reason="one bias value a partition and output tile"):
+            nc.sync.dma_start(bq_cols, bq.rearrange("(u p) -> p u", p=P))
+        round_w1(0, 1, 0, nc.vector.tensor_copy)
+        round_w1(0, 1, 1, nc.scalar.copy)
         for tp in range(2):
             quantize_w1(0, 1, tp)
         reorder_w3(0, nc.gpsimd.tensor_copy)
@@ -377,58 +356,56 @@ def tile_list_subsumption_box_features_kernel(
         for t in range(4):
             product("a", 0, t, "ABCD"[t])
             multiply(0, t)
-        round_w1(1, 0, 0, on_scalar)
+        round_w1(1, 0, 0, nc.scalar.copy)
         round_w1_on_gpsimd(1, 0, 1)
-        product_c_half(0, 0, "AB")
-        product_c_half(0, 1, "CD")
-        make_h_rows(0, 0)
+        for t in range(4):
+            product("c", 0, t, "ABCD"[t])
+        make_h0_row(0)
         quantize_w1(1, 0, 0)
+        make_h0_row(1)
         for t in range(2):
-            first_stage_pass("a", 1, t, 0, "AB"[t])
-        make_h_rows(0, 1)
-        round_w1(1, 1, 0, on_scalar)
-        round_w1_on_gpsimd(1, 1, 1)
-        quantize_w1(1, 1, 0)
+            open_sum("a", 1, t, 0, "AB"[t])
+        for t in range(2, 4):
+            make_h0_row(t)
+        by_tile = last_rounded[:].rearrange("p (t qh q e i) -> p qh q t e i", t=4, qh=2, e=4, i=4)
+        gpsimd_round(by_tile[:, 0], w1_last[0][:].rearrange("p i (q t e) -> p q t e i", t=4, e=4))
+        nc.scalar.copy(
+            by_tile[:, 1].rearrange("p q t e i -> p q t i e"), w1_last[1][:].rearrange("p i (q t e) -> p q t i e", t=4, e=4))
+        for tp in range(2):
+            rounded_half(1, 1, tp)
         quantize_w1(1, 0, 1)
+        quantize_w1(1, 1, 0)
         quantize_w1(1, 1, 1)
-        reorder_w3(1, on_scalar)
-        interleave_h(0, 0)
-        interleave_h(0, 1, False)
+        reorder_w3(1, nc.scalar.copy)
+        interleave_h0_on_gpsimd(0)
+        interleave_h0_on_scalar(1)
         round_w4_on_gpsimd(0, 0)
-        round_w4(0, 1, on_scalar)
+        round_w4(0, 1, nc.scalar.copy)
         for t in range(4):
             if t >= 2:
-                first_stage_pass("a", 1, t, 0, "ABCD"[t])
-            first_stage_pass("a", 1, t, 1)
+                open_sum("a", 1, t, 0, "ABCD"[t])
+            close_sum("a", 1, t, 1)
             multiply(1, t)
-        for half in range(2):
-            product_c_half(1, half, ("FG", "HE")[half])
-            empty_c_half(1, half)
+        product_c1(0, "AB")
+        product_c1(1, "CD")
         for nh in range(2):
-            round_w4(1, nh, on_scalar)
-        for half in range(2):
-            quantize_h(0, half)
-        quantize_w4(0, 0)
-        for half in range(2):
-            for u in range(2):
-                out_pass(0, half, u, "ABCD"[2 * half + u])
-        make_h(1, 0)
-        quantize_w4(0, 1)
-        for half in range(2):
-            for u in range(2, 4):
-                out_pass(0, half, u, "FGHE"[2 * half + u % 2])
-        quantize_h(1, 0)
-        make_h(1, 1)
+            round_w4(1, nh, nc.scalar.copy)
+        quantize_h0()
+        for nh in range(2):
+            quantize_w4(0, nh)
+            for half in range(2):
+                for u in range(2 * nh, 2 * nh + 2):
+                    out_pass(0, half, u, ("EFGH", "ABCD")[nh][2 * half + u % 2])
+        make_h1(0)
+        quantize_h1(0)
+        make_h1(1)
         quantize_w4(1, 0)
         for u in range(2):
-            out_pass(1, 0, u)
             finish(0, u, True)
-        quantize_h(1, 1)
+        quantize_h1(1)
         for u in range(2):
-            out_pass(1, 1, u)
             finish(1, u, True)
         quantize_w4(1, 1)
         for u in range(2, 4):
             for half in range(2):
-                out_pass(1, half, u)
                 finish(half, u, (half, u) == (0, 3))

@@ -23,43 +23,42 @@ CHUNK = 2048
 
 AT = {
     "table0": 4 * KB,
-    "w1_last0": 1 * KB,
-    "w1_last1": 5 * KB,
-    "w3_cols1": 5 * KB,
-    "w4_rounded10": 5 * KB,
-    "w4_rounded11": 7 * KB,
-    "w3_raw1": 9 * KB,
-    "h_rows": 114 * KB,
-    "w4_rounded01": 114 * KB,
-    "h10": 114 * KB,
     "zeros": 12 * KB - 64,
     "table1": 12 * KB,
-    "w4_first": 13 * KB,
-    "c10": 13 * KB,
-    "w1_rounded000": 21 * KB,
-    "w4_last": 21 * KB,
     "w3_raw0": 30 * KB,
-    "b13": 30 * KB,
-    "w4_mx00": 30 * KB,
     "gathered_scales": 34 * KB - S,
     "staging": 34 * KB,
+    "w1_last": 1 * KB,
+    "w3_raw1": 9 * KB,
+    "w4_first": 13 * KB,
+    "w1_rounded000": 21 * KB,
+    "w4_last": 21 * KB,
+    "b10": 92 * KB,
+    "w1_rounded010": 93 * KB,
+    "b11": 94 * KB,
+    "b12": 86 * KB,
+    "w1_rounded011": 87 * KB,
+    "w3_cols0": 88 * KB,
+    "b13": 30 * KB,
+    "b03": 96 * KB,
+    "w1_mx100": 96 * KB,
     "ab0": 60 * KB,
     "w1_mx110": 60 * KB,
     "w1_mx101": 61 * KB,
     "w1_mx111": 62 * KB,
-    "b03": 96 * KB,
-    "w1_mx100": 96 * KB,
-    "b12": 86 * KB,
-    "h_mx0": 86 * KB,
-    "w1_rounded011": 87 * KB,
-    "w3_cols0": 88 * KB,
-    "b10": 92 * KB,
-    "w1_rounded010": 93 * KB,
-    "b11": 94 * KB,
     "ab1": 98 * KB,
     "w1_rounded11": 105 * KB,
     "w4_rounded00": 106 * KB,
     "h0": 108 * KB,
+    "w3_cols1": 64 * KB,
+    "h_rows": 114 * KB,
+    "w4_rounded01": 114 * KB,
+    "c10": 13 * KB,
+    "w4_rounded10": 64 * KB,
+    "w4_rounded11": 66 * KB,
+    "h_mx0": 86 * KB,
+    "w4_mx00": 30 * KB,
+    "h10": 114 * KB,
 }
 
 
@@ -136,7 +135,7 @@ def tile_list_subsumption_box_features_kernel(
             nc.vector.tensor_copy(v_words[a][:], table[a][:].bitcast(U32).indirect(offsets[:]))
 
         staging = new([P, 3 * CHUNK + 32], F32, "staging")
-        w1_last = [new([P, 4, 256], F32, "w1_last0"), new([P, 4, 256], F32, "w1_last1")]
+        w1_last = new([P, CHUNK], F32, "w1_last")
         w4_first = new([P, CHUNK], F32, "w4_first")
         w4_last = new([P, CHUNK + 8], F32, "w4_last")
 
@@ -144,6 +143,7 @@ def tile_list_subsumption_box_features_kernel(
             return tile[:, slot * CHUNK : (slot + 1) * CHUNK].rearrange("p (i c) -> p i c", i=4)
 
         w1_raw = {(0, 0): chunk_of(staging, 0), (0, 1): chunk_of(staging, 1), (1, 0): chunk_of(staging, 2)}
+        w1_raw[1, 1] = chunk_of(w1_last, 0)
         w4_raw = [chunk_of(w4_first, 0), chunk_of(w4_last, 0)]
         b3_cols = staging[:, 3 * CHUNK : 3 * CHUNK + 32].rearrange("p (g s) -> p g s", g=2)
         bq_cols = w4_last[:, CHUNK : CHUNK + 4]
@@ -169,9 +169,7 @@ def tile_list_subsumption_box_features_kernel(
         for e in range(4):
             nc.sync.dma_start(b3_cols[e:P:4, :, 0:13], b3_runs[:, :, e : e + 13])
         load_w1(1, 0)
-        for qh in range(2):
-            columns = w1[512:1024, 512 + 256 * qh : 512 + 256 * (qh + 1)]
-            nc.sync.dma_start(w1_last[qh][:], columns.rearrange("(p i) c -> p i c", i=4))
+        load_w1(1, 1)
         load_w3(1)
         load_w4(0)
 
@@ -309,7 +307,7 @@ def tile_list_subsumption_box_features_kernel(
         def quantize_w4(g, nh):
             w4_mx[g, nh] = quantize("w4_mx%d%d" % (g, nh), w4_rounded[g, nh][:])
 
-        out_sums, results = {}, {}
+        out_sums = {}
 
         def out_pass(g, half, u, letter=None):
             if letter:
@@ -320,14 +318,14 @@ def tile_list_subsumption_box_features_kernel(
                 out_sums[half, u], lhsT=codes[:, cols].bitcast(FP8X4), lhsT_scale=scales[:, cols],
                 rhs=h_mx[g, half][0].bitcast(FP8X4), rhs_scale=h_mx[g, half][1], start=(g == 0), stop=(g == 1))
 
-        def finish(half, u, on_scalar, queue=nc.sync):
+        def finish(half, u, on_scalar):
             out_pass(1, half, u)
-            results[half, u] = new([P, HALF], F32, "result%d%d" % (half, u))
+            result = new([P, HALF], F32, "result%d%d" % (half, u))
             if on_scalar:
-                nc.scalar.activation(results[half, u][:], out_sums[half, u], ACT.Identity, bias=bq_cols[:, u : u + 1])
+                nc.scalar.activation(result[:], out_sums[half, u], ACT.Identity, bias=bq_cols[:, u : u + 1])
             else:
-                nc.vector.tensor_scalar(results[half, u][:], out_sums[half, u], bq_cols[:, u : u + 1], None, ALU.add)
-            queue.dma_start(out[P * u : P * (u + 1), half * HALF : (half + 1) * HALF], results[half, u][:])
+                nc.vector.tensor_scalar(result[:], out_sums[half, u], bq_cols[:, u : u + 1], None, ALU.add)
+            nc.sync.dma_start(out[P * u : P * (u + 1), half * HALF : (half + 1) * HALF], result[:])
 
         for t in range(2):
             open_sum("b", 0, t, 0, "AB"[t])
@@ -368,9 +366,10 @@ def tile_list_subsumption_box_features_kernel(
         for t in range(2, 4):
             make_h0_row(t)
         by_tile = last_rounded[:].rearrange("p (t qh q e i) -> p qh q t e i", t=4, qh=2, e=4, i=4)
-        gpsimd_round(by_tile[:, 0], w1_last[0][:].rearrange("p i (q t e) -> p q t e i", t=4, e=4))
+        gpsimd_round(by_tile[:, 0], w1_raw[1, 1][:, :, 0:256].rearrange("p i (q t e) -> p q t e i", t=4, e=4))
         nc.scalar.copy(
-            by_tile[:, 1].rearrange("p q t e i -> p q t i e"), w1_last[1][:].rearrange("p i (q t e) -> p q t i e", t=4, e=4))
+            by_tile[:, 1].rearrange("p q t e i -> p q t i e"),
+            w1_raw[1, 1][:, :, 256:512].rearrange("p i (q t e) -> p q t i e", t=4, e=4))
         for tp in range(2):
             rounded_half(1, 1, tp)
         quantize_w1(1, 0, 1)
@@ -401,11 +400,11 @@ def tile_list_subsumption_box_features_kernel(
         make_h1(1)
         quantize_w4(1, 0)
         for u in range(2):
-            finish(0, u, True)
+            finish(0, u, on_scalar=True)
         quantize_h1(1)
         for u in range(2):
-            finish(1, u, True)
+            finish(1, u, on_scalar=True)
         quantize_w4(1, 1)
         for u in range(2, 4):
             for half in range(2):
-                finish(half, u, (half, u) == (0, 3))
+                finish(half, u, on_scalar=(half, u) == (0, 3))

from contextlib import ExitStack

import concourse.mybir as mybir

K, H, N, T, S = 1024, 1024, 512, 2048, 512
FLOPS = 2 * S * (3 * K * H + H * N)

F32 = mybir.dt.float32
BF16 = mybir.dt.bfloat16
I32 = mybir.dt.int32
U32 = mybir.dt.uint32
U16 = mybir.dt.uint16
U8 = mybir.dt.uint8
FP8X4 = mybir.dt.float8_e4m3fn_x4
FP4X4 = mybir.dt.float4_e2m1fn_x4
ALU = mybir.AluOpType
ACT = mybir.ActivationFunctionType

P = 128
HALF = S // 2
KB = 1024
CHUNK = 2048

AT = {
    "table0": 4 * KB,
    "zeros": 12 * KB - 64,
    "table1": 12 * KB,
    "w3_raw0": 30 * KB,
    "gathered_scales": 34 * KB - S,
    "staging": 34 * KB,
    "w1_last": 1 * KB,
    "w3_raw1": 9 * KB,
    "w4_first": 13 * KB,
    "w1_rounded000": 21 * KB,
    "w4_last": 21 * KB,
    "b10": 92 * KB,
    "w1_rounded010": 93 * KB,
    "b11": 94 * KB,
    "b12": 86 * KB,
    "w1_rounded011": 87 * KB,
    "w3_cols0": 88 * KB,
    "b13": 30 * KB,
    "b03": 96 * KB,
    "w1_mx100": 96 * KB,
    "ab0": 60 * KB,
    "w1_mx110": 60 * KB,
    "w1_mx101": 61 * KB,
    "w1_mx111": 62 * KB,
    "ab1": 98 * KB,
    "w1_rounded11": 105 * KB,
    "w4_rounded00": 106 * KB,
    "h0": 108 * KB,
    "w3_cols1": 64 * KB,
    "h_rows": 114 * KB,
    "w4_rounded01": 114 * KB,
    "c10": 13 * KB,
    "w4_rounded10": 64 * KB,
    "w4_rounded11": 66 * KB,
    "h_mx0": 86 * KB,
    "w4_mx00": 30 * KB,
    "h10": 114 * KB,
}


def tile_list_subsumption_box_features_kernel(
    tc, tab_words, tab_scales, offs, w1, w2_words, w2_scales, w3_words, w3_scales, b3, w4, bq, out
):
    nc = tc.nc
    with ExitStack() as ctx:
        keep = ctx.enter_context(tc.tile_pool(name="keep", bufs=1))
        shared = ctx.enter_context(tc.tile_pool(name="shared", bufs=1))
        psum = ctx.enter_context(tc.psum_pool(name="psum", bufs=1))

        def new(shape, dtype, name):
            if name in AT:
                return shared.tile(shape, dtype, name=name, offset=AT[name], align_bytes=64)
            return keep.tile(shape, dtype, name=name, align_bytes=64)

        def bank(letter):
            return psum.tile([P, S], F32, name="bank" + letter, tag="bank" + letter)

        def gpsimd_round(dst, src):
            nc.gpsimd.tensor_scalar(dst, src, 1.0, 0.0, ALU.mult, ALU.add)

        offsets = keep.tile([P, S // 16], U16, name="offsets")
        nc.sync.dma_start(offsets[:], offs)
        w2_raw = new([P, 2, 512], I32, "w2_raw")
        nc.sync.dma_start(w2_raw[:], w2_words.bitcast(I32).rearrange("a p n -> p a n"))

        scale_window = [new([P, T], U8, "scale_window0"), new([P, T], U8, "scale_window1")]
        scale_rows = new([P, 512], I32, "scale_rows")
        zeros = new([P, 32], I32, "zeros")
        nc.gpsimd.memset(scale_window[0][:].bitcast(I32), 0)
        nc.sync.dma_start(scale_window[0][:].bitcast(I32)[0:P:8, :], tab_scales[0].bitcast(I32))
        nc.vector.memset(scale_window[1][:].bitcast(I32), 0)
        nc.sync.dma_start(scale_window[1][:].bitcast(I32)[0:P:8, :], tab_scales[1].bitcast(I32))
        nc.vector.memset(zeros[:], 0)
        nc.vector.tensor_copy(
            scale_rows[:].rearrange("p (n w) -> p n w", w=32), zeros[:].unsqueeze(1).to_broadcast([P, 16, 32]))
        for first, src in ((0, w2_scales), (4, w3_scales)):
            nc.sync.dma_start(
                scale_rows[first:P:8, :].rearrange("m (a n) -> m a n", a=2), src.bitcast(I32).rearrange("a m n -> m a n"))
        table = []
        for a in range(2):
            table.append(new([P, T], I32, "table%d" % a))
            nc.sync.dma_start(table[a][:], tab_words[a].rearrange("p t i -> p (t i)").bitcast(I32))

        w2_cols, w3_raw, w3_cols, v_words = {}, {}, {}, {}

        def reorder_w2(g):
            w2_cols[g] = new([P, 2, 256], U32, "w2_cols%d" % g)
            nc.scalar.copy(
                w2_cols[g][:].rearrange("p a (t q e) -> p a t q e", t=4, e=2),
                w2_raw[:].bitcast(U32)[:, :, 256 * g : 256 * (g + 1)].rearrange("p a (q t e) -> p a t q e", t=4, e=2),
            )

        planes = new([P, 2 * S + 2 * H], U8, "planes")
        planes_i32 = planes[:].bitcast(I32)
        reorder_w2(0)
        nc.scalar.copy(
            planes[:].bitcast(U32)[:, 256:768].rearrange("p (x t qh ql) -> p x qh t ql", x=4, t=4, ql=4),
            scale_rows[:].bitcast(U32).rearrange("p (x qh ql t) -> p x qh t ql", x=4, t=4, ql=4),
        )
        reorder_w2(1)
        for i in range(1, 4):
            nc.sync.dma_start(planes_i32[4 + i : P : 32, 256:768], planes_i32[4 + 8 * i : P : 32, 256:768])
        gathered_scales = new([P, 2 * S], U8, "gathered_scales")
        for a in range(2):
            nc.vector.tensor_copy(gathered_scales[:, a * S : (a + 1) * S], scale_window[a][:].indirect(offsets[:]))
        nc.vector.tensor_copy(planes_i32[:, 0:256], gathered_scales[:].bitcast(I32))
        for i in range(1, 4):
            nc.sync.dma_start(planes_i32[i:P:32, :], planes_i32[8 * i : P : 32, :])
        for a in range(2):
            v_words[a] = new([P, S], U32, "v_words%d" % a)
            nc.vector.tensor_copy(v_words[a][:], table[a][:].bitcast(U32).indirect(offsets[:]))

        staging = new([P, 3 * CHUNK + 32], F32, "staging")
        w1_last = new([P, CHUNK], F32, "w1_last")
        w4_first = new([P, CHUNK], F32, "w4_first")
        w4_last = new([P, CHUNK + 8], F32, "w4_last")

        def chunk_of(tile, slot):
            return tile[:, slot * CHUNK : (slot + 1) * CHUNK].rearrange("p (i c) -> p i c", i=4)

        w1_raw = {(0, 0): chunk_of(staging, 0), (0, 1): chunk_of(staging, 1), (1, 0): chunk_of(staging, 2)}
        w1_raw[1, 1] = chunk_of(w1_last, 0)
        w4_raw = [chunk_of(w4_first, 0), chunk_of(w4_last, 0)]
        b3_cols = staging[:, 3 * CHUNK : 3 * CHUNK + 32].rearrange("p (g s) -> p g s", g=2)
        bq_cols = w4_last[:, CHUNK : CHUNK + 4]

        def load_w1(g, a):
            chunk = w1[512 * a : 512 * (a + 1), 512 * g : 512 * (g + 1)]
            nc.sync.dma_start(w1_raw[g, a], chunk.rearrange("(p i) c -> p i c", i=4))

        def load_w3(g):
            w3_raw[g] = new([P, 2, 512], I32, "w3_raw%d" % g)
            words = w3_words.rearrange("a p n i -> a p (n i)").bitcast(I32)
            nc.sync.dma_start(w3_raw[g][:], words[:, :, 512 * g : 512 * (g + 1)].rearrange("a p n -> p a n"))

        def load_w4(g):
            rows = w4[512 * g : 512 * (g + 1), :].rearrange("(q t e) n -> t q e n", t=4, e=4)
            for t in range(4):
                nc.sync.dma_start(w4_raw[g][:, t, :], rows[t])

        load_w1(0, 0)
        load_w1(0, 1)
        load_w3(0)
        b3_runs = b3.rearrange("(g q s) -> q g s", g=2, s=16)
        for e in range(4):
            nc.sync.dma_start(b3_cols[e:P:4, :, 0:13], b3_runs[:, :, e : e + 13])
        load_w1(1, 0)
        load_w1(1, 1)
        load_w3(1)
        load_w4(0)

        def reorder_w3(g, copy):
            w3_cols[g] = new([P, 2, 512], U32, "w3_cols%d" % g)
            copy(
                w3_cols[g][:].rearrange("p a (t q e) -> p a t q e", t=4, e=4),
                w3_raw[g][:].bitcast(U32).rearrange("p a (q t e) -> p a t q e", t=4, e=4),
            )

        sums, b_sb, c_sb, w1_rounded, w1_mx = {}, {}, {}, {}, {}
        ab = [new([P, 4, S], F32, "ab0"), new([P, 4, S], F32, "ab1")]

        def stationary(x, g, t, a):
            c0 = 2 * S + H * a + 512 * g + P * t
            if x == "a":
                codes, scales = w1_mx[g, a, t // 2]
                cols = slice(P * (t % 2), P * (t % 2 + 1))
                return dict(lhsT=codes[:, cols].bitcast(FP8X4), lhsT_scale=scales[:, cols])
            if x == "b":
                words = w2_cols[g][:, a, 64 * t : 64 * (t + 1)].bitcast(U8)
                return dict(lhsT=words.bitcast(FP4X4), lhsT_scale=planes[:, c0 : c0 + P])
            return dict(lhsT=w3_cols[g][:, a, P * t : P * (t + 1)].bitcast(FP8X4), lhsT_scale=planes[4:P, c0 : c0 + P])

        def one_pass(key, a, first, j0=0, width=S):
            x, g, t = key[:3]
            nc.tensor.matmul_mx(
                sums[key], rhs=v_words[a][:, j0 : j0 + width].bitcast(FP8X4),
                rhs_scale=planes[:, a * S + j0 : a * S + j0 + width], start=first, stop=not first, **stationary(x, g, t, a))

        def open_sum(x, g, t, a, letter):
            sums[x, g, t] = bank(letter)[:]
            one_pass((x, g, t), a, True)

        def close_sum(x, g, t, a):
            one_pass((x, g, t), a, False)

        def product(x, g, t, letter, first=1):
            open_sum(x, g, t, first, letter)
            close_sum(x, g, t, 1 - first)

        def product_c1(half, letters):
            c_sb[half] = new([P, 4, HALF], F32, "c1%d" % half)
            for t in range(4):
                if t % 2 == 0:
                    pair = bank(letters[t // 2])
                sums["c", 1, t, half] = pair[:, HALF * (t % 2) : HALF * (t % 2 + 1)]
                for a in range(2):
                    one_pass(("c", 1, t, half), a, a == 0, half * HALF, HALF)
            for t in range(4):
                nc.scalar.activation(
                    c_sb[half][:, t, :], sums["c", 1, t, half], ACT.Identity, bias=b3_cols[:, 1, 4 * t : 4 * t + 1])

        def empty_b(g, t):
            b_sb[g, t] = new([P, S], F32, "b%d%d" % (g, t))
            nc.scalar.copy(b_sb[g, t][:], sums["b", g, t])

        def multiply(g, t):
            nc.vector.tensor_tensor(ab[g][:, t, :], sums["a", g, t], b_sb[g, t][:], ALU.mult)

        def quantize(name, rounded, width=256):
            codes = new([P, width], U32, name)
            scales = new([P, width], U8, name + "_scales")
            nc.vector.quantize_mx(codes[:].bitcast(FP8X4), scales[:], rounded)
            return codes[:], scales[:]

        last_rounded = new([P, 2048], BF16, "w1_rounded11")

        def rounded_half(g, a, tp):
            if (g, a) == (1, 1):
                w1_rounded[g, a, tp] = last_rounded[:, 1024 * tp : 1024 * (tp + 1)]
            else:
                w1_rounded[g, a, tp] = new([P, 1024], BF16, "w1_rounded%d%d%d" % (g, a, tp))[:]
            return w1_rounded[g, a, tp]

        def round_w1(g, a, tp, copy):
            src = w1_raw[g, a].rearrange("p i (q t e) -> p t q i e", t=4, e=4)[:, 2 * tp : 2 * tp + 2]
            copy(rounded_half(g, a, tp).rearrange("p (t q e i) -> p t q i e", t=2, e=4, i=4), src)

        def round_w1_on_gpsimd(g, a, tp):
            src = w1_raw[g, a].rearrange("p i (q t e) -> p t q e i", t=4, e=4)
            dst = rounded_half(g, a, tp).rearrange("p (t q e i) -> p t q e i", t=2, e=4, i=4)
            for t in range(2):
                gpsimd_round(dst[:, t], src[:, 2 * tp + t])

        def quantize_w1(g, a, tp):
            w1_mx[g, a, tp] = quantize("w1_mx%d%d%d" % (g, a, tp), w1_rounded[g, a, tp])

        h1, h_mx, w4_rounded, w4_mx = {}, {}, {}, {}
        h_rows = new([P, 4, S], BF16, "h_rows")
        h0 = new([P, 4 * S], BF16, "h0")

        def make_h0_row(t):
            nc.vector.scalar_tensor_tensor(
                h_rows[:, t, :], sums["c", 0, t], b3_cols[:, 0, 4 * t : 4 * t + 1], ab[0][:, t, :], ALU.add, ALU.max)

        def h0_half(half):
            return h0[:, 4 * HALF * half : 4 * HALF * (half + 1)], h_rows[:, :, HALF * half : HALF * (half + 1)]

        def interleave_h0_on_gpsimd(half):
            dst, src = h0_half(half)
            gpsimd_round(dst.rearrange("p (j t) -> p j t", t=4), src.rearrange("p t j -> p j t"))

        def interleave_h0_on_scalar(half):
            dst, src = h0_half(half)
            nc.scalar.copy(dst.rearrange("p (c j t) -> p c t j", j=4, t=4), src.rearrange("p t (c j) -> p c t j", j=4))

        def quantize_h0():
            codes, scales = quantize("h_mx0", h0[:], S)
            for half in range(2):
                h_mx[0, half] = codes[:, HALF * half : HALF * (half + 1)], scales[:, HALF * half : HALF * (half + 1)]

        def make_h1(half):
            h1[half] = new([P, 4 * HALF], BF16, "h1%d" % half)
            nc.vector.tensor_tensor(
                h1[half][:].rearrange("p (c j t) -> p c t j", j=2, t=4),
                ab[1][:, :, half * HALF : (half + 1) * HALF].rearrange("p t (c j) -> p c t j", j=2),
                c_sb[half][:].rearrange("p t (c j) -> p c t j", j=2), ALU.max)

        def quantize_h1(half):
            h_mx[1, half] = quantize("h_mx1%d" % half, h1[half][:])

        def w4_quarter(g, nh):
            w4_rounded[g, nh] = new([P, 1024], BF16, "w4_rounded%d%d" % (g, nh))
            return w4_rounded[g, nh][:], w4_raw[g][:, :, 256 * nh : 256 * (nh + 1)]

        def round_w4(g, nh, copy):
            dst, src = w4_quarter(g, nh)
            copy(dst.rearrange("p (c n t) -> p c t n", n=2, t=4), src.rearrange("p t (c n) -> p c t n", n=2))

        def round_w4_on_gpsimd(g, nh):
            dst, src = w4_quarter(g, nh)
            gpsimd_round(dst.rearrange("p (n t) -> p n t", t=4), src.rearrange("p t n -> p n t"))

        def quantize_w4(g, nh):
            w4_mx[g, nh] = quantize("w4_mx%d%d" % (g, nh), w4_rounded[g, nh][:])

        out_sums = {}

        def out_pass(g, half, u, letter=None):
            if letter:
                out_sums[half, u] = bank(letter)[:, 0:HALF]
            cols = slice(P * (u % 2), P * (u % 2 + 1))
            codes, scales = w4_mx[g, u // 2]
            nc.tensor.matmul_mx(
                out_sums[half, u], lhsT=codes[:, cols].bitcast(FP8X4), lhsT_scale=scales[:, cols],
                rhs=h_mx[g, half][0].bitcast(FP8X4), rhs_scale=h_mx[g, half][1], start=(g == 0), stop=(g == 1))

        def finish(half, u, on_scalar):
            out_pass(1, half, u)
            result = new([P, HALF], F32, "result%d%d" % (half, u))
            if on_scalar:
                nc.scalar.activation(result[:], out_sums[half, u], ACT.Identity, bias=bq_cols[:, u : u + 1])
            else:
                nc.vector.tensor_scalar(result[:], out_sums[half, u], bq_cols[:, u : u + 1], None, ALU.add)
            nc.sync.dma_start(out[P * u : P * (u + 1), half * HALF : (half + 1) * HALF], result[:])

        for t in range(2):
            open_sum("b", 0, t, 0, "AB"[t])
        for t in range(2):
            close_sum("b", 0, t, 1)
            empty_b(0, t)
        for t in range(2, 4):
            product("b", 0, t, "ABCD"[t], first=0)
            empty_b(0, t)
        for t in range(4):
            product("b", 1, t, "EFGH"[t])
        for tp in range(2):
            round_w1(0, 0, tp, nc.vector.tensor_copy)
        for tp in range(2):
            quantize_w1(0, 0, tp)
        load_w4(1)
        with nc.allow_non_contiguous_dma(reason="one bias value a partition and output tile"):
            nc.sync.dma_start(bq_cols, bq.rearrange("(u p) -> p u", p=P))
        round_w1(0, 1, 0, nc.vector.tensor_copy)
        round_w1(0, 1, 1, nc.scalar.copy)
        for tp in range(2):
            quantize_w1(0, 1, tp)
        reorder_w3(0, nc.gpsimd.tensor_copy)
        for t in range(4):
            empty_b(1, t)
        for t in range(4):
            product("a", 0, t, "ABCD"[t])
            multiply(0, t)
        round_w1(1, 0, 0, nc.scalar.copy)
        round_w1_on_gpsimd(1, 0, 1)
        for t in range(4):
            product("c", 0, t, "ABCD"[t])
        make_h0_row(0)
        quantize_w1(1, 0, 0)
        make_h0_row(1)
        for t in range(2):
            open_sum("a", 1, t, 0, "AB"[t])
        for t in range(2, 4):
            make_h0_row(t)
        by_tile = last_rounded[:].rearrange("p (t qh q e i) -> p qh q t e i", t=4, qh=2, e=4, i=4)
        gpsimd_round(by_tile[:, 0], w1_raw[1, 1][:, :, 0:256].rearrange("p i (q t e) -> p q t e i", t=4, e=4))
        nc.scalar.copy(
            by_tile[:, 1].rearrange("p q t e i -> p q t i e"),
            w1_raw[1, 1][:, :, 256:512].rearrange("p i (q t e) -> p q t i e", t=4, e=4))
        for tp in range(2):
            rounded_half(1, 1, tp)
        quantize_w1(1, 0, 1)
        quantize_w1(1, 1, 0)
        quantize_w1(1, 1, 1)
        reorder_w3(1, nc.scalar.copy)
        interleave_h0_on_gpsimd(0)
        interleave_h0_on_scalar(1)
        round_w4_on_gpsimd(0, 0)
        round_w4(0, 1, nc.scalar.copy)
        for t in range(4):
            if t >= 2:
                open_sum("a", 1, t, 0, "ABCD"[t])
            close_sum("a", 1, t, 1)
            multiply(1, t)
        product_c1(0, "AB")
        product_c1(1, "CD")
        for nh in range(2):
            round_w4(1, nh, nc.scalar.copy)
        quantize_h0()
        for nh in range(2):
            quantize_w4(0, nh)
            for half in range(2):
                for u in range(2 * nh, 2 * nh + 2):
                    out_pass(0, half, u, ("EFGH", "ABCD")[nh][2 * half + u % 2])
        make_h1(0)
        quantize_h1(0)
        make_h1(1)
        quantize_w4(1, 0)
        for u in range(2):
            finish(0, u, on_scalar=True)
        quantize_h1(1)
        for u in range(2):
            finish(1, u, on_scalar=True)
        quantize_w4(1, 1)
        for u in range(2, 4):
            for half in range(2):
                finish(half, u, on_scalar=(half, u) == (0, 3))
